import numpy as np, ml_dtypes
CORES = [36,164,52,180,100,228,116,244]
N = 8
BF = ml_dtypes.bfloat16
W, C, RU, S, M = 4096, 128, 3, 3, 7
def bf(x):
    return np.ascontiguousarray(x).astype(np.float32).astype(BF)
def parts(rng):
    d = {"ends": rng.integers(0, 256, (N, 8, 16, C)), "db": rng.integers(0, 256, (N, 8, 16, W), dtype=np.int16)}
    d["db"][:, :, 15] = rng.integers(0, M + 1, (N, 8, W)) * (rng.random((N, 8, W)) < 0.75)
    d["wt"] = rng.integers(0, rng.choice(np.array([2, 6, 12, 18]), (N, 8, 1, 16)), (N, 8, 16, 16))
    d["salt"] = rng.integers(0, W, (N, 8, 16, C)); d["nz"] = rng.integers(0, 256, (N, 8, 16, RU, S, C))
    k = rng.random((N, 8, RU, C))
    d["sl"] = np.where(k < 0.0625, 4000, np.where(k > 0.9375, -4000, rng.integers(-700, 401, (N, 8, RU, C))))
    return d
def pack(d):
    for k in ("ends", "wt", "nz"): d[k][:, :, 15] = 0
    return {"ends": bf(d["ends"].reshape(N, 128, C)), "db": bf(d["db"].reshape(N, 128, W)), "wt": bf(d["wt"].reshape(N, 128, 16)),
            "salt": np.ascontiguousarray(d["salt"].reshape(N, 128, C)).astype(np.int32), "nz": bf(d["nz"].reshape(N, 128, RU * S * C)),
            "sl": np.ascontiguousarray(d["sl"].reshape(N, 8, RU * C)).astype(np.int32)}
def walk(e, D, wt, salt, nz, sl, delta=None):
    e = e.astype(np.int32); D = D.astype(np.int32); w = wt.astype(np.int32).transpose(0, 1, 3, 2); a = salt.astype(np.int32); z = nz.astype(np.int32)
    verdicts, places = [], []
    for m in range(RU):
        v = np.roll(e, 1, axis=0); t = np.roll(e, -1, axis=0)
        shadow = []
        for s in range(S):
            u = np.matmul(w, v) >> 6
            pl = ((u * u >> 3) + 37 * u + 211 * s + a) & (W - 1)
            got = np.take_along_axis(D, pl.transpose(0, 1, 3, 2).reshape(N, 8, 1, C * 16), 3).reshape(N, 8, 16, C, 16)
            ask = (u & M).transpose(0, 1, 3, 2)
            hit = (got[:, :, 15] == ask) & (((np.arange(C) + m) & 3) != s)[:, None]
            f = (v + z[:, :, :, m, s]) & 255
            x = np.where(hit[:, :, None], got, f[..., None])
            first = np.argmin(hit, axis=3)
            place = np.take_along_axis(pl, first[:, :, None, :], 2)[:, :, 0]
            rec = f + 0; rec[:, :, 15] = np.take_along_axis(ask, first[..., None], 3)[..., 0]
            place = np.where(np.all(hit, axis=3), -1, place)
            shadow.append((place, rec)); places.append(place)
            v = (2 * v + np.max(x, axis=4) + np.min(x, axis=4)) >> 2; v[:, :, 15] = 0
        A = np.sum(np.abs(v - t), axis=2); B = np.sum(np.abs(e - t), axis=2)
        if delta is not None: sl[:, :, m] = A - B + delta[:, :, m]
        ok = A <= B + sl[:, :, m]
        e = np.where(ok[:, :, None], v, e); verdicts.append(ok)
        for place, rec in shadow:
            for q in range(N):
                for g in range(8):
                    c = np.flatnonzero(ok[q, g] & (place[q, g] >= 0))
                    to, at = np.unique(place[q, g, c], return_index=True)
                    D[q, g][:, to] = rec[q, g][:, c[at]]
    return e, np.stack(verdicts, 2), np.stack(places, 2)
def setup_inputs(rng):
    return pack(parts(rng))
def setup_inputs_again(rng):
    d = parts(rng)
    turn = (np.arange(N)[:, None, None, None] + np.arange(8)[:, None, None] + np.arange(RU)[:, None]) & 1
    d["sl"] = np.where(rng.random((N, 8, RU, C)) < 0.875, np.where(turn == 1, 4000, -4000), d["sl"])
    return pack(d)
def setup_inputs_alike(rng):
    d = parts(rng); c = np.arange(C)
    d["wt"][:, :3] = 0
    d["salt"][:, :3] = (rng.integers(0, W, (N, 3, 16, 1)) + 211 * (c & 3) * (np.arange(3)[:, None, None] > 0)) & (W - 1)
    d["db"][::2, 0, 15] = rng.integers(1, M + 1, d["db"][::2, 0, 15].shape); d["sl"][::2, 0, 0] = 4000
    ix = rng.integers(0, 4, C)
    d["ends"][:, 3:6] = d["ends"][:, 3:6][..., ix]; d["salt"][:, 3:6] = d["salt"][:, 3:6][..., ix]
    d["wt"][:, 6] = d["wt"][:, 6][:, :, :1] + np.zeros((1, 1, 16), np.int64); d["salt"][:, 6] = d["salt"][:, 6][:, :1] + np.zeros((1, 16, 1), np.int64)
    d["wt"][:, 7] = 0; d["db"][:, 7, 15] = rng.integers(1, M + 1, (N, W))
    x = 8 * np.argsort(rng.random((N, W // 8)), axis=1)[:, :C]
    for p in range(4):
        d["salt"][:, 7, p] = (x - 211 * p) & (W - 1)
        for q in range(N):
            if p > 0: d["db"][q, 7, 15, (x[q] + 211 * p) & (W - 1)] = 0
    d["sl"][:, 7] = np.where(rng.random((N, RU, C)) < 0.75, 4000, d["sl"][:, 7])
    return pack(d)
def setup_inputs_full(rng):
    d = parts(rng); c = np.arange(C)
    d["wt"][:, 0] = 0; d["db"][:, 0, 15] = 0
    d["wt"][:, 1] = 0; d["db"][:, 1, 15] = rng.integers(1, M + 1, (N, W))
    d["wt"][:, 2] = 0; d["wt"][:, 2, :, 15] = rng.integers(1, 18, (N, 16)); d["db"][:, 2, 15] = 0
    d["wt"][:, 3] = 17; d["ends"][:, 3, :, c % 2 == 0] = 255; d["nz"][:, 3, :, :, :, c % 2 == 0] = 0
    d["db"][:, 3, :15] = 255 - rng.integers(0, 5, (N, 15, W)) * (np.arange(N) & 1)[:, None, None]
    d["db"][:, 4, :15] = 255 * rng.integers(0, 2, (N, 15, W)); d["ends"][:, 4] = 255 * rng.integers(0, 2, (N, 16, C))
    d["ends"][:, 5, :, c % 2 == 0] = 0; d["nz"][:, 5, :, :, :, c % 2 == 0] = 0
    d["salt"][:, :2] = np.where(rng.random((N, 2, 16, C)) < 0.5, (W - 1) * rng.integers(0, 2, (N, 2, 16, C)), d["salt"][:, :2])
    d["salt"][:, 0, 0] = (W - 1) * (((c >> 2) + np.arange(N)[:, None]) & 1)
    d["wt"][:, 6] = 0; d["db"][:, 6, 15] = rng.integers(1, M + 1, (N, W))
    d["salt"][:, 6, 0] = 8 * np.argsort(rng.random((N, W // 8)), axis=1)[:, :C] + rng.integers(0, 8, (N, 1))
    d["sl"][:, 6, 0] = np.where((np.arange(N) & 1) == 0, 4000, -4000)[:, None]
    return pack(d)
def setup_inputs_ties(rng):
    d = parts(rng); r = np.arange(N)
    d["ends"][:, 0] = 0; d["nz"][:, 0] = 0; d["db"][:, 0, :15] = 0
    for g, b in ((1, (r >> 1) & 1), (2, r & 1)):
        b = b[:, None, None]
        d["ends"][:, g] = np.abs(255 * b - rng.integers(0, 16, (N, 16, C))); d["nz"][:, g] = 0
        d["db"][:, g, :15] = np.abs(255 * np.roll(b, 1, axis=0) - rng.integers(0, 16, (N, 15, W)))
    for k in ("ends", "wt", "nz"): d[k][:, :, 15] = 0
    walk(d["ends"], d["db"], d["wt"], d["salt"], d["nz"], d["sl"], rng.integers(-1, 2, (N, 8, RU, C)))
    return pack(d)
def setup_inputs_spread(rng):
    d = parts(rng)
    d["ends"] = (np.exp2(8 * rng.random((N, 8, 1, C))) * rng.random((N, 8, 16, C))).astype(np.int64)
    d["nz"] = (np.exp2(8 * rng.random((N, 8, 1, RU, S, C))) * rng.random((N, 8, 16, RU, S, C))).astype(np.int64)
    d["db"] = (np.exp2(8 * rng.random((N, 8, 1, W))) * rng.random((N, 8, 16, W))).astype(np.int16)
    d["db"][:, :, 15] = np.minimum((M + 1) * rng.random((N, 8, W)) ** rng.choice(np.array([0.5, 1.0, 3.0]), (N, 8, 1)), M).astype(np.int16)
    d["wt"] = np.minimum((np.exp2(4.2 * rng.random((N, 8, 1, 16))) * rng.random((N, 8, 16, 16))).astype(np.int64), 17)
    d["sl"] = rng.integers(-4000, 4001, (N, 8, RU, C))
    return pack(d)
def check_inputs(d):
    bad = []
    for k, lo, hi in (("ends", 0, 255), ("db", 0, 255), ("wt", 0, 17), ("salt", 0, W - 1), ("nz", 0, 255), ("sl", -4000, 4000)):
        x = np.asarray(d[k]).astype(np.float64)
        if not (np.min(x) >= lo and np.max(x) <= hi): bad.append("range of " + k)
        elif np.any(x != np.floor(x)): bad.append("whole numbers in " + k)
    for k, hi in (("ends", 0), ("wt", 0), ("nz", 0), ("db", M)):
        x = np.asarray(d[k]).astype(np.float64).reshape(N, 8, 16, -1)[:, :, 15]
        if not np.max(x) <= hi: bad.append("rows 16*g + 15 of " + k)
    return bad
def reference(ends, db, wt, salt, nz, sl):
    h = [x.astype(np.float32).astype(np.int32) for x in (ends, db, wt, nz)]
    e, ok, place = walk(h[0].reshape(N, 8, 16, C), h[1].reshape(N, 8, 16, W), h[2].reshape(N, 8, 16, 16), salt.reshape(N, 8, 16, C), h[3].reshape(N, 8, 16, RU, S, C), sl.astype(np.int64).reshape(N, 8, RU, C))
    return {"ye": e.reshape(N, 128, C).astype(np.float32).astype(BF), "yv": ok.reshape(N, 8, RU * C).astype(np.float32), "yp": place.reshape(N, 8, RU * S * C).astype(np.float32)}

@@ -1,0 +1,541 @@
+import numpy as np
+from concourse.mybir import AluOpType as ALU, ActivationFunctionType as AF
+
+F32, BF16, I32, U16 = "float32", "bfloat16", "int32", "uint16"
+RU, ST = 3, 3
+MAGIC = 12582912.0
+BIG = 8192.0
+FA, PAD, DB, DUM, FB, WEND = 0, 192, 208, 4304, 4496, 4688
+OPT = {"g1": "VS", "g2": "VS", "f": "S", "y": "S", "tries": 500, "seed": 0}
+
+SCRATCH = {
+    "win": ("sbuf", [128, WEND], BF16), "endn": ("sbuf", [128, 128], BF16), "wtb": ("sbuf", [128, 16], BF16),
+    "salti": ("sbuf", [128, 128], I32), "nzb": ("sbuf", [128, 1152], BF16), "sli": ("sbuf", [128, 384], I32),
+    "slf": ("sbuf", [128, 384], F32), "saltf": ("sbuf", [128, 2, 4, 16], F32), "salt8": ("sbuf", [128, 384], F32),
+    "nzp": ("sbuf", [128, 18, 4, 16], BF16), "own": ("sbuf", [128, 6, 4, 16], BF16),
+    "prv": ("sbuf", [128, 384], BF16), "nxt": ("sbuf", [128, 384], BF16),
+    "dif": ("sbuf", [128, 144], F32), "gi": ("sbuf", [128, 128], F32), "ai": ("sbuf", [128, 192], F32), "xi": ("sbuf", [128, 192], F32),
+    "pi": ("sbuf", [128, 4], I32), "pc": ("sbuf", [128, 8], F32),
+    "ident": ("sbuf", [128, 128], BF16), "idh": ("sbuf", [128, 128], BF16), "idq": ("sbuf", [128, 128], BF16),
+    "nid": ("sbuf", [128, 128], BF16), "idb": ("sbuf", [128, 128], BF16), "n128": ("sbuf", [128, 128], BF16),
+    "zb": ("sbuf", [128, 144], BF16), "blk": ("sbuf", [128, 128], BF16),
+    "blkf": ("sbuf", [128, 128], F32), "blk8": ("sbuf", [128, 128], BF16), "trib": ("sbuf", [128, 128], BF16),
+    "trif": ("sbuf", [128, 128], F32), "ntrif": ("sbuf", [128, 128], F32), "tmp": ("sbuf", [128, 768], F32),
+    "sel15": ("sbuf", [128, 128], BF16), "sel8": ("sbuf", [128, 128], F32), "wbd": ("sbuf", [128, 128], BF16),
+    "cst": ("sbuf", [128, 368], BF16), "keep": ("sbuf", [128, 512], BF16), "rst": ("sbuf", [128, 512], BF16),
+    "dg0": ("sbuf", [128, 192], F32), "cc": ("sbuf", [128, 192], BF16),
+    "yeb": ("sbuf", [128, 128], BF16), "yvb": ("sbuf", [128, 384], F32), "ypb": ("sbuf", [128, 1152], F32),
+}
+for _q in range(2):
+    for _n, _w, _d in (("v", 192, BF16), ("um", 64, F32), ("ui", 64, I32), ("ask", 64, I32), ("y", 64, I32),
+                       ("pl", 64, I32), ("o1", 64, U16), ("o2", 64, U16), ("da", 384, F32), ("dbb", 384, F32),
+                       ("so", 128, F32), ("ga", 1024, BF16), ("gb", 1024, BF16), ("hi", 1024, BF16), ("lo", 1024, BF16),
+                       ("fq", 64, F32), ("ab", 128, BF16), ("bsl", 64, F32),
+                       ("acc", 64, BF16), ("dl", 64, BF16), ("rec", 192, BF16), ("pm", 192, F32), ("hold", 192, F32),
+                       ("eq", 384, BF16), ("drop", 192, F32), ("offf", 12, F32), ("offs", 12, U16)):
+        SCRATCH["%s%d" % (_n, _q)] = ("sbuf", [128, _w], _d)
+    SCRATCH["sp%d" % _q] = ("sbuf", [128, 3, 4, 16], F32)
+    SCRATCH["sa%d" % _q] = ("sbuf", [128, 3, 4, 16], BF16)
+    for _k in range(4):
+        SCRATCH["ps%d%d" % (_q, _k)] = ("psum", [128, 512], F32)
+
+LOADS = ["l_end", "l_wt", "l_salt", "l_nz", "l_sl", "l_db0", "l_db1"]
+STORES = ["s_ye", "s_yv", "s_yp0", "s_yp1", "s_yp2"]
+ARRIVALS = ["a_p0"] + ["a_p%d%d" % (m, q) for m in range(1, RU) for q in range(2)] + ["a_n%d" % m for m in range(RU)]
+SEMAPHORES = ["cV", "cS", "cP", "cG", "sent"] + LOADS + STORES + ARRIVALS
+
+PICTURES = [dict(c=1.04, p=0.52, hop=110.0, own=70.0, fix=15.0, g=1.56, s=3.8, net=2800.0),
+            dict(c=0.9, p=0.9, hop=60.0, own=40.0, fix=40.0, g=1.2, s=2.5, net=2200.0),
+            dict(c=1.15, p=0.6, hop=200.0, own=150.0, fix=30.0, g=1.9, s=5.0, net=3600.0)]
+
+
+def A(name, c0, c1, step=1, p0=0, p1=128, ps=1):
+    return (name, c0, c1, step, p0, p1, ps)
+
+
+def cnt(a):
+    return len(range(a[1], a[2], a[3])) if a[3] > 0 else (a[2] - a[1]) // 4
+
+
+def res(T, a):
+    if not isinstance(a, tuple):
+        return a
+    if a[3] <= 0:
+        return T[a[0]][:, a[1] // 64:a[2] // 64, -a[3], :]
+    if len(SCRATCH[a[0]][1]) == 4:
+        if a[1] % 64 == 0 and a[2] % 64 == 0:
+            return T[a[0]][:, a[1] // 64:a[2] // 64]
+        return T[a[0]][:, a[1] // 64, a[1] % 64 // 16]
+    return T[a[0]][a[4]:a[5]:a[6], a[1]:a[2]:a[3]]
+
+
+def two(a):
+    return SCRATCH[a[0]][2] in (BF16, U16)
+
+
+def psum(a):
+    return SCRATCH[a[0]][0] == "psum"
+
+
+def meet(a, b, exact):
+    if exact and a[3] <= 0 and b[3] <= 0 and a[3] != b[3]:
+        return False
+    la, lb = [x[1] + (cnt(x) - 1) * x[3] if x[3] > 0 else x[2] - 1 for x in (a, b)]
+    if la < b[1] or lb < a[1]:
+        return False
+    if exact and a[3] == b[3] and a[3] > 1 and (a[1] - b[1]) % a[3]:
+        return False
+    return True
+
+
+def build():
+    ops, seen = [], {}
+
+    def add(eng, fn, reads, writes, cost, sem=None, late=0.0, after=()):
+        i = len(ops)
+        deps = {}
+        for d in after:
+            deps[d] = True
+        for acc, wr in [(a, False) for a in reads if isinstance(a, tuple)] + [(a, True) for a in writes]:
+            for j, b, bw in seen.get(acc[0], []):
+                o = ops[j]
+                same = o["eng"] == eng and o["sem"] is None and sem is None
+                if psum(acc):
+                    if same and not (wr or bw):
+                        continue
+                    need = (not same) or (eng != "P" and meet(acc, b, True))
+                elif (wr or bw) and meet(acc, b, same):
+                    need = True
+                else:
+                    continue
+                deps[j] = deps.get(j, False) or need
+        for a in reads:
+            if isinstance(a, tuple):
+                seen.setdefault(a[0], []).append((i, a, False))
+        for a in writes:
+            seen.setdefault(a[0], []).append((i, a, True))
+        ops.append(dict(eng=eng, fn=fn, deps=deps, cost=cost, sem=sem, late=late))
+        return i
+
+    def vc(n, rate):
+        return ("v", max(64.0, n * rate))
+
+    def ts(o, a, s1, s2, op0, op1=None):
+        if op1 is None:
+            fn = lambda q, T, X: q.tensor_scalar(res(T, o), res(T, a), res(T, s1), None, op0)
+        else:
+            fn = lambda q, T, X: q.tensor_scalar(res(T, o), res(T, a), res(T, s1), res(T, s2), op0, op1)
+        return add("V", fn, [a, s1, s2], [o], vc(cnt(o), 0.5 if two(o) and two(a) else 1))
+
+    def tt(o, a, b, op):
+        return add("V", lambda q, T, X: q.tensor_tensor(res(T, o), res(T, a), res(T, b), op), [a, b], [o],
+                   vc(cnt(o), 1 if psum(a) or psum(b) else 2))
+
+    def cp(o, a):
+        return add("V", lambda q, T, X: q.tensor_copy(res(T, o), res(T, a)), [a], [o], vc(cnt(o), 0.5 if two(o) and two(a) else 1))
+
+    def ms(o, val):
+        return add("V", lambda q, T, X: q.memset(res(T, o), val), [], [o], vc(cnt(o), 0.5 if two(o) else 1))
+
+    def scan(o, a, b, init, op0, op1):
+        return add("V", lambda q, T, X: q.tensor_tensor_scan(res(T, o), res(T, a), res(T, b), init, op0, op1), [a, b], [o],
+                   vc(cnt(o), 0.5 if two(o) and two(a) and two(b) else 1))
+
+    def act(o, a, func, bias=0.0, scale=1.0):
+        return add("S", lambda q, T, X: q.activation(res(T, o), res(T, a), func, bias=bias, scale=scale), [a], [o], vc(cnt(o), 1))
+
+    def mm(*terms):
+        for k, (o, l, r) in enumerate(terms):
+            wide = 4 if SCRATCH[r[0]][2] == F32 else 1
+            add("P", lambda q, T, X, o=o, l=l, r=r, k=k: q.matmul(res(T, o), res(T, l), res(T, r), k == 0, k == len(terms) - 1),
+                [l, r], [o], ("p", max(64, cnt(r)) * wide))
+
+    def gather(eng, o, w, off):
+        if eng == "V":
+            fn = lambda q, T, X: q.tensor_copy(res(T, o), res(T, w).indirect(res(T, off)))
+        else:
+            fn = lambda q, T, X: q.activation(res(T, o), res(T, w).indirect(res(T, off)), AF.Copy)
+        return add(eng, fn, [w, off], [o], ("g", cnt(o)))
+
+    def iota(o, pat, base, mult):
+        if SCRATCH[o[0]][2] == I32:
+            fn = lambda q, T, X: q.iota(res(T, o), pat, base, mult)
+        else:
+            fn = lambda q, T, X: q.iota(res(T, o), pat, base, mult, allow_small_or_imprecise_dtypes=True)
+        return add("G", fn, [], [o], ("n", 150 + 2.1 * cnt(o)))
+
+    def load(eng, sem, o, src, late):
+        return add(eng, lambda q, T, X: q.dma_start(res(T, o), src(T)), [], [o], ("n", 60), sem=(sem, 16), late=late)
+
+    def store(sem, dst, a):
+        return add("Y", lambda q, T, X: q.dma_start(dst(T), res(T, a)), [a], [], ("n", 60), sem=(sem, 16), late=2200.0)
+
+    def send(sem, to, o, a):
+        def fn(q, T, X):
+            rid, pid, mask = X[to]
+            q.remote_dma(res(T, o), res(T, a), T.sem[sem], T.sem.sent, pid, rid, mask)
+        i = add("G", fn, [a], [], ("n", 300), sem=("sent", 0))
+        return add("N", None, [], [o], ("n", 0), sem=(sem, -1), late=-1.0, after=[i])
+
+    M = lambda n: A(n, 0, 128)
+    col = lambda k: A("pc", k, k + 1)
+    ID = M("ident")
+
+    y0 = load("Y", "l_end", M("endn"), lambda T: T.ends[:], 2200.0)
+    load("S", "l_db0", A("win", DB, DB + 2048), lambda T: T.db[:, 0:2048], 6000.0)
+    load("Y", "l_wt", A("wtb", 0, 16), lambda T: T.wt[:], 3000.0)
+    load("Y", "l_salt", M("salti"), lambda T: T.salt[:], 3000.0)
+    load("Y", "l_db1", A("win", DB + 2048, DUM), lambda T: T.db[:, 2048:4096], 6000.0)
+    load("S", "l_nz", A("nzb", 0, 1152), lambda T: T.nz[:], 6500.0)
+    load("Y", "l_sl", A("sli", 0, 384, 1, 0, 8), lambda T: T.sl[:], 6500.0)
+    for r in range(4):
+        cp(A("own", 0, 128, -r), A("endn", r, 128, 4))
+    send("a_p0", "next", A("prv", 0, 128), A("own", 0, 128))
+    send("a_n0", "prev", A("nxt", 0, 128), A("own", 0, 128))
+
+    iota(A("pi", 0, 1), [[0, 1]], 0, 1)
+    iota(A("dif", 0, 144), [[1, 144]], 0, -1)
+    iota(M("gi"), [[1, 8], [0, 16]], 0, 0)
+    ts(A("pi", 1, 2), A("pi", 0, 1), 4, None, ALU.arith_shift_right)
+    ts(A("pi", 2, 3), A("pi", 0, 1), 15, None, ALU.bitwise_and)
+    cp(A("pc", 0, 3), A("pi", 0, 3))
+    ts(col(3), col(2), 15.0, 0.5, ALU.not_equal, ALU.mult)
+    ts(col(4), col(2), 15.0, 0.25, ALU.not_equal, ALU.mult)
+    ts(col(5), col(2), 15.0, None, ALU.is_equal)
+    D128 = M("dif")
+    ts(ID, D128, 0.0, None, ALU.is_equal)
+    ts(M("blkf"), M("gi"), col(1), None, ALU.is_equal)
+    for k in range(8):
+        ts(A("wbd", 16 * k, 16 * k + 16), A("wtb", 0, 16), A("blkf", 16 * k, 16 * k + 1), 1.0 / 64, ALU.mult, ALU.mult)
+    ms(A("cst", 0, 64), -63.0 / 128)
+    ms(A("cst", 64, 128), -0.375)
+    ms(A("cst", 128, 192), 1.0)
+    ms(A("cst", 192, 256), -1.0)
+    ms(A("cst", 256, 304), 0.0)
+    ms(A("cst", 304, 320), 64.0)
+    ms(A("cst", 320, 368), 0.0)
+    for r in range(4):
+        cp(A("saltf", 0, 128, -r), A("salti", r, 128, 4))
+        cp(A("nzp", 0, 1152, -r), A("nzb", r, 1152, 4))
+    for s in range(ST):
+        act(A("salt8", 128 * s, 128 * s + 128), M("saltf"), AF.Identity, bias=8.0 * 211 * s - 148.0 ** 2, scale=8.0)
+    ts(A("zb", 0, 144), A("dif", 0, 144), 0.0, col(5), ALU.is_equal, ALU.mult)
+    ts(M("idh"), D128, 0.0, col(3), ALU.is_equal, ALU.mult)
+    ts(M("idq"), D128, 0.0, col(4), ALU.is_equal, ALU.mult)
+    act(M("nid"), ID, AF.Copy, scale=-1.0)
+    act(M("idb"), ID, AF.Copy, scale=BIG)
+    act(M("n128"), ID, AF.Copy, scale=-128.0)
+    ms(A("win", FA, DB), 0.0)
+    ms(A("win", DUM, WEND), 0.0)
+    ms(A("keep", 0, 512), 1.0)
+    ms(A("keep", 0, 512, 16), 0.0)
+    ms(A("rst", 0, 512), 0.0)
+    ms(A("rst", 0, 512, 16), 255.0)
+    ms(A("da0", 0, 384, 2), 0.0)
+    ms(A("da1", 0, 384, 2), 0.0)
+    iota(A("xi", 0, 192), [[1, 192]], 0, 0)
+    act(A("dbb0", 1, 384, 2), A("xi", 0, 192), AF.Identity, bias=float(FA))
+    act(A("da1", 1, 384, 2), A("xi", 0, 192), AF.Identity, bias=float(FB - PAD))
+    act(M("blk"), M("blkf"), AF.Copy)
+    act(M("blk8"), M("blkf"), AF.Copy, scale=2 * BIG)
+    ts(A("tmp", 0, 128), D128, 0.0, -BIG, ALU.is_gt, ALU.mult)
+    tt(A("tmp", 128, 256), A("tmp", 0, 128), M("idb"), ALU.add)
+    tt(M("trif"), A("tmp", 128, 256), M("blkf"), ALU.mult)
+    act(M("trib"), M("trif"), AF.Copy)
+    act(M("ntrif"), M("trif"), AF.Copy, scale=-1.0)
+    ms(M("sel15"), 0.0)
+    cp(A("sel15", 15, 128, 16), A("blkf", 15, 128, 16))
+    ts(A("sel8", 0, 128, 1, 0, 8), A("gi", 0, 128, 1, 0, 8), A("pc", 0, 1, 1, 0, 8), None, ALU.is_equal)
+    cp(A("slf", 0, 384, 1, 0, 8), A("sli", 0, 384, 1, 0, 8))
+    iota(A("ai", 0, 192), [[0, 12], [1, 16]], 0, 0)
+    ts(A("tmp", 256, 448), A("ai", 0, 192), col(2), 4 * BIG, ALU.not_equal, ALU.mult)
+    act(A("tmp", 448, 640), A("xi", 0, 192), AF.Identity, bias=4096.0)
+    tt(A("dg0", 0, 192), A("tmp", 448, 640), A("tmp", 256, 448), ALU.subtract)
+    act(A("cc", 0, 192), A("tmp", 256, 448), AF.Identity, bias=-3 * BIG, scale=2.0)
+
+    def views(q):
+        return (lambda n, c0=0, c1=64, st=1: A("%s%d" % (n, q), c0, c1, st)), (lambda k, c0=0, c1=64, st=1: A("ps%d%d" % (q, k), c0, c1, st))
+
+    def step(m, s, q):
+        B, P = views(q)
+        v = A("prv", 128 * m + 64 * q, 128 * m + 64 * q + 64) if s == 0 else B("v", 64 * (s - 1), 64 * s)
+        t0 = 16 * ((s - m) % 4)
+        one, pair = {0: ((16, 32), (32, 64)), 16: ((0, 16), (32, 64)), 32: ((48, 64), (0, 32)), 48: ((32, 48), (0, 32))}[t0]
+        cut = lambda o: list(zip(o, (one, pair) if len(o) == 2 else (one, (pair[0], pair[0] + 16), (pair[0] + 16, pair[1]))))
+        spans = [(a, b) for a, b in ((0, t0), (t0 + 16, 64)) if b > a]
+        n0, n1 = spans[0][0], spans[-1][1]
+        f0 = (FA if q == 0 else FB) + 64 * s
+        base = DB - FA if q == 0 else DB - PAD
+        wide = A("win", FA, DUM) if q == 0 else A("win", PAD, WEND)
+        d0 = 128 * s
+        plf = B("da" if q == 0 else "dbb", d0 + 1, d0 + 128, 2)
+        flag = B("dbb", d0, d0 + 128, 2)
+        mm((P(0), ID, A("cst", 0, 64)), (P(0), M("wbd"), v))
+        act(B("um"), P(0), AF.Identity, bias=MAGIC)
+        act(P(0, 64, 128), B("um"), AF.Square, bias=148.0 - MAGIC)
+        tt(B("y"), P(0, 64, 128), A("salt8", 128 * s + 64 * q, 128 * s + 64 * q + 64), ALU.add)
+        ts(B("pl"), B("y"), 3, 4095, ALU.arith_shift_right, ALU.bitwise_and)
+        cp(B("o1"), B("pl"))
+        for e, (a, b) in cut(OPT["g1"]):
+            gather(e, B("ga", 16 * a, 16 * b), A("win", DB, DUM), B("o1", a, b))
+        ts(B("ui"), B("um"), MAGIC, None, ALU.subtract)
+        ts(B("ask"), B("ui"), 7, None, ALU.bitwise_and)
+        ts(plf, B("pl"), float(base), None, ALU.add)
+        z = (m * ST + s) * 128 + 64 * q
+        mm((P(2), ID, A("nzp", z, z + 64)), (P(2), ID, v))
+        if OPT["f"] == "V":
+            ts(B("fq"), P(2), 256.0, -256.0, ALU.is_ge, ALU.mult)
+            tt(A("win", f0, f0 + 64), P(2), B("fq"), ALU.add)
+        else:
+            act(B("dl"), P(2), AF.Sign, bias=-255.5)
+            mm((P(2), ID, A("nzp", z, z + 64)), (P(2), ID, v), (P(2), M("n128"), B("dl")))
+            act(A("win", f0, f0 + 64), P(2), AF.Identity, bias=-128.0)
+        mm((P(0), ID, A("cst", 304 - t0, 368 - t0)),
+           *[(P(0, n0, n1), A("zb", 15 - p, 143 - p), B("ga", 16 * n0 + p, 16 * n1, 16)) for p in range(16)])
+        tt(flag, P(0), B("ask"), ALU.is_equal if q == 0 else ALU.not_equal)
+        scan(B("so", 2 * n0, 2 * n1), B("da", d0 + 2 * n0, d0 + 2 * n1), B("dbb", d0 + 2 * n0, d0 + 2 * n1), 0.0, ALU.mult, ALU.max)
+        cp(B("o2", n0, n1), B("so", 2 * n0 + 1, 2 * n1, 2))
+        parts = cut(OPT["g2"])[::-1]
+        for e, (a, b) in parts:
+            gather(e, B("gb", 16 * a, 16 * b), wide, B("o2", a, b))
+        for e, (a, b) in parts:
+            scan(B("hi", 16 * a, 16 * b), A("keep", 0, 16 * (b - a)), B("gb", 16 * a, 16 * b), 0.0, ALU.mult, ALU.max)
+            scan(B("lo", 16 * a, 16 * b), A("rst", 0, 16 * (b - a)), B("gb", 16 * a, 16 * b), 0.0, ALU.max, ALU.min)
+        terms = [(P(1), ID, A("cst", 64, 128)), (P(1), M("idh"), v), (P(1, t0, t0 + 16), M("idh"), A("win", f0 + t0, f0 + t0 + 16))]
+        for a, b in spans:
+            terms += [(P(1, a, b), M("idq"), B(n, 16 * a + 15, 16 * b, 16)) for n in ("hi", "lo")]
+        mm(*terms)
+        ts(B("v", 64 * s, 64 * s + 64), P(1), MAGIC, MAGIC, ALU.add, ALU.subtract)
+        if q == 0:
+            mm((P(3), M("trib"), A("cst", 128, 192)), (P(3), M("ntrif"), flag))
+        else:
+            mm((P(3), M("trif"), flag))
+        act(P(3, 64, 128), P(3), AF.Relu)
+        x = 64 * (2 - s)
+        tt(B("sp", x, x + 64), P(3, 64, 128), plf, ALU.min)
+        if m < RU - 1:
+            tt(B("sa", x, x + 64), P(3, 64, 128), B("ask"), ALU.min)
+        if s == ST - 1:
+            for r in range(4):
+                mm((P(3, 128 + r, 320, 4), M("blkf"), B("sp", 0, 192, -r)))
+            if OPT["y"] == "S":
+                act(P(3, 128, 320), P(3, 128, 320), AF.Relu, bias=1.0 - base)
+            for k in range(ST):
+                z = (m * ST + k) * 128 + 64 * q
+                if OPT["y"] == "S":
+                    act(A("ypb", z, z + 64), P(3, 256 - 64 * k, 320 - 64 * k), AF.Identity, bias=-1.0)
+                else:
+                    ts(A("ypb", z, z + 64), P(3, 256 - 64 * k, 320 - 64 * k), -float(base), -1.0, ALU.add, ALU.max)
+            if m < RU - 1:
+                for r in range(4):
+                    mm((P(3, 320 + r, 512, 4), M("sel15"), B("sa", 0, 192, -r)),
+                       *[(P(3, 448 - 64 * k + r, 512 - 64 * k, 4), ID, A("win", f0 - 128 + 64 * k + 16 * r, f0 - 112 + 64 * k + 16 * r)) for k in range(ST)])
+                act(B("rec", 0, 192), P(3, 320, 512), AF.Copy)
+
+    def bound(m, q):
+        B, P = views(q)
+        c = 128 * m + 64 * q
+        mm((P(2, 64, 128), ID, A("own", c, c + 64)), (P(2, 64, 128), M("nid"), A("nxt", c, c + 64)))
+        act(B("ab", 64, 128), P(2, 64, 128), AF.Abs)
+        mm((P(2, 128, 192), M("blk"), B("ab", 64, 128)),
+           *[(P(2, 128 + 16 * r, 144 + 16 * r), A("sel8", 0, 128, 1, 0, 8), A("slf", c + r, c + 64, 4, 0, 8)) for r in range(4)])
+        act(B("bsl"), P(2, 128, 192), AF.Copy)
+
+    def verdict(m, q):
+        B, P = views(q)
+        c = 128 * m + 64 * q
+        v, e = B("v", 128, 192), A("own", c, c + 64)
+        mm((P(1), ID, v), (P(1), M("nid"), A("nxt", c, c + 64)))
+        mm((P(0), ID, v), (P(0), M("nid"), e))
+        act(B("ab"), P(1), AF.Abs)
+        mm((P(2), M("blk"), B("ab")))
+        tt(B("acc"), P(2), B("bsl"), ALU.is_le)
+        tt(P(0, 64, 128), P(0), B("acc"), ALU.mult)
+        if m < RU - 1:
+            tt(A("own", c + 128, c + 192), P(0, 64, 128), e, ALU.add)
+            send("a_p%d%d" % (m + 1, q), "next", A("prv", c + 128, c + 192), A("own", c + 128, c + 192))
+        else:
+            for r in range(4):
+                tt(A("yeb", 64 * q + r, 64 * q + 64, 4), P(0, 64 + 16 * r, 80 + 16 * r), A("own", c + 16 * r, c + 16 * r + 16), ALU.add)
+        for r in range(4):
+            mm((P(2, 192 + r, 256, 4), ID, A("cst", 192, 208)), (P(2, 192 + r, 256, 4), M("idb"), B("acc", 16 * r, 16 * r + 16)))
+        if m < RU - 1:
+            for s in range(ST):
+                z = (m * ST + s) * 128 + 64 * q
+                tt(P(1, 64 * (2 - s), 64 * (3 - s)), P(2, 192, 256), A("ypb", z, z + 64), ALU.min)
+        act(A("yvb", c, c + 64), P(2, 192, 256), AF.Identity, bias=1.0 / BIG, scale=1.0 / BIG)
+        if m < RU - 1:
+            tt(B("pm", 0, 192), P(1, 0, 192), A("cc", 0, 192), ALU.max)
+            scan(B("hold", 0, 192), A("dg0", 0, 192), B("pm", 0, 192), -5.0, ALU.max, ALU.min)
+            tt(B("eq", 0, 192), P(1, 0, 192), B("hold", 0, 192), ALU.is_equal)
+            tt(B("eq", 192, 368), P(1, 16, 192), B("hold", 0, 176), ALU.is_equal)
+            mm((P(0, 0, 192), ID, A("cc", 0, 192)), (P(0, 0, 192), M("blk8"), B("eq", 0, 192)), (P(0, 16, 192), M("blk8"), B("eq", 192, 368)))
+            scan(B("drop", 0, 192), A("dg0", 0, 192), P(0, 0, 192), -5.0, ALU.max, ALU.min)
+            tt(B("offf", 0, 12), B("drop", 15, 192, 16), B("hold", 15, 192, 16), ALU.max)
+            ts(B("offs", 0, 12), B("offf", 0, 12), float(DB - PAD), None, ALU.add)
+
+    def commit(m):
+        send("a_n%d" % (m + 1), "prev", A("nxt", 128 * m + 128, 128 * m + 256), A("own", 128 * m + 128, 128 * m + 256))
+        w = A("win", PAD, FB)
+        for s in range(ST):
+            for q in (1, 0):
+                for b in (5 - 2 * s, 4 - 2 * s):
+                    src, off = A("rec%d" % q, 32 * b, 32 * b + 32), A("offs%d" % q, 2 * b, 2 * b + 2)
+                    add("V", lambda e, T, X, src=src, off=off: e.tensor_copy(res(T, w).indirect(res(T, off)), res(T, src)),
+                        [src, off], [w], ("s", 32))
+
+    def places(m):
+        store("s_yp%d" % m, lambda T: T.yp[:, 384 * m:384 * m + 384], A("ypb", 384 * m, 384 * m + 384, 1, 0, 128, 16))
+
+    for m in range(RU):
+        for s in range(ST):
+            for q in (1, 0):
+                step(m, s, q)
+                if s == 1:
+                    bound(m, q)
+        for q in (1, 0):
+            verdict(m, q)
+        if m < RU - 1:
+            commit(m)
+        places(m)
+    store("s_ye", lambda T: T.ye[:], M("yeb"))
+    store("s_yv", lambda T: T.yv[:], A("yvb", 0, 384, 1, 0, 128, 16))
+    return ops
+
+
+def price(ops, k):
+    cost = []
+    for o in ops:
+        kind, n = o["cost"]
+        cost.append({"v": k["fix"] + n * k["c"], "p": 5 + n * k["p"], "g": 65 + n * k["g"] * k["c"], "s": 55 + n * k["s"] * k["c"], "n": n}[kind])
+    late = [k["net"] if o["late"] < 0 else o["late"] for o in ops]
+    pred = [[(d, (late[d] + (k["own"] if ops[d]["eng"] == o["eng"] else k["hop"])) if need else 0.0) for d, need in o["deps"].items()] for o in ops]
+    return cost, late, pred
+
+
+def replay(ops, order, priced):
+    cost, late, pred = priced
+    done, free = {}, {}
+    for i in order:
+        e = ops[i]["eng"]
+        done[i] = free[e] = max([free.get(e, 0.0)] + [done[d] + w for d, w in pred[i]]) + cost[i]
+    return max(done[i] + late[i] for i in order), done
+
+
+def schedule(ops, priced, noise, look):
+    cost, late, pred = priced
+    n = len(ops)
+    succ = [[] for _ in ops]
+    for i in range(n):
+        for d, w in pred[i]:
+            succ[d].append((i, w))
+    level = [0.0] * n
+    for i in range(n - 1, -1, -1):
+        level[i] = cost[i] + max([w + level[j] for j, w in succ[i]] + [late[i]])
+    level = [x + y for x, y in zip(level, noise)]
+    for i in range(len(LOADS)):
+        level[i] = 1e9 - i
+    left = [len(p) for p in pred]
+    can = [0.0] * n
+    ready = [i for i in range(n) if left[i] == 0]
+    free, order = {}, []
+    while ready:
+        first = min(ready, key=lambda i: (max(can[i], free.get(ops[i]["eng"], 0.0)), -level[i]))
+        e = ops[first]["eng"]
+        t = max(can[first], free.get(e, 0.0))
+        i = max((j for j in ready if ops[j]["eng"] == e and can[j] <= t + look * cost[first]), key=lambda j: level[j])
+        free[e] = max(can[i], free.get(e, 0.0)) + cost[i]
+        order.append(i)
+        ready.remove(i)
+        for j, w in succ[i]:
+            can[j] = max(can[j], free[e] + w)
+            left[j] -= 1
+            if left[j] == 0:
+                ready.append(j)
+    return order
+
+
+PLAN = {}
+
+
+def plan():
+    if not PLAN:
+        ops = build()
+        n = len(ops)
+        priced = [price(ops, k) for k in PICTURES]
+        rng = np.random.RandomState(OPT["seed"])
+        best, noise = None, np.zeros(n)
+        for t in range(OPT["tries"]):
+            z = noise.copy()
+            if t:
+                a, w = rng.randint(n), (5, 20, 80, 200)[rng.randint(4)]
+                z[a:a + w] += rng.randn() * 600 if rng.rand() < 0.5 else rng.randn(len(z[a:a + w])) * 300
+            order = schedule(ops, priced[0], z.tolist(), 0.3)
+            ends = [replay(ops, order, p)[0] for p in priced]
+            score = ends[0] + ends[1] + 0.8 * ends[2]
+            if best is None or score <= best[0]:
+                best, noise = (score, order, ends), z
+        order = best[1]
+        place = {i: k for k, i in enumerate(order)}
+        for o in ops:
+            last = {}
+            for d, need in o["deps"].items():
+                if need:
+                    key = ops[d]["eng"] if ops[d]["sem"] is None else d
+                    if key not in last or place[d] > place[last[key]]:
+                        last[key] = d
+            o["waits"] = list(last.values())
+        seen, wanted = {}, set()
+        for i in order:
+            o = ops[i]
+            for d in o["waits"]:
+                key = (o["eng"], ops[d]["eng"])
+                if ops[d]["sem"] is None and seen.get(key, -1) < place[d]:
+                    seen[key] = place[d]
+                    wanted.add(d)
+        total = {}
+        for i in order:
+            o = ops[i]
+            if i in wanted:
+                total[o["eng"]] = total.get(o["eng"], 0) + 1
+            o["tick"] = total.get(o["eng"], 0)
+        PLAN.update(ops=ops, order=order, total=total, wanted=wanted, ends=best[2], priced=priced)
+    return PLAN
+
+
+def rank_program(g, core, T, topo):
+    rank = T.rank_of(core)
+    if rank is None:
+        return
+    n = len(T.cores)
+    after, before = T.cores[(rank + 1) % n], T.cores[(rank - 1) % n]
+    X = {name: tuple(topo.addr(other, core)) + (topo.mask(core, other),) for name, other in (("next", after), ("prev", before))}
+    came = {"p": len(topo.engines(before, core)), "n": len(topo.engines(after, core))}
+    p = plan()
+    ops = p["ops"]
+    queue = {"V": g.vector, "S": g.scalar, "P": g.tensor, "G": g, "Y": g.sync}
+    known = {}
+    for i in p["order"]:
+        o = ops[i]
+        if o["eng"] == "N":
+            continue
+        q = queue[o["eng"]]
+        for d in o["waits"]:
+            b = ops[d]
+            if b["sem"] is None:
+                sem, val = "c" + b["eng"], b["tick"]
+            elif b["eng"] == "N":
+                sem, val = b["sem"][0], came[b["sem"][0][2]]
+            else:
+                sem, val = b["sem"]
+            if known.get((o["eng"], sem), 0) < val:
+                q.wait_ge(T.sem[sem], val)
+                known[(o["eng"], sem)] = val
+        ins = o["fn"](q, T, X)
+        if i in p["wanted"]:
+            ins.then_inc(T.sem["c" + o["eng"]], 1)
+        elif o["sem"] is not None and o["sem"][1] == 16:
+            ins.then_inc(T.sem[o["sem"][0]], 16)
+    g.wait_ge(T.sem.sent, len(topo.engines(core, after)) * (2 * RU - 1) + len(topo.engines(core, before)) * RU)
+    for sem in STORES:
+        g.sync.wait_ge(T.sem[sem], 16)

@@ -6,33 +6,33 @@ RU, ST = 3, 3
 MAGIC = 12582912.0
 BIG = 8192.0
 FA, PAD, DB, DUM, FB, WEND = 0, 192, 208, 4304, 4496, 4688
-OPT = {"g1": "VS", "g2": "VS", "f": "S", "y": "S", "tries": 500, "seed": 0}
 
 SCRATCH = {
     "win": ("sbuf", [128, WEND], BF16), "endn": ("sbuf", [128, 128], BF16), "wtb": ("sbuf", [128, 16], BF16),
     "salti": ("sbuf", [128, 128], I32), "nzb": ("sbuf", [128, 1152], BF16), "sli": ("sbuf", [128, 384], I32),
     "slf": ("sbuf", [128, 384], F32), "saltf": ("sbuf", [128, 2, 4, 16], F32), "salt8": ("sbuf", [128, 384], F32),
     "nzp": ("sbuf", [128, 18, 4, 16], BF16), "own": ("sbuf", [128, 6, 4, 16], BF16),
-    "prv": ("sbuf", [128, 384], BF16), "nxt": ("sbuf", [128, 384], BF16),
+    "prv": ("sbuf", [128, 384], BF16), "prp": ("sbuf", [128, 2, 4, 16], BF16), "dlt": ("sbuf", [128, 384], BF16),
+    "nxt": ("sbuf", [128, 384], BF16),
     "dif": ("sbuf", [128, 144], F32), "gi": ("sbuf", [128, 128], F32), "ai": ("sbuf", [128, 192], F32), "xi": ("sbuf", [128, 192], F32),
     "pi": ("sbuf", [128, 4], I32), "pc": ("sbuf", [128, 8], F32),
     "ident": ("sbuf", [128, 128], BF16), "idh": ("sbuf", [128, 128], BF16), "idq": ("sbuf", [128, 128], BF16),
     "nid": ("sbuf", [128, 128], BF16), "idb": ("sbuf", [128, 128], BF16), "n128": ("sbuf", [128, 128], BF16),
-    "zb": ("sbuf", [128, 144], BF16), "blk": ("sbuf", [128, 128], BF16),
+    "zb": ("sbuf", [128, 144], BF16), "blk": ("sbuf", [128, 128], BF16), "nblk": ("sbuf", [128, 128], BF16), "blk2": ("sbuf", [128, 128], BF16),
     "blkf": ("sbuf", [128, 128], F32), "blk8": ("sbuf", [128, 128], BF16), "trib": ("sbuf", [128, 128], BF16),
     "trif": ("sbuf", [128, 128], F32), "ntrif": ("sbuf", [128, 128], F32), "tmp": ("sbuf", [128, 768], F32),
     "sel15": ("sbuf", [128, 128], BF16), "sel8": ("sbuf", [128, 128], F32), "wbd": ("sbuf", [128, 128], BF16),
-    "cst": ("sbuf", [128, 368], BF16), "keep": ("sbuf", [128, 512], BF16), "rst": ("sbuf", [128, 512], BF16),
+    "cst": ("sbuf", [128, 368], BF16), "keep": ("sbuf", [128, 768], BF16), "rst": ("sbuf", [128, 768], BF16),
     "dg0": ("sbuf", [128, 192], F32), "cc": ("sbuf", [128, 192], BF16),
     "yeb": ("sbuf", [128, 128], BF16), "yvb": ("sbuf", [128, 384], F32), "ypb": ("sbuf", [128, 1152], F32),
 }
 for _q in range(2):
-    for _n, _w, _d in (("v", 192, BF16), ("um", 64, F32), ("ui", 64, I32), ("ask", 64, I32), ("y", 64, I32),
+    for _n, _w, _d in (("v", 192, BF16), ("um", 64, F32), ("ui", 64, I32), ("ask", 192, I32), ("y", 64, I32),
                        ("pl", 64, I32), ("o1", 64, U16), ("o2", 64, U16), ("da", 384, F32), ("dbb", 384, F32),
                        ("so", 128, F32), ("ga", 1024, BF16), ("gb", 1024, BF16), ("hi", 1024, BF16), ("lo", 1024, BF16),
-                       ("fq", 64, F32), ("ab", 128, BF16), ("bsl", 64, F32),
+                       ("ab", 128, BF16), ("bsl", 64, F32),
                        ("acc", 64, BF16), ("dl", 64, BF16), ("rec", 192, BF16), ("pm", 192, F32), ("hold", 192, F32),
-                       ("eq", 384, BF16), ("drop", 192, F32), ("offf", 12, F32), ("offs", 12, U16)):
+                       ("eq", 768, BF16), ("drop", 192, F32), ("offf", 12, F32), ("offs", 12, U16)):
         SCRATCH["%s%d" % (_n, _q)] = ("sbuf", [128, _w], _d)
     SCRATCH["sp%d" % _q] = ("sbuf", [128, 3, 4, 16], F32)
     SCRATCH["sa%d" % _q] = ("sbuf", [128, 3, 4, 16], BF16)
@@ -44,9 +44,9 @@ STORES = ["s_ye", "s_yv", "s_yp0", "s_yp1", "s_yp2"]
 ARRIVALS = ["a_p0"] + ["a_p%d%d" % (m, q) for m in range(1, RU) for q in range(2)] + ["a_n%d" % m for m in range(RU)]
 SEMAPHORES = ["cV", "cS", "cP", "cG", "sent"] + LOADS + STORES + ARRIVALS
 
-PICTURES = [dict(c=1.04, p=0.52, hop=110.0, own=70.0, fix=15.0, g=1.56, s=3.8, net=2800.0),
-            dict(c=0.9, p=0.9, hop=60.0, own=40.0, fix=40.0, g=1.2, s=2.5, net=2200.0),
-            dict(c=1.15, p=0.6, hop=200.0, own=150.0, fix=30.0, g=1.9, s=5.0, net=3600.0)]
+PICTURE = dict(c=0.83, p=0.5, hop=220.0, own=160.0, fix=30.0, g=1.5, s=3.8, net=4500.0)
+MOVES = [8, 11, 16, 25, 26, 53, 57, 60, 65, 87, 88, 92, 96, 102, 106, 109, 185, 203, 230, 234, 243, 259, 279, 282, 283, 320,
+         325, 363, 387, 426, 480, 494, 537, 557, 585, 733, 749, 780, 871, 926, 935, 983, 1014, 1018, 1049, 1073, 1074, 1144]
 
 
 def A(name, c0, c1, step=1, p0=0, p1=128, ps=1):
@@ -181,16 +181,18 @@ def build():
     col = lambda k: A("pc", k, k + 1)
     ID = M("ident")
 
-    y0 = load("Y", "l_end", M("endn"), lambda T: T.ends[:], 2200.0)
+    load("Y", "l_end", M("endn"), lambda T: T.ends[:], 2200.0)
     load("S", "l_db0", A("win", DB, DB + 2048), lambda T: T.db[:, 0:2048], 6000.0)
     load("Y", "l_wt", A("wtb", 0, 16), lambda T: T.wt[:], 3000.0)
     load("Y", "l_salt", M("salti"), lambda T: T.salt[:], 3000.0)
     load("Y", "l_db1", A("win", DB + 2048, DUM), lambda T: T.db[:, 2048:4096], 6000.0)
     load("S", "l_nz", A("nzb", 0, 1152), lambda T: T.nz[:], 6500.0)
     load("Y", "l_sl", A("sli", 0, 384, 1, 0, 8), lambda T: T.sl[:], 6500.0)
+    send("a_p0", "next", A("prv", 0, 128), A("endn", 0, 128))
     for r in range(4):
         cp(A("own", 0, 128, -r), A("endn", r, 128, 4))
-    send("a_p0", "next", A("prv", 0, 128), A("own", 0, 128))
+    for r in range(4):
+        cp(A("prp", 0, 128, -r), A("prv", r, 128, 4))
     send("a_n0", "prev", A("nxt", 0, 128), A("own", 0, 128))
 
     iota(A("pi", 0, 1), [[0, 1]], 0, 1)
@@ -227,16 +229,18 @@ def build():
     act(M("n128"), ID, AF.Copy, scale=-128.0)
     ms(A("win", FA, DB), 0.0)
     ms(A("win", DUM, WEND), 0.0)
-    ms(A("keep", 0, 512), 1.0)
-    ms(A("keep", 0, 512, 16), 0.0)
-    ms(A("rst", 0, 512), 0.0)
-    ms(A("rst", 0, 512, 16), 255.0)
+    ms(A("keep", 0, 768), 1.0)
+    ms(A("keep", 0, 768, 16), 0.0)
+    ms(A("rst", 0, 768), 0.0)
+    ms(A("rst", 0, 768, 16), 255.0)
     ms(A("da0", 0, 384, 2), 0.0)
     ms(A("da1", 0, 384, 2), 0.0)
     iota(A("xi", 0, 192), [[1, 192]], 0, 0)
     act(A("dbb0", 1, 384, 2), A("xi", 0, 192), AF.Identity, bias=float(FA))
     act(A("da1", 1, 384, 2), A("xi", 0, 192), AF.Identity, bias=float(FB - PAD))
     act(M("blk"), M("blkf"), AF.Copy)
+    act(M("nblk"), M("blkf"), AF.Copy, scale=-1.0)
+    act(M("blk2"), M("blkf"), AF.Copy, scale=2.0)
     act(M("blk8"), M("blkf"), AF.Copy, scale=2 * BIG)
     ts(A("tmp", 0, 128), D128, 0.0, -BIG, ALU.is_gt, ALU.mult)
     tt(A("tmp", 128, 256), A("tmp", 0, 128), M("idb"), ALU.add)
@@ -258,10 +262,24 @@ def build():
 
     def step(m, s, q):
         B, P = views(q)
-        v = A("prv", 128 * m + 64 * q, 128 * m + 64 * q + 64) if s == 0 else B("v", 64 * (s - 1), 64 * s)
+
+        def of_v(k, l):
+            if s:
+                return [(P(k), l, B("v", 64 * (s - 1), 64 * s))]
+            if m == 0:
+                return [(P(k, 16 * r, 16 * r + 16), l, A("prv", 64 * q + r, 64 * q + 64, 4)) for r in range(4)]
+            return [(P(k), l, A("prp", 64 * q, 64 * q + 64))] + [(P(k), l, A("prv", 128 * j + 64 * q, 128 * j + 64 * q + 64)) for j in range(1, m + 1)]
         t0 = 16 * ((s - m) % 4)
         one, pair = {0: ((16, 32), (32, 64)), 16: ((0, 16), (32, 64)), 32: ((48, 64), (0, 32)), 48: ((32, 48), (0, 32))}[t0]
-        cut = lambda o: list(zip(o, (one, pair) if len(o) == 2 else (one, (pair[0], pair[0] + 16), (pair[0] + 16, pair[1]))))
+
+        def cut(e):
+            if not e:
+                return [("V", one), ("S", pair)]
+            if one[1] == pair[0]:
+                return [("V", (one[0], one[1] + e)), ("S", (pair[0] + e, pair[1]))]
+            if one[0] == pair[1]:
+                return [("V", (one[0] - e, one[1])), ("S", (pair[0], pair[1] - e))]
+            return [("V", one), ("V", (pair[0], pair[0] + e)), ("S", (pair[0] + e, pair[1]))]
         spans = [(a, b) for a, b in ((0, t0), (t0 + 16, 64)) if b > a]
         n0, n1 = spans[0][0], spans[-1][1]
         f0 = (FA if q == 0 else FB) + 64 * s
@@ -270,66 +288,57 @@ def build():
         d0 = 128 * s
         plf = B("da" if q == 0 else "dbb", d0 + 1, d0 + 128, 2)
         flag = B("dbb", d0, d0 + 128, 2)
-        mm((P(0), ID, A("cst", 0, 64)), (P(0), M("wbd"), v))
+        ask = B("ask", 64 * s, 64 * s + 64)
+        mm((P(0), ID, A("cst", 0, 64)), *of_v(0, M("wbd")))
         act(B("um"), P(0), AF.Identity, bias=MAGIC)
         act(P(0, 64, 128), B("um"), AF.Square, bias=148.0 - MAGIC)
         tt(B("y"), P(0, 64, 128), A("salt8", 128 * s + 64 * q, 128 * s + 64 * q + 64), ALU.add)
         ts(B("pl"), B("y"), 3, 4095, ALU.arith_shift_right, ALU.bitwise_and)
         cp(B("o1"), B("pl"))
-        for e, (a, b) in cut(OPT["g1"]):
+        for e, (a, b) in cut(8):
             gather(e, B("ga", 16 * a, 16 * b), A("win", DB, DUM), B("o1", a, b))
         ts(B("ui"), B("um"), MAGIC, None, ALU.subtract)
-        ts(B("ask"), B("ui"), 7, None, ALU.bitwise_and)
+        ts(ask, B("ui"), 7, None, ALU.bitwise_and)
         ts(plf, B("pl"), float(base), None, ALU.add)
         z = (m * ST + s) * 128 + 64 * q
-        mm((P(2), ID, A("nzp", z, z + 64)), (P(2), ID, v))
-        if OPT["f"] == "V":
-            ts(B("fq"), P(2), 256.0, -256.0, ALU.is_ge, ALU.mult)
-            tt(A("win", f0, f0 + 64), P(2), B("fq"), ALU.add)
-        else:
-            act(B("dl"), P(2), AF.Sign, bias=-255.5)
-            mm((P(2), ID, A("nzp", z, z + 64)), (P(2), ID, v), (P(2), M("n128"), B("dl")))
-            act(A("win", f0, f0 + 64), P(2), AF.Identity, bias=-128.0)
+        mm((P(2), ID, A("nzp", z, z + 64)), *of_v(2, ID))
+        act(B("dl"), P(2), AF.Sign, bias=-255.5)
+        mm((P(2), ID, A("nzp", z, z + 64)), *of_v(2, ID), (P(2), M("n128"), B("dl")))
+        act(A("win", f0, f0 + 64), P(2), AF.Identity, bias=-128.0)
         mm((P(0), ID, A("cst", 304 - t0, 368 - t0)),
            *[(P(0, n0, n1), A("zb", 15 - p, 143 - p), B("ga", 16 * n0 + p, 16 * n1, 16)) for p in range(16)])
-        tt(flag, P(0), B("ask"), ALU.is_equal if q == 0 else ALU.not_equal)
+        tt(flag, P(0), ask, ALU.is_equal if q == 0 else ALU.not_equal)
         scan(B("so", 2 * n0, 2 * n1), B("da", d0 + 2 * n0, d0 + 2 * n1), B("dbb", d0 + 2 * n0, d0 + 2 * n1), 0.0, ALU.mult, ALU.max)
         cp(B("o2", n0, n1), B("so", 2 * n0 + 1, 2 * n1, 2))
-        parts = cut(OPT["g2"])[::-1]
-        for e, (a, b) in parts:
+        for e, (a, b) in cut(0)[::-1]:
             gather(e, B("gb", 16 * a, 16 * b), wide, B("o2", a, b))
-        for e, (a, b) in parts:
+        for a, b in spans:
             scan(B("hi", 16 * a, 16 * b), A("keep", 0, 16 * (b - a)), B("gb", 16 * a, 16 * b), 0.0, ALU.mult, ALU.max)
             scan(B("lo", 16 * a, 16 * b), A("rst", 0, 16 * (b - a)), B("gb", 16 * a, 16 * b), 0.0, ALU.max, ALU.min)
-        terms = [(P(1), ID, A("cst", 64, 128)), (P(1), M("idh"), v), (P(1, t0, t0 + 16), M("idh"), A("win", f0 + t0, f0 + t0 + 16))]
+        terms = [(P(1), ID, A("cst", 64, 128)), *of_v(1, M("idh")), (P(1, t0, t0 + 16), M("idh"), A("win", f0 + t0, f0 + t0 + 16))]
         for a, b in spans:
             terms += [(P(1, a, b), M("idq"), B(n, 16 * a + 15, 16 * b, 16)) for n in ("hi", "lo")]
         mm(*terms)
         ts(B("v", 64 * s, 64 * s + 64), P(1), MAGIC, MAGIC, ALU.add, ALU.subtract)
         if q == 0:
-            mm((P(3), M("trib"), A("cst", 128, 192)), (P(3), M("ntrif"), flag))
+            mm((P(3, 64 * s, 64 * s + 64), M("trib"), A("cst", 128, 192)), (P(3, 64 * s, 64 * s + 64), M("ntrif"), flag))
         else:
-            mm((P(3), M("trif"), flag))
-        act(P(3, 64, 128), P(3), AF.Relu)
-        x = 64 * (2 - s)
-        tt(B("sp", x, x + 64), P(3, 64, 128), plf, ALU.min)
-        if m < RU - 1:
-            tt(B("sa", x, x + 64), P(3, 64, 128), B("ask"), ALU.min)
+            mm((P(3, 64 * s, 64 * s + 64), M("trif"), flag))
         if s == ST - 1:
+            act(P(3, 0, 192), P(3, 0, 192), AF.Relu)
+            tt(B("sp", 0, 192), P(3, 0, 192), B("da" if q == 0 else "dbb", 1, 384, 2), ALU.min)
+            if m < RU - 1:
+                tt(B("sa", 0, 192), P(3, 0, 192), B("ask", 0, 192), ALU.min)
             for r in range(4):
                 mm((P(3, 128 + r, 320, 4), M("blkf"), B("sp", 0, 192, -r)))
-            if OPT["y"] == "S":
-                act(P(3, 128, 320), P(3, 128, 320), AF.Relu, bias=1.0 - base)
+            act(P(3, 128, 320), P(3, 128, 320), AF.Relu, bias=1.0 - base)
             for k in range(ST):
                 z = (m * ST + k) * 128 + 64 * q
-                if OPT["y"] == "S":
-                    act(A("ypb", z, z + 64), P(3, 256 - 64 * k, 320 - 64 * k), AF.Identity, bias=-1.0)
-                else:
-                    ts(A("ypb", z, z + 64), P(3, 256 - 64 * k, 320 - 64 * k), -float(base), -1.0, ALU.add, ALU.max)
+                act(A("ypb", z, z + 64), P(3, 128 + 64 * k, 192 + 64 * k), AF.Identity, bias=-1.0)
             if m < RU - 1:
                 for r in range(4):
                     mm((P(3, 320 + r, 512, 4), M("sel15"), B("sa", 0, 192, -r)),
-                       *[(P(3, 448 - 64 * k + r, 512 - 64 * k, 4), ID, A("win", f0 - 128 + 64 * k + 16 * r, f0 - 112 + 64 * k + 16 * r)) for k in range(ST)])
+                       *[(P(3, 320 + 64 * k + r, 384 + 64 * k, 4), ID, A("win", f0 - 128 + 64 * k + 16 * r, f0 - 112 + 64 * k + 16 * r)) for k in range(ST)])
                 act(B("rec", 0, 192), P(3, 320, 512), AF.Copy)
 
     def bound(m, q):
@@ -345,16 +354,16 @@ def build():
         B, P = views(q)
         c = 128 * m + 64 * q
         v, e = B("v", 128, 192), A("own", c, c + 64)
-        mm((P(1), ID, v), (P(1), M("nid"), A("nxt", c, c + 64)))
-        mm((P(0), ID, v), (P(0), M("nid"), e))
-        act(B("ab"), P(1), AF.Abs)
-        mm((P(2), M("blk"), B("ab")))
+        tt(B("ab"), v, A("nxt", c, c + 64), ALU.max)
+        mm((P(2), M("nblk"), A("nxt", c, c + 64)), (P(2), M("nblk"), v), (P(2), M("blk2"), B("ab")))
+        mm((P(0), M("nid"), e), (P(0), ID, v))
         tt(B("acc"), P(2), B("bsl"), ALU.is_le)
-        tt(P(0, 64, 128), P(0), B("acc"), ALU.mult)
         if m < RU - 1:
-            tt(A("own", c + 128, c + 192), P(0, 64, 128), e, ALU.add)
-            send("a_p%d%d" % (m + 1, q), "next", A("prv", c + 128, c + 192), A("own", c + 128, c + 192))
+            tt(A("dlt", c + 128, c + 192), P(0), B("acc"), ALU.mult)
+            send("a_p%d%d" % (m + 1, q), "next", A("prv", c + 128, c + 192), A("dlt", c + 128, c + 192))
+            tt(A("own", c + 128, c + 192), A("dlt", c + 128, c + 192), e, ALU.add)
         else:
+            tt(P(0, 64, 128), P(0), B("acc"), ALU.mult)
             for r in range(4):
                 tt(A("yeb", 64 * q + r, 64 * q + 64, 4), P(0, 64 + 16 * r, 80 + 16 * r), A("own", c + 16 * r, c + 16 * r + 16), ALU.add)
         for r in range(4):
@@ -367,9 +376,9 @@ def build():
         if m < RU - 1:
             tt(B("pm", 0, 192), P(1, 0, 192), A("cc", 0, 192), ALU.max)
             scan(B("hold", 0, 192), A("dg0", 0, 192), B("pm", 0, 192), -5.0, ALU.max, ALU.min)
-            tt(B("eq", 0, 192), P(1, 0, 192), B("hold", 0, 192), ALU.is_equal)
-            tt(B("eq", 192, 368), P(1, 16, 192), B("hold", 0, 176), ALU.is_equal)
-            mm((P(0, 0, 192), ID, A("cc", 0, 192)), (P(0, 0, 192), M("blk8"), B("eq", 0, 192)), (P(0, 16, 192), M("blk8"), B("eq", 192, 368)))
+            for k in range(4):
+                tt(B("eq", 192 * k, 192 * k + 192 - 16 * k), P(1, 16 * k, 192), B("hold", 0, 192 - 16 * k), ALU.is_equal)
+            mm((P(0, 0, 192), ID, A("cc", 0, 192)), *[(P(0, 16 * k, 192), M("blk8"), B("eq", 192 * k, 192 * k + 192 - 16 * k)) for k in range(4)])
             scan(B("drop", 0, 192), A("dg0", 0, 192), P(0, 0, 192), -5.0, ALU.max, ALU.min)
             tt(B("offf", 0, 12), B("drop", 15, 192, 16), B("hold", 15, 192, 16), ALU.max)
             ts(B("offs", 0, 12), B("offf", 0, 12), float(DB - PAD), None, ALU.add)
@@ -379,10 +388,9 @@ def build():
         w = A("win", PAD, FB)
         for s in range(ST):
             for q in (1, 0):
-                for b in (5 - 2 * s, 4 - 2 * s):
-                    src, off = A("rec%d" % q, 32 * b, 32 * b + 32), A("offs%d" % q, 2 * b, 2 * b + 2)
-                    add("V", lambda e, T, X, src=src, off=off: e.tensor_copy(res(T, w).indirect(res(T, off)), res(T, src)),
-                        [src, off], [w], ("s", 32))
+                src, off = A("rec%d" % q, 64 * s, 64 * s + 64), A("offs%d" % q, 8 - 4 * s, 12 - 4 * s)
+                add("V", lambda e, T, X, src=src, off=off: e.tensor_copy(res(T, w).indirect(res(T, off)), res(T, src)),
+                    [src, off], [w], ("s", 64))
 
     def places(m):
         store("s_yp%d" % m, lambda T: T.yp[:, 384 * m:384 * m + 384], A("ypb", 384 * m, 384 * m + 384, 1, 0, 128, 16))
@@ -413,15 +421,6 @@ def price(ops, k):
     return cost, late, pred
 
 
-def replay(ops, order, priced):
-    cost, late, pred = priced
-    done, free = {}, {}
-    for i in order:
-        e = ops[i]["eng"]
-        done[i] = free[e] = max([free.get(e, 0.0)] + [done[d] + w for d, w in pred[i]]) + cost[i]
-    return max(done[i] + late[i] for i in order), done
-
-
 def schedule(ops, priced, noise, look):
     cost, late, pred = priced
     n = len(ops)
@@ -442,8 +441,8 @@ def schedule(ops, priced, noise, look):
     while ready:
         first = min(ready, key=lambda i: (max(can[i], free.get(ops[i]["eng"], 0.0)), -level[i]))
         e = ops[first]["eng"]
-        t = max(can[first], free.get(e, 0.0))
-        i = max((j for j in ready if ops[j]["eng"] == e and can[j] <= t + look * cost[first]), key=lambda j: level[j])
+        t = max(can[first], free.get(e, 0.0)) + look * cost[first]
+        i = max((j for j in ready if ops[j]["eng"] == e and can[j] <= t), key=lambda j: level[j])
         free[e] = max(can[i], free.get(e, 0.0)) + cost[i]
         order.append(i)
         ready.remove(i)
@@ -461,21 +460,12 @@ PLAN = {}
 def plan():
     if not PLAN:
         ops = build()
-        n = len(ops)
-        priced = [price(ops, k) for k in PICTURES]
-        rng = np.random.RandomState(OPT["seed"])
-        best, noise = None, np.zeros(n)
-        for t in range(OPT["tries"]):
-            z = noise.copy()
-            if t:
-                a, w = rng.randint(n), (5, 20, 80, 200)[rng.randint(4)]
-                z[a:a + w] += rng.randn() * 600 if rng.rand() < 0.5 else rng.randn(len(z[a:a + w])) * 300
-            order = schedule(ops, priced[0], z.tolist(), 0.3)
-            ends = [replay(ops, order, p)[0] for p in priced]
-            score = ends[0] + ends[1] + 0.8 * ends[2]
-            if best is None or score <= best[0]:
-                best, noise = (score, order, ends), z
-        order = best[1]
+        z = np.zeros(len(ops))
+        for t in MOVES:
+            rng = np.random.RandomState(t)
+            a, w = rng.randint(len(z)), (5, 20, 80, 200)[rng.randint(4)]
+            z[a:a + w] += rng.randn() * 600 if rng.rand() < 0.5 else rng.randn(len(z[a:a + w])) * 300
+        order = schedule(ops, price(ops, PICTURE), z.tolist(), 0.3)
         place = {i: k for k, i in enumerate(order)}
         for o in ops:
             last = {}
@@ -499,7 +489,7 @@ def plan():
             if i in wanted:
                 total[o["eng"]] = total.get(o["eng"], 0) + 1
             o["tick"] = total.get(o["eng"], 0)
-        PLAN.update(ops=ops, order=order, total=total, wanted=wanted, ends=best[2], priced=priced)
+        PLAN.update(ops=ops, order=order, wanted=wanted)
     return PLAN
 
 

@@ -3,118 +3,148 @@ from concourse.mybir import AluOpType as ALU, ActivationFunctionType as AF
 
 F32, BF16, I32, U16 = "float32", "bfloat16", "int32", "uint16"
 RU, ST = 3, 3
-MAGIC = 12582912.0
+M1, M2, M8, M256 = 1.5 * 2 ** 23, 1.5 * 2 ** 24, 1.5 * 2 ** 26, 1.5 * 2 ** 31
 BIG = 8192.0
-FA, PAD, DB, DUM, FB, WEND = 0, 192, 208, 4304, 4496, 4688
+ONE = 73.0
+DB, SP, WEND = 16, 4112, 4496
+GA = 192
+C, B, A, D = 0, 1, 2, 3
+
+PARAMS = dict(
+    streams=[[([(D, 0)], []), ([(D, 1)], []), ([(D, 2)], [])],
+             [([(A, 0)], []), ([(A, 1)], []), ([], [(A, 2)])],
+             [([(C, 1), (B, 0)], [(C, 0)]), ([(C, 2), (B, 2)], [(B, 1)])]],
+    verdicts=[[A], [C, B], [D]],
+    cut1=(16, 8, 24), cut2=(16, 0, 24), scans=(1, 1, 2), vq=("V", "S", "S"), reach=4, parts=((192, 384), (0, 192)), tries=2000,
+)
+PICTURE = dict(c=0.83, p=0.45, hop=220.0, own=160.0, fix=30.0, g=1.5, s=3.8, net=3500.0)
 
 SCRATCH = {
     "win": ("sbuf", [128, WEND], BF16), "endn": ("sbuf", [128, 128], BF16), "wtb": ("sbuf", [128, 16], BF16),
     "salti": ("sbuf", [128, 128], I32), "nzb": ("sbuf", [128, 1152], BF16), "sli": ("sbuf", [128, 384], I32),
-    "slf": ("sbuf", [128, 384], F32), "saltf": ("sbuf", [128, 2, 4, 16], F32), "salt8": ("sbuf", [128, 384], F32),
-    "nzp": ("sbuf", [128, 18, 4, 16], BF16), "own": ("sbuf", [128, 6, 4, 16], BF16),
-    "prv": ("sbuf", [128, 384], BF16), "prp": ("sbuf", [128, 2, 4, 16], BF16), "dlt": ("sbuf", [128, 384], BF16),
-    "nxt": ("sbuf", [128, 384], BF16),
-    "dif": ("sbuf", [128, 144], F32), "gi": ("sbuf", [128, 128], F32), "ai": ("sbuf", [128, 192], F32), "xi": ("sbuf", [128, 192], F32),
-    "pi": ("sbuf", [128, 4], I32), "pc": ("sbuf", [128, 8], F32),
-    "ident": ("sbuf", [128, 128], BF16), "idh": ("sbuf", [128, 128], BF16), "idq": ("sbuf", [128, 128], BF16),
-    "nid": ("sbuf", [128, 128], BF16), "idb": ("sbuf", [128, 128], BF16), "n128": ("sbuf", [128, 128], BF16),
-    "zb": ("sbuf", [128, 144], BF16), "blk": ("sbuf", [128, 128], BF16), "nblk": ("sbuf", [128, 128], BF16), "blk2": ("sbuf", [128, 128], BF16),
-    "blkf": ("sbuf", [128, 128], F32), "blk8": ("sbuf", [128, 128], BF16), "trib": ("sbuf", [128, 128], BF16),
-    "trif": ("sbuf", [128, 128], F32), "ntrif": ("sbuf", [128, 128], F32), "tmp": ("sbuf", [128, 768], F32),
-    "sel15": ("sbuf", [128, 128], BF16), "sel8": ("sbuf", [128, 128], F32), "wbd": ("sbuf", [128, 128], BF16),
-    "cst": ("sbuf", [128, 368], BF16), "keep": ("sbuf", [128, 768], BF16), "rst": ("sbuf", [128, 768], BF16),
-    "dg0": ("sbuf", [128, 192], F32), "cc": ("sbuf", [128, 192], BF16),
+    "slf": ("sbuf", [128, 384], F32), "saltf": ("sbuf", [128, 7, 32], F32), "salt8": ("sbuf", [128, 21, 32], F32),
+    "own": ("sbuf", [128, 1024], BF16), "prv": ("sbuf", [128, 768], BF16), "nxt": ("sbuf", [128, 768], BF16),
+    "dif": ("sbuf", [128, 144], F32), "gi": ("sbuf", [128, 128], F32), "ai": ("sbuf", [128, 384], F32), "xi": ("sbuf", [128, 384], F32),
+    "pi": ("sbuf", [128, 4], I32), "pc": ("sbuf", [128, 16], F32), "w1": ("sbuf", [128, 16], F32), "w2": ("sbuf", [128, 16], F32),
+    "rep": ("sbuf", [128, 8], U16), "zb": ("sbuf", [128, 144], BF16), "tmp": ("sbuf", [128, 768], F32),
+    "cst": ("sbuf", [128, 8, 128], BF16), "fid": ("sbuf", [128, 96], BF16),
+    "keep": ("sbuf", [128, 1536], BF16), "rst": ("sbuf", [128, 1536], BF16),
+    "dg0": ("sbuf", [128, 384], F32), "cc": ("sbuf", [128, 384], BF16),
+    "pl": ("sbuf", [128, 12, 32], I32), "adr": ("sbuf", [128, 128], F32), "hold": ("sbuf", [128, 384], F32), "mf": ("sbuf", [128, 12, 64], BF16), "ask": ("sbuf", [128, 12, 32], BF16),
+    "vin": ("sbuf", [128, 16, 32], BF16), "mx": ("sbuf", [128, 128], BF16), "d0e": ("sbuf", [128, 256], BF16),
+    "ab": ("sbuf", [128, 128], BF16), "bsl": ("sbuf", [128, 128], F32), "sg": ("sbuf", [128, 128], F32),
+    "sp": ("sbuf", [128, 384], F32), "sa": ("sbuf", [128, 384], BF16), "rec": ("sbuf", [128, 384], BF16),
+    "plc": ("sbuf", [128, 384], F32), "pm": ("sbuf", [128, 384], F32), "eq": ("sbuf", [128, 3072], BF16),
+    "drop": ("sbuf", [128, 384], F32), "offf": ("sbuf", [128, 24], F32), "offs": ("sbuf", [128, 24], U16),
     "yeb": ("sbuf", [128, 128], BF16), "yvb": ("sbuf", [128, 384], F32), "ypb": ("sbuf", [128, 1152], F32),
+    "p6": ("psum", [128, 512], F32), "p7": ("psum", [128, 512], F32),
 }
-for _q in range(2):
-    for _n, _w, _d in (("v", 192, BF16), ("um", 64, F32), ("ui", 64, I32), ("ask", 192, I32), ("y", 64, I32),
-                       ("pl", 64, I32), ("o1", 64, U16), ("o2", 64, U16), ("da", 384, F32), ("dbb", 384, F32),
-                       ("so", 128, F32), ("ga", 1024, BF16), ("gb", 1024, BF16), ("hi", 1024, BF16), ("lo", 1024, BF16),
-                       ("ab", 128, BF16), ("bsl", 64, F32),
-                       ("acc", 64, BF16), ("dl", 64, BF16), ("rec", 192, BF16), ("pm", 192, F32), ("hold", 192, F32),
-                       ("eq", 768, BF16), ("drop", 192, F32), ("offf", 12, F32), ("offs", 12, U16)):
+for _n in ("ident", "nid", "nid1", "idh1", "id3", "idq", "idn", "nidn", "blk", "nblkb", "blk2b", "tri", "ntri", "sel15", "wbd", "wneg"):
+    SCRATCH[_n] = ("sbuf", [128, 128], BF16)
+for _n in ("blkf", "nbig", "sel8"):
+    SCRATCH[_n] = ("sbuf", [128, 128], F32)
+for _q in range(3):
+    for _n, _w, _d in (("y", 128, I32), ("o1", 128, U16), ("o2", 128, U16), ("so", 256, F32),
+                       ("ga", 1408, BF16), ("gb", 1024, BF16), ("hi", 1024, BF16), ("lo", 1024, BF16)):
         SCRATCH["%s%d" % (_n, _q)] = ("sbuf", [128, _w], _d)
-    SCRATCH["sp%d" % _q] = ("sbuf", [128, 3, 4, 16], F32)
-    SCRATCH["sa%d" % _q] = ("sbuf", [128, 3, 4, 16], BF16)
-    for _k in range(4):
-        SCRATCH["ps%d%d" % (_q, _k)] = ("psum", [128, 512], F32)
+    for _n in ("pu", "pd"):
+        SCRATCH["%s%d" % (_n, _q)] = ("psum", [128, 512], F32)
 
 LOADS = ["l_end", "l_wt", "l_salt", "l_nz", "l_sl", "l_db0", "l_db1"]
-STORES = ["s_ye", "s_yv", "s_yp0", "s_yp1", "s_yp2"]
-ARRIVALS = ["a_p0"] + ["a_p%d%d" % (m, q) for m in range(1, RU) for q in range(2)] + ["a_n%d" % m for m in range(RU)]
-SEMAPHORES = ["cV", "cS", "cP", "cG", "sent"] + LOADS + STORES + ARRIVALS
-
-PICTURE = dict(c=0.83, p=0.5, hop=220.0, own=160.0, fix=30.0, g=1.5, s=3.8, net=4500.0)
-MOVES = [8, 11, 16, 25, 26, 53, 57, 60, 65, 87, 88, 92, 96, 102, 106, 109, 185, 203, 230, 234, 243, 259, 279, 282, 283, 320,
-         325, 363, 387, 426, 480, 494, 537, 557, 585, 733, 749, 780, 871, 926, 935, 983, 1014, 1018, 1049, 1073, 1074, 1144]
+ARRIVALS = ["a_p0"] + ["a_p%d%d" % (m, k) for m in range(1, RU) for k in range(4)] + ["a_n%d" % m for m in range(RU)]
+SEMAPHORES = ["cV", "cS", "cP", "cG", "sent", "stored"] + LOADS + ARRIVALS
 
 
-def A(name, c0, c1, step=1, p0=0, p1=128, ps=1):
-    return (name, c0, c1, step, p0, p1, ps)
+def R(name, c0, c1, step=1, part=(0, 128, 1)):
+    return (name, tuple(range(c0, c1, step)), part)
 
 
-def cnt(a):
-    return len(range(a[1], a[2], a[3])) if a[3] > 0 else (a[2] - a[1]) // 4
+def U(name, units, c0=0, step=1):
+    w = SCRATCH[name][1][2]
+    return (name, tuple(u * w + c for u in units for c in range(c0, w, step)), (0, 128, 1))
+
+
+def run_of(x):
+    step = x[1] - x[0] if len(x) > 1 else 1
+    return slice(x[0], x[-1] + 1, step) if step > 0 and list(x) == list(range(x[0], x[-1] + 1, step)) else None
+
+
+def index(a):
+    shape, part = SCRATCH[a[0]][1], slice(*a[2])
+    if len(shape) == 2:
+        s = run_of(a[1])
+        return None if s is None else (part, s)
+    units = sorted(set(c // shape[2] for c in a[1]))
+    inner = [c % shape[2] for c in a[1] if c // shape[2] == units[0]]
+    if tuple(u * shape[2] + c for u in units for c in inner) != a[1] or run_of(units) is None or run_of(inner) is None:
+        return None
+    return (part, units[0] if len(units) == 1 else run_of(units), run_of(inner))
+
+
+def join(*rows):
+    out = []
+    for item in zip(*rows):
+        if out:
+            both = [(a[0], a[1] + b[1], a[2]) if a[0] == b[0] else None for a, b in zip(out[-1], item)]
+            if all(x is not None and index(x) is not None for x in both):
+                out[-1] = both
+                continue
+        out.append(list(item))
+    return out
 
 
 def res(T, a):
-    if not isinstance(a, tuple):
-        return a
-    if a[3] <= 0:
-        return T[a[0]][:, a[1] // 64:a[2] // 64, -a[3], :]
-    if len(SCRATCH[a[0]][1]) == 4:
-        if a[1] % 64 == 0 and a[2] % 64 == 0:
-            return T[a[0]][:, a[1] // 64:a[2] // 64]
-        return T[a[0]][:, a[1] // 64, a[1] % 64 // 16]
-    return T[a[0]][a[4]:a[5]:a[6], a[1]:a[2]:a[3]]
+    return T[a[0]][index(a)] if isinstance(a, tuple) else a
 
 
-def two(a):
-    return SCRATCH[a[0]][2] in (BF16, U16)
+def cnt(a):
+    return len(a[1])
+
+
+def two(*aps):
+    return all(SCRATCH[a[0]][2] in (BF16, U16) for a in aps)
 
 
 def psum(a):
     return SCRATCH[a[0]][0] == "psum"
 
 
-def meet(a, b, exact):
-    if exact and a[3] <= 0 and b[3] <= 0 and a[3] != b[3]:
-        return False
-    la, lb = [x[1] + (cnt(x) - 1) * x[3] if x[3] > 0 else x[2] - 1 for x in (a, b)]
-    if la < b[1] or lb < a[1]:
-        return False
-    if exact and a[3] == b[3] and a[3] > 1 and (a[1] - b[1]) % a[3]:
-        return False
-    return True
+def bits(a, exact=True):
+    if exact:
+        return sum(1 << c for c in a[1])
+    return (1 << (max(a[1]) // 8 * 8 + 8)) - (1 << (min(a[1]) // 8 * 8))
 
 
-def build():
-    ops, seen = [], {}
+def build(par):
+    ops, seen, begun = [], {}, []
 
-    def add(eng, fn, reads, writes, cost, sem=None, late=0.0, after=()):
+    def add(eng, fn, reads, writes, cost, sem=None, late=0.0, after=(), loose=None, held=False):
         i = len(ops)
-        deps = {}
-        for d in after:
-            deps[d] = True
-        for acc, wr in [(a, False) for a in reads if isinstance(a, tuple)] + [(a, True) for a in writes]:
-            for j, b, bw in seen.get(acc[0], []):
+        deps, either = {d: True for d in after}, []
+        dma = sem is not None
+        uses = [(a, False, False) for a in reads if isinstance(a, tuple)] + [(a, True, False) for a in writes]
+        if loose:
+            uses.append((loose, False, True))
+        mine = []
+        for a, wr, lo in uses:
+            e, w = bits(a), bits(a, False)
+            for j, be, bw, bwr, blo in seen.get(a[0], []):
                 o = ops[j]
-                same = o["eng"] == eng and o["sem"] is None and sem is None
-                if psum(acc):
-                    if same and not (wr or bw):
-                        continue
-                    need = (not same) or (eng != "P" and meet(acc, b, True))
-                elif (wr or bw) and meet(acc, b, same):
-                    need = True
-                else:
-                    continue
-                deps[j] = deps.get(j, False) or need
-        for a in reads:
-            if isinstance(a, tuple):
-                seen.setdefault(a[0], []).append((i, a, False))
-        for a in writes:
-            seen.setdefault(a[0], []).append((i, a, True))
-        ops.append(dict(eng=eng, fn=fn, deps=deps, cost=cost, sem=sem, late=late))
+                if eng == "P" and o["eng"] == "P" and psum(a):
+                    if held or o["held"] or e & be:
+                        deps.setdefault(j, False)
+                elif (wr or bwr) and ((w & bw) if dma or o["sem"] is not None else (e & be)):
+                    if (lo or blo) and not o["first"]:
+                        either.append(j)
+                        o["either"].append(i)
+                    else:
+                        deps[j] = True
+            mine.append((a[0], (i, e, w, wr, lo)))
+        for n, x in mine:
+            seen.setdefault(n, []).append(x)
+        ops.append(dict(eng=eng, fn=fn, deps=deps, cost=cost, sem=sem, late=late, either=either, first=not begun, held=held, part=len(begun),
+                        tag=(writes or reads)[0][0] + str((writes or reads)[0][1][0]),
+                        banks=sorted(set(a[0] for a, _, _ in uses if psum(a)))))
         return i
 
     def vc(n, rate):
@@ -125,37 +155,41 @@ def build():
             fn = lambda q, T, X: q.tensor_scalar(res(T, o), res(T, a), res(T, s1), None, op0)
         else:
             fn = lambda q, T, X: q.tensor_scalar(res(T, o), res(T, a), res(T, s1), res(T, s2), op0, op1)
-        return add("V", fn, [a, s1, s2], [o], vc(cnt(o), 0.5 if two(o) and two(a) else 1))
+        return add("V", fn, [a, s1, s2], [o], vc(cnt(o), 0.5 if two(o, a) else 1))
 
     def tt(o, a, b, op):
         return add("V", lambda q, T, X: q.tensor_tensor(res(T, o), res(T, a), res(T, b), op), [a, b], [o],
                    vc(cnt(o), 1 if psum(a) or psum(b) else 2))
 
     def cp(o, a):
-        return add("V", lambda q, T, X: q.tensor_copy(res(T, o), res(T, a)), [a], [o], vc(cnt(o), 0.5 if two(o) and two(a) else 1))
+        return add("V", lambda q, T, X: q.tensor_copy(res(T, o), res(T, a)), [a], [o], vc(cnt(o), 0.5 if two(o, a) else 1))
 
     def ms(o, val):
         return add("V", lambda q, T, X: q.memset(res(T, o), val), [], [o], vc(cnt(o), 0.5 if two(o) else 1))
 
     def scan(o, a, b, init, op0, op1):
         return add("V", lambda q, T, X: q.tensor_tensor_scan(res(T, o), res(T, a), res(T, b), init, op0, op1), [a, b], [o],
-                   vc(cnt(o), 0.5 if two(o) and two(a) and two(b) else 1))
+                   vc(cnt(o), 0.5 if two(o, a, b) else 1))
 
     def act(o, a, func, bias=0.0, scale=1.0):
-        return add("S", lambda q, T, X: q.activation(res(T, o), res(T, a), func, bias=bias, scale=scale), [a], [o], vc(cnt(o), 1))
+        return add("S", lambda q, T, X: q.activation(res(T, o), res(T, a), func, bias=res(T, bias), scale=scale), [a, bias], [o], vc(cnt(o), 1))
 
-    def mm(*terms):
-        for k, (o, l, r) in enumerate(terms):
-            wide = 4 if SCRATCH[r[0]][2] == F32 else 1
-            add("P", lambda q, T, X, o=o, l=l, r=r, k=k: q.matmul(res(T, o), res(T, l), res(T, r), k == 0, k == len(terms) - 1),
-                [l, r], [o], ("p", max(64, cnt(r)) * wide))
+    def mm(*parts):
+        for k, terms in enumerate(parts):
+            def fn(q, T, X, terms=terms, k=k):
+                for j, (o, l, r) in enumerate(terms):
+                    ins = q.matmul(res(T, o), res(T, l), res(T, r), k == 0 and j == 0, k == len(parts) - 1 and j == len(terms) - 1)
+                return ins
+            add("P", fn, [a for t in terms for a in t[1:]], [t[0] for t in terms],
+                ("p", sum(10 + max(64, cnt(r)) * (4 if SCRATCH[r[0]][2] == F32 else 1) for _, _, r in terms)), held=len(parts) > 1)
 
-    def gather(eng, o, w, off):
+    def gather(eng, o, w, off, loose=None):
+        whole = w if not loose else R(w[0], min(w[1][0], loose[1][0]), max(w[1][-1], loose[1][-1]) + 1)
         if eng == "V":
-            fn = lambda q, T, X: q.tensor_copy(res(T, o), res(T, w).indirect(res(T, off)))
+            fn = lambda q, T, X: q.tensor_copy(res(T, o), res(T, whole).indirect(res(T, off)))
         else:
-            fn = lambda q, T, X: q.activation(res(T, o), res(T, w).indirect(res(T, off)), AF.Copy)
-        return add(eng, fn, [w, off], [o], ("g", cnt(o)))
+            fn = lambda q, T, X: q.activation(res(T, o), res(T, whole).indirect(res(T, off)), AF.Copy)
+        return add(eng, fn, [w, off], [o], ("g", cnt(o)), loose=loose)
 
     def iota(o, pat, base, mult):
         if SCRATCH[o[0]][2] == I32:
@@ -167,8 +201,8 @@ def build():
     def load(eng, sem, o, src, late):
         return add(eng, lambda q, T, X: q.dma_start(res(T, o), src(T)), [], [o], ("n", 60), sem=(sem, 16), late=late)
 
-    def store(sem, dst, a):
-        return add("Y", lambda q, T, X: q.dma_start(dst(T), res(T, a)), [a], [], ("n", 60), sem=(sem, 16), late=2200.0)
+    def store(dst, a):
+        return add("Y", lambda q, T, X: q.dma_start(dst(T), res(T, a)), [a], [], ("n", 60), sem=("stored", 16), late=2200.0)
 
     def send(sem, to, o, a):
         def fn(q, T, X):
@@ -177,237 +211,286 @@ def build():
         i = add("G", fn, [a], [], ("n", 300), sem=("sent", 0))
         return add("N", None, [], [o], ("n", 0), sem=(sem, -1), late=-1.0, after=[i])
 
-    M = lambda n: A(n, 0, 128)
-    col = lambda k: A("pc", k, k + 1)
-    ID = M("ident")
+    M = lambda n: R(n, 0, 128)
+    col = lambda k: R("pc", k, k + 1)
+    ID, NID, D128 = M("ident"), M("nid"), M("dif")
+    const = lambda k, n: ("cst", tuple(range(128 * k, 128 * k + n)), (0, 128, 1))
+    unit = lambda k, s: 4 * (2 - s) + k
+    fresh = {it: ("ga%d" % q, 64 * j + 32 * i) for q, st in enumerate(par["streams"]) for j, jb in enumerate(st) for i, it in enumerate(jb[0])}
+    fresh.update({(k, k): ("fid", 32 * k) for k in (C, B, A)})
+    F = lambda k, s: R(fresh[k, s][0], fresh[k, s][1], fresh[k, s][1] + 32)
+    after = lambda k, s: U("vin", [unit(k, s + 1) if s < ST - 1 else 12 + k])
 
     load("Y", "l_end", M("endn"), lambda T: T.ends[:], 2200.0)
-    load("S", "l_db0", A("win", DB, DB + 2048), lambda T: T.db[:, 0:2048], 6000.0)
-    load("Y", "l_wt", A("wtb", 0, 16), lambda T: T.wt[:], 3000.0)
+    load("S", "l_db0", R("win", DB, DB + 2048), lambda T: T.db[:, 0:2048], 6000.0)
+    load("Y", "l_wt", R("wtb", 0, 16), lambda T: T.wt[:], 3000.0)
     load("Y", "l_salt", M("salti"), lambda T: T.salt[:], 3000.0)
-    load("Y", "l_db1", A("win", DB + 2048, DUM), lambda T: T.db[:, 2048:4096], 6000.0)
-    load("S", "l_nz", A("nzb", 0, 1152), lambda T: T.nz[:], 6500.0)
-    load("Y", "l_sl", A("sli", 0, 384, 1, 0, 8), lambda T: T.sl[:], 6500.0)
-    send("a_p0", "next", A("prv", 0, 128), A("endn", 0, 128))
-    for r in range(4):
-        cp(A("own", 0, 128, -r), A("endn", r, 128, 4))
-    for r in range(4):
-        cp(A("prp", 0, 128, -r), A("prv", r, 128, 4))
-    send("a_n0", "prev", A("nxt", 0, 128), A("own", 0, 128))
+    load("Y", "l_db1", R("win", DB + 2048, SP), lambda T: T.db[:, 2048:4096], 6000.0)
+    load("S", "l_nz", R("nzb", 0, 1152), lambda T: T.nz[:], 6500.0)
+    load("Y", "l_sl", R("sli", 0, 384, 1, (0, 8, 1)), lambda T: T.sl[:], 6500.0)
+    send("a_p0", "next", R("prv", 0, 128), M("endn"))
 
-    iota(A("pi", 0, 1), [[0, 1]], 0, 1)
-    iota(A("dif", 0, 144), [[1, 144]], 0, -1)
+    iota(R("pi", 0, 1), [[0, 1]], 0, 1)
+    iota(R("dif", 0, 144), [[1, 144]], 0, -1)
     iota(M("gi"), [[1, 8], [0, 16]], 0, 0)
-    ts(A("pi", 1, 2), A("pi", 0, 1), 4, None, ALU.arith_shift_right)
-    ts(A("pi", 2, 3), A("pi", 0, 1), 15, None, ALU.bitwise_and)
-    cp(A("pc", 0, 3), A("pi", 0, 3))
-    ts(col(3), col(2), 15.0, 0.5, ALU.not_equal, ALU.mult)
-    ts(col(4), col(2), 15.0, 0.25, ALU.not_equal, ALU.mult)
-    ts(col(5), col(2), 15.0, None, ALU.is_equal)
-    D128 = M("dif")
+    iota(R("xi", 0, 384), [[1, 384]], 0, 0)
+    iota(R("ai", 0, 384), [[0, 24], [1, 16]], 0, 0)
+    ts(R("pi", 1, 2), R("pi", 0, 1), 4, None, ALU.arith_shift_right)
+    ts(R("pi", 2, 3), R("pi", 0, 1), 15, None, ALU.bitwise_and)
+    cp(R("pc", 0, 3), R("pi", 0, 3))
+    for k, val in ((3, 1.0), (4, ONE), (5, -55.0 / 8192), (6, 7.0 / 128), (7, 1.75), (8, -1.0 / 256), (9, -121.0)):
+        ts(col(k), col(2), 15.0, val, ALU.is_equal, ALU.mult)
+    ts(col(10), col(2), 15.0, None, ALU.not_equal)
+    ts(col(11), col(3), 0.5 + 1.0 / 256, 0.5, ALU.mult, ALU.add)
+    ms(R("own", 0, 256, 2), 0.0)
+    for k in range(4):
+        ts(R("own", 64 * k + 1, 64 * k + 64, 2), R("endn", k, 128, 4), col(4), None, ALU.add)
+    send("a_n0", "prev", R("nxt", 0, 256), R("own", 0, 256))
     ts(ID, D128, 0.0, None, ALU.is_equal)
     ts(M("blkf"), M("gi"), col(1), None, ALU.is_equal)
-    for k in range(8):
-        ts(A("wbd", 16 * k, 16 * k + 16), A("wtb", 0, 16), A("blkf", 16 * k, 16 * k + 1), 1.0 / 64, ALU.mult, ALU.mult)
-    ms(A("cst", 0, 64), -63.0 / 128)
-    ms(A("cst", 64, 128), -0.375)
-    ms(A("cst", 128, 192), 1.0)
-    ms(A("cst", 192, 256), -1.0)
-    ms(A("cst", 256, 304), 0.0)
-    ms(A("cst", 304, 320), 64.0)
-    ms(A("cst", 320, 368), 0.0)
-    for r in range(4):
-        cp(A("saltf", 0, 128, -r), A("salti", r, 128, 4))
-        cp(A("nzp", 0, 1152, -r), A("nzb", r, 1152, 4))
+    ts(R("rep", 0, 8), R("gi", 0, 8), col(2), None, ALU.add)
+    for w, to, sign, k in (("w1", "wbd", 1.0, 5), ("w2", "wneg", -1.0, 6)):
+        ts(R(w, 0, 16), R("wtb", 0, 16), sign / 64, col(k), ALU.mult, ALU.add)
+        add("V", lambda q, T, X, w=w, to=to: q.tensor_tensor(T[to][:], T[w][:].indirect(T["rep"][:]), T["blkf"][:], ALU.mult),
+            [R(w, 0, 16), R("rep", 0, 8), M("blkf")], [M(to)], ("g", 128))
+    for k, val in ((0, M1), (1, M8), (2, -M8), (3, M256), (4, -M256), (5, 15.0), (7, M2)):
+        ms(const(k, 128), val)
+    ts(const(6, 128), M("gi"), 0.0, col(4), ALU.mult, ALU.add)
+    for r in range(7):
+        cp(U("saltf", [r]), R("salti", r % 4, 128, 4))
     for s in range(ST):
-        act(A("salt8", 128 * s, 128 * s + 128), M("saltf"), AF.Identity, bias=8.0 * 211 * s - 148.0 ** 2, scale=8.0)
-    ts(A("zb", 0, 144), A("dif", 0, 144), 0.0, col(5), ALU.is_equal, ALU.mult)
-    ts(M("idh"), D128, 0.0, col(3), ALU.is_equal, ALU.mult)
-    ts(M("idq"), D128, 0.0, col(4), ALU.is_equal, ALU.mult)
-    act(M("nid"), ID, AF.Copy, scale=-1.0)
-    act(M("idb"), ID, AF.Copy, scale=BIG)
-    act(M("n128"), ID, AF.Copy, scale=-128.0)
-    ms(A("win", FA, DB), 0.0)
-    ms(A("win", DUM, WEND), 0.0)
-    ms(A("keep", 0, 768), 1.0)
-    ms(A("keep", 0, 768, 16), 0.0)
-    ms(A("rst", 0, 768), 0.0)
-    ms(A("rst", 0, 768, 16), 255.0)
-    ms(A("da0", 0, 384, 2), 0.0)
-    ms(A("da1", 0, 384, 2), 0.0)
-    iota(A("xi", 0, 192), [[1, 192]], 0, 0)
-    act(A("dbb0", 1, 384, 2), A("xi", 0, 192), AF.Identity, bias=float(FA))
-    act(A("da1", 1, 384, 2), A("xi", 0, 192), AF.Identity, bias=float(FB - PAD))
+        act(U("salt8", range(14 - 7 * s, 21 - 7 * s)), U("saltf", range(7)), AF.Identity, bias=8.0 * 211 * s - 148.0 ** 2, scale=8.0)
+    act(NID, ID, AF.Copy, scale=-1.0)
+    ts(R("tmp", 0, 128), M("blkf"), col(7), None, ALU.mult)
+    tt(M("nid1"), R("tmp", 0, 128), ID, ALU.subtract)
+    ts(R("zb", 0, 144), R("dif", 0, 144), 0.0, col(3), ALU.is_equal, ALU.mult)
+    ts(M("idn"), D128, 0.0, col(10), ALU.is_equal, ALU.mult)
+    act(M("idq"), M("idn"), AF.Copy, scale=0.25)
+    act(M("nidn"), M("idn"), AF.Copy, scale=-1.0)
+    ts(R("tmp", 128, 256), M("blkf"), col(8), None, ALU.mult)
+    ts(R("tmp", 256, 384), D128, 0.0, col(11), ALU.is_equal, ALU.mult)
+    tt(M("idh1"), R("tmp", 128, 256), R("tmp", 256, 384), ALU.add)
+    act(R("tmp", 640, 768), M("idh1"), AF.Copy, scale=2.0)
+    tt(M("id3"), R("tmp", 640, 768), M("idn"), ALU.add)
+    ms(R("win", 0, DB), 0.0)
+    ms(R("win", SP, WEND), 0.0)
+    for q in range(3):
+        ms(R("ga%d" % q, 0, GA), 0.0)
+    wide = 512 * max(len(j[0]) for st in par["streams"] for j in st)
+    ms(R("keep", 0, wide), 1.0)
+    ms(R("keep", 0, wide, 16), 0.0)
+    act(R("rst", 0, wide), R("keep", 0, wide), AF.Identity, bias=255.0, scale=-255.0)
+    ms(U("mf", range(12)), -BIG)
+    ts(col(12), col(2), float(GA), None, ALU.add)
+    act(R("adr", 0, 128, 2), R("xi", 0, 64), AF.Identity, bias=col(12), scale=16.0)
+    act(R("adr", 1, 128, 2), R("xi", 0, 64), AF.Copy)
+    ms(R("d0e", 0, 256, 2), 0.0)
     act(M("blk"), M("blkf"), AF.Copy)
-    act(M("nblk"), M("blkf"), AF.Copy, scale=-1.0)
-    act(M("blk2"), M("blkf"), AF.Copy, scale=2.0)
-    act(M("blk8"), M("blkf"), AF.Copy, scale=2 * BIG)
-    ts(A("tmp", 0, 128), D128, 0.0, -BIG, ALU.is_gt, ALU.mult)
-    tt(A("tmp", 128, 256), A("tmp", 0, 128), M("idb"), ALU.add)
-    tt(M("trif"), A("tmp", 128, 256), M("blkf"), ALU.mult)
-    act(M("trib"), M("trif"), AF.Copy)
-    act(M("ntrif"), M("trif"), AF.Copy, scale=-1.0)
+    act(M("nblkb"), M("blkf"), AF.Copy, scale=-BIG)
+    act(M("blk2b"), M("blkf"), AF.Copy, scale=2 * BIG)
+    act(M("nbig"), ID, AF.Copy, scale=-BIG)
+    ts(R("tmp", 384, 512), D128, 0.0, None, ALU.is_gt)
+    tt(R("tmp", 512, 640), R("tmp", 384, 512), ID, ALU.subtract)
+    tt(M("ntri"), R("tmp", 512, 640), M("blkf"), ALU.mult)
     ms(M("sel15"), 0.0)
-    cp(A("sel15", 15, 128, 16), A("blkf", 15, 128, 16))
-    ts(A("sel8", 0, 128, 1, 0, 8), A("gi", 0, 128, 1, 0, 8), A("pc", 0, 1, 1, 0, 8), None, ALU.is_equal)
-    cp(A("slf", 0, 384, 1, 0, 8), A("sli", 0, 384, 1, 0, 8))
-    iota(A("ai", 0, 192), [[0, 12], [1, 16]], 0, 0)
-    ts(A("tmp", 256, 448), A("ai", 0, 192), col(2), 4 * BIG, ALU.not_equal, ALU.mult)
-    act(A("tmp", 448, 640), A("xi", 0, 192), AF.Identity, bias=4096.0)
-    tt(A("dg0", 0, 192), A("tmp", 448, 640), A("tmp", 256, 448), ALU.subtract)
-    act(A("cc", 0, 192), A("tmp", 256, 448), AF.Identity, bias=-3 * BIG, scale=2.0)
+    cp(R("sel15", 15, 128, 16), R("blkf", 15, 128, 16))
+    eight = (0, 8, 1)
+    ts(R("sel8", 0, 128, 1, eight), R("gi", 0, 128, 1, eight), R("pc", 0, 1, 1, eight), None, ALU.is_equal)
+    cp(R("slf", 0, 384, 1, eight), R("sli", 0, 384, 1, eight))
+    ts(R("pm", 0, 384), R("ai", 0, 384), col(2), 4 * BIG, ALU.not_equal, ALU.mult)
+    act(R("drop", 0, 384), R("xi", 0, 384), AF.Identity, bias=4096.0)
+    tt(R("dg0", 0, 384), R("drop", 0, 384), R("pm", 0, 384), ALU.subtract)
+    act(R("cc", 0, 384), R("pm", 0, 384), AF.Identity, bias=-3 * BIG, scale=2.0)
+    begun.append(1)
 
-    def views(q):
-        return (lambda n, c0=0, c1=64, st=1: A("%s%d" % (n, q), c0, c1, st)), (lambda k, c0=0, c1=64, st=1: A("ps%d%d" % (q, k), c0, c1, st))
+    def of_v(m, items, P, c0, l):
+        src = [U("vin", [unit(k, s)]) if s else R("prv", 256 * m + 64 * k + 1, 256 * m + 64 * k + 64, 2) if m else R("prv", k, 128, 4) for k, s in items]
+        out = [R(P, c0 + 32 * j, c0 + 32 * j + 32) for j in range(len(items))]
+        terms = [(o, l, v) for o, v in join(out, src)]
+        if l is not ID:
+            terms += [(o[0], l, const(6, cnt(o[0]))) for o in join([o for o, (k, s) in zip(out, items) if m == 0 and s == 0])]
+        return terms
 
-    def step(m, s, q):
-        B, P = views(q)
+    def fresh_terms(m, items, P, c0, l):
+        n = 32 * len(items)
+        out = [R(P, c0 + 32 * j, c0 + 32 * j + 32) for j in range(len(items))]
+        nz = [R("nzb", 128 * (m * ST + s) + (k - m) % 4, 128 * (m * ST + s) + 128, 4) for k, s in items]
+        return ([(o, NID, z) for o, z in zip(out, nz)] + of_v(m, items, P, c0, M("nid1"))
+                + [(R(P, c0, c0 + n), ID, const(3, n)), (R(P, c0, c0 + n), ID, const(4, n))]
+                + [(o, ID, z) for o, z in zip(out, nz)] + of_v(m, items, P, c0, l))
 
-        def of_v(k, l):
-            if s:
-                return [(P(k), l, B("v", 64 * (s - 1), 64 * s))]
-            if m == 0:
-                return [(P(k, 16 * r, 16 * r + 16), l, A("prv", 64 * q + r, 64 * q + 64, 4)) for r in range(4)]
-            return [(P(k), l, A("prp", 64 * q, 64 * q + 64))] + [(P(k), l, A("prv", 128 * j + 64 * q, 128 * j + 64 * q + 64)) for j in range(1, m + 1)]
-        t0 = 16 * ((s - m) % 4)
-        one, pair = {0: ((16, 32), (32, 64)), 16: ((0, 16), (32, 64)), 32: ((48, 64), (0, 32)), 48: ((32, 48), (0, 32))}[t0]
+    def fresh_of(m, items, P, c0):
+        mm(fresh_terms(m, items, P, c0, ID))
+        for o, a in join([F(k, s) for k, s in items], [R(P, c0 + 32 * j, c0 + 32 * j + 32) for j in range(len(items))]):
+            act(o, a, AF.Copy)
 
-        def cut(e):
-            if not e:
-                return [("V", one), ("S", pair)]
-            if one[1] == pair[0]:
-                return [("V", (one[0], one[1] + e)), ("S", (pair[0] + e, pair[1]))]
-            if one[0] == pair[1]:
-                return [("V", (one[0] - e, one[1])), ("S", (pair[0], pair[1] - e))]
-            return [("V", one), ("V", (pair[0], pair[0] + e)), ("S", (pair[0] + e, pair[1]))]
-        spans = [(a, b) for a, b in ((0, t0), (t0 + 16, 64)) if b > a]
-        n0, n1 = spans[0][0], spans[-1][1]
-        f0 = (FA if q == 0 else FB) + 64 * s
-        base = DB - FA if q == 0 else DB - PAD
-        wide = A("win", FA, DUM) if q == 0 else A("win", PAD, WEND)
-        d0 = 128 * s
-        plf = B("da" if q == 0 else "dbb", d0 + 1, d0 + 128, 2)
-        flag = B("dbb", d0, d0 + 128, 2)
-        ask = B("ask", 64 * s, 64 * s + 64)
-        mm((P(0), ID, A("cst", 0, 64)), *of_v(0, M("wbd")))
-        act(B("um"), P(0), AF.Identity, bias=MAGIC)
-        act(P(0, 64, 128), B("um"), AF.Square, bias=148.0 - MAGIC)
-        tt(B("y"), P(0, 64, 128), A("salt8", 128 * s + 64 * q, 128 * s + 64 * q + 64), ALU.add)
-        ts(B("pl"), B("y"), 3, 4095, ALU.arith_shift_right, ALU.bitwise_and)
-        cp(B("o1"), B("pl"))
-        for e, (a, b) in cut(8):
-            gather(e, B("ga", 16 * a, 16 * b), A("win", DB, DUM), B("o1", a, b))
-        ts(B("ui"), B("um"), MAGIC, None, ALU.subtract)
-        ts(ask, B("ui"), 7, None, ALU.bitwise_and)
-        ts(plf, B("pl"), float(base), None, ALU.add)
-        z = (m * ST + s) * 128 + 64 * q
-        mm((P(2), ID, A("nzp", z, z + 64)), *of_v(2, ID))
-        act(B("dl"), P(2), AF.Sign, bias=-255.5)
-        mm((P(2), ID, A("nzp", z, z + 64)), *of_v(2, ID), (P(2), M("n128"), B("dl")))
-        act(A("win", f0, f0 + 64), P(2), AF.Identity, bias=-128.0)
-        mm((P(0), ID, A("cst", 304 - t0, 368 - t0)),
-           *[(P(0, n0, n1), A("zb", 15 - p, 143 - p), B("ga", 16 * n0 + p, 16 * n1, 16)) for p in range(16)])
-        tt(flag, P(0), ask, ALU.is_equal if q == 0 else ALU.not_equal)
-        scan(B("so", 2 * n0, 2 * n1), B("da", d0 + 2 * n0, d0 + 2 * n1), B("dbb", d0 + 2 * n0, d0 + 2 * n1), 0.0, ALU.mult, ALU.max)
-        cp(B("o2", n0, n1), B("so", 2 * n0 + 1, 2 * n1, 2))
-        for e, (a, b) in cut(0)[::-1]:
-            gather(e, B("gb", 16 * a, 16 * b), wide, B("o2", a, b))
-        for a, b in spans:
-            scan(B("hi", 16 * a, 16 * b), A("keep", 0, 16 * (b - a)), B("gb", 16 * a, 16 * b), 0.0, ALU.mult, ALU.max)
-            scan(B("lo", 16 * a, 16 * b), A("rst", 0, 16 * (b - a)), B("gb", 16 * a, 16 * b), 0.0, ALU.max, ALU.min)
-        terms = [(P(1), ID, A("cst", 64, 128)), *of_v(1, M("idh")), (P(1, t0, t0 + 16), M("idh"), A("win", f0 + t0, f0 + t0 + 16))]
-        for a, b in spans:
-            terms += [(P(1, a, b), M("idq"), B(n, 16 * a + 15, 16 * b, 16)) for n in ("hi", "lo")]
-        mm(*terms)
-        ts(B("v", 64 * s, 64 * s + 64), P(1), MAGIC, MAGIC, ALU.add, ALU.subtract)
-        if q == 0:
-            mm((P(3, 64 * s, 64 * s + 64), M("trib"), A("cst", 128, 192)), (P(3, 64 * s, 64 * s + 64), M("ntrif"), flag))
-        else:
-            mm((P(3, 64 * s, 64 * s + 64), M("trif"), flag))
-        if s == ST - 1:
-            act(P(3, 0, 192), P(3, 0, 192), AF.Relu)
-            tt(B("sp", 0, 192), P(3, 0, 192), B("da" if q == 0 else "dbb", 1, 384, 2), ALU.min)
-            if m < RU - 1:
-                tt(B("sa", 0, 192), P(3, 0, 192), B("ask", 0, 192), ALU.min)
-            for r in range(4):
-                mm((P(3, 128 + r, 320, 4), M("blkf"), B("sp", 0, 192, -r)))
-            act(P(3, 128, 320), P(3, 128, 320), AF.Relu, bias=1.0 - base)
-            for k in range(ST):
-                z = (m * ST + k) * 128 + 64 * q
-                act(A("ypb", z, z + 64), P(3, 128 + 64 * k, 192 + 64 * k), AF.Identity, bias=-1.0)
-            if m < RU - 1:
-                for r in range(4):
-                    mm((P(3, 320 + r, 512, 4), M("sel15"), B("sa", 0, 192, -r)),
-                       *[(P(3, 320 + 64 * k + r, 384 + 64 * k, 4), ID, A("win", f0 - 128 + 64 * k + 16 * r, f0 - 112 + 64 * k + 16 * r)) for k in range(ST)])
-                act(B("rec", 0, 192), P(3, 320, 512), AF.Copy)
+    def state(m, q, items, P, c0, terms):
+        n = 32 * len(items)
+        on_s = par["vq"][q] == "S"
+        mm(of_v(m, items, P, c0, M("idh1")) + terms + ([(R(P, c0, c0 + n), ID, const(0, n))] if on_s else []))
+        for o, a in join([after(k, s) for k, s in items], [R(P, c0 + 32 * j, c0 + 32 * j + 32) for j in range(len(items))]):
+            if on_s:
+                act(o, a, AF.Identity, bias=-M1)
+            else:
+                ts(o, a, M1, M1, ALU.add, ALU.subtract)
 
-    def bound(m, q):
-        B, P = views(q)
-        c = 128 * m + 64 * q
-        mm((P(2, 64, 128), ID, A("own", c, c + 64)), (P(2, 64, 128), M("nid"), A("nxt", c, c + 64)))
-        act(B("ab", 64, 128), P(2, 64, 128), AF.Abs)
-        mm((P(2, 128, 192), M("blk"), B("ab", 64, 128)),
-           *[(P(2, 128 + 16 * r, 144 + 16 * r), A("sel8", 0, 128, 1, 0, 8), A("slf", c + r, c + 64, 4, 0, 8)) for r in range(4)])
-        act(B("bsl"), P(2, 128, 192), AF.Copy)
-
-    def verdict(m, q):
-        B, P = views(q)
-        c = 128 * m + 64 * q
-        v, e = B("v", 128, 192), A("own", c, c + 64)
-        tt(B("ab"), v, A("nxt", c, c + 64), ALU.max)
-        mm((P(2), M("nblk"), A("nxt", c, c + 64)), (P(2), M("nblk"), v), (P(2), M("blk2"), B("ab")))
-        mm((P(0), M("nid"), e), (P(0), ID, v))
-        tt(B("acc"), P(2), B("bsl"), ALU.is_le)
+    def idle(m, q, k):
+        P = "pu%d" % q
+        mm(fresh_terms(m, [(k, k)], P, 416, M("id3")) + [(R(P, 416, 448), ID, const(7, 32))])
+        act(after(k, k), R(P, 416, 448), AF.Identity, bias=-M2 / 2, scale=0.5)
         if m < RU - 1:
-            tt(A("dlt", c + 128, c + 192), P(0), B("acc"), ALU.mult)
-            send("a_p%d%d" % (m + 1, q), "next", A("prv", c + 128, c + 192), A("dlt", c + 128, c + 192))
-            tt(A("own", c + 128, c + 192), A("dlt", c + 128, c + 192), e, ALU.add)
-        else:
-            tt(P(0, 64, 128), P(0), B("acc"), ALU.mult)
-            for r in range(4):
-                tt(A("yeb", 64 * q + r, 64 * q + 64, 4), P(0, 64 + 16 * r, 80 + 16 * r), A("own", c + 16 * r, c + 16 * r + 16), ALU.add)
-        for r in range(4):
-            mm((P(2, 192 + r, 256, 4), ID, A("cst", 192, 208)), (P(2, 192 + r, 256, 4), M("idb"), B("acc", 16 * r, 16 * r + 16)))
-        if m < RU - 1:
-            for s in range(ST):
-                z = (m * ST + s) * 128 + 64 * q
-                tt(P(1, 64 * (2 - s), 64 * (3 - s)), P(2, 192, 256), A("ypb", z, z + 64), ALU.min)
-        act(A("yvb", c, c + 64), P(2, 192, 256), AF.Identity, bias=1.0 / BIG, scale=1.0 / BIG)
-        if m < RU - 1:
-            tt(B("pm", 0, 192), P(1, 0, 192), A("cc", 0, 192), ALU.max)
-            scan(B("hold", 0, 192), A("dg0", 0, 192), B("pm", 0, 192), -5.0, ALU.max, ALU.min)
-            for k in range(4):
-                tt(B("eq", 192 * k, 192 * k + 192 - 16 * k), P(1, 16 * k, 192), B("hold", 0, 192 - 16 * k), ALU.is_equal)
-            mm((P(0, 0, 192), ID, A("cc", 0, 192)), *[(P(0, 16 * k, 192), M("blk8"), B("eq", 192 * k, 192 * k + 192 - 16 * k)) for k in range(4)])
-            scan(B("drop", 0, 192), A("dg0", 0, 192), P(0, 0, 192), -5.0, ALU.max, ALU.min)
-            tt(B("offf", 0, 12), B("drop", 15, 192, 16), B("hold", 15, 192, 16), ALU.max)
-            ts(B("offs", 0, 12), B("offf", 0, 12), float(DB - PAD), None, ALU.add)
+            fresh_of(m, [(k, k)], P, 384)
 
-    def commit(m):
-        send("a_n%d" % (m + 1), "prev", A("nxt", 128 * m + 128, 128 * m + 256), A("own", 128 * m + 128, 128 * m + 256))
-        w = A("win", PAD, FB)
-        for s in range(ST):
-            for q in (1, 0):
-                src, off = A("rec%d" % q, 64 * s, 64 * s + 64), A("offs%d" % q, 8 - 4 * s, 12 - 4 * s)
-                add("V", lambda e, T, X, src=src, off=off: e.tensor_copy(res(T, w).indirect(res(T, off)), res(T, src)),
-                    [src, off], [w], ("s", 64))
+    def job(m, q, real, riders):
+        items = real + riders
+        n, na = 32 * len(items), 32 * len(real)
+        PU, PD = "pu%d" % q, "pd%d" % q
+        b = lambda name, c0, c1, step=1: R("%s%d" % (name, q), c0, c1, step)
+        each = lambda name, its, w=32, c0=0, step=1: [R(name, w * j + c0, w * j + w, step) for j in range(len(its))]
+        mm(of_v(m, items, PU, 0, M("wbd")) + [(R(PU, 0, n), ID, const(0, n))])
+        act(R(PU, 0, n), R(PU, 0, n), AF.Square, bias=148.0 - M1)
+        for o, x, z in join(each("y%d" % q, items), each(PU, items), [U("salt8", [14 - 7 * s + (-m) % 4 + k]) for k, s in items]):
+            tt(o, x, z, ALU.add)
+        for o, x in join([U("pl", [unit(k, s)]) for k, s in items], each("y%d" % q, items)):
+            ts(o, x, 3, 4095, ALU.arith_shift_right, ALU.bitwise_and)
+        if real:
+            w0 = fresh[real[0]][1]
+            for o, x in join(each("o1%d" % q, real), [U("pl", [unit(k, s)]) for k, s in real]):
+                cp(o, x)
+            e = par["cut1"][q]
+            for eng, a0, a1 in (("S", e, na), ("V", 0, e)):
+                if a1 > a0:
+                    gather(eng, b("ga", w0 + GA + 16 * a0, w0 + GA + 16 * a1), R("win", DB, SP), b("o1", a0, a1))
+        its = items if m < RU - 1 else real
+        if its:
+            w = 32 * len(its)
+            mm(of_v(m, its, PD, 128, M("wneg")) + [(R(PD, 128, 128 + w), ID, const(1, w)), (R(PD, 128, 128 + w), ID, const(2, w))]
+               + of_v(m, its, PD, 128, M("wbd")))
+            for o, x in join([U("ask", [unit(k, s)]) for k, s in its], [R(PD, 128 + 32 * j, 160 + 32 * j) for j in range(len(its))]):
+                act(o, x, AF.Identity, bias=136.0)
+        if not real:
+            return
+        fresh_of(m, real, PU, 128)
+        mm([(o, NID, x) for o, x in join(each(PD, real), [U("ask", [unit(k, s)]) for k, s in real])]
+           + [(R(PD, 0, na), R("zb", 15 - p, 143 - p), b("ga", w0 + GA + p, w0 + GA + 16 * na, 16)) for p in range(16)])
+        for o, x in join([U("mf", [unit(k, s)], 1, 2) for k, s in real], each(PD, real)):
+            ts(o, x, -136.0, -BIG, ALU.not_equal, ALU.mult)
+        for j, (k, s) in enumerate(real):
+            scan(b("so", 64 * j, 64 * j + 64), U("mf", [unit(k, s)]), R("adr", 64 * j, 64 * j + 64), 0.0, ALU.add, ALU.max)
+        cp(b("o2", 0, na), b("so", 1, 2 * na, 2))
+        e = par["cut2"][q]
+        for eng, a0, a1 in (("S", e, na), ("V", 0, e)):
+            if a1 > a0:
+                gather(eng, b("gb", 16 * a0, 16 * a1), b("ga", w0, w0 + GA + 16 * na), b("o2", a0, a1))
+        for a0, a1 in ((0, e), (e, na)) if par["scans"][q] == 2 and 0 < e < na else ((0, na),):
+            scan(b("hi", 16 * a0, 16 * a1), R("keep", 0, 16 * (a1 - a0)), b("gb", 16 * a0, 16 * a1), 0.0, ALU.mult, ALU.max)
+            scan(b("lo", 16 * a0, 16 * a1), R("rst", 0, 16 * (a1 - a0)), b("gb", 16 * a0, 16 * a1), 0.0, ALU.max, ALU.min)
+        state(m, q, real, PU, 256, [(R(PU, 256, 256 + na), M("idq"), b(x, 15, 16 * na, 16)) for x in ("hi", "lo")])
+
+    def listed(m, k, what, j=None):
+        P, c = dict(place=("p6", 0), rec=("p7", 0), z=("p6", 384))[what]
+        r = (k - m) % 4
+        return R(P, c + r, c + 384, 4) if j is None else R(P, c + 128 * j + r, c + 128 * (j + 1), 4)
+
+    def shadow(m, q, k):
+        r, units = (k - m) % 4, (k, k + 4, k + 8)
+        P, sp, sa = R("pd%d" % q, 256, 352), R("sp", 96 * k, 96 * k + 96), R("sa", 96 * k, 96 * k + 96)
+        mm([(P, M("ntri"), U("mf", units, 1, 2))])
+        ts(P, P, -1.0, -1.0, ALU.add, ALU.max)
+        tt(sp, P, U("pl", units), ALU.min)
+        if m < RU - 1:
+            tt(sa, P, U("ask", units), ALU.min)
+        mm([(listed(m, k, "place"), ID, const(5, 96)), (listed(m, k, "place"), M("blkf"), sp)])
+        act(R("ypb", 384 * m + r, 384 * m + 384, 4), listed(m, k, "place"), AF.Copy)
+        if m < RU - 1:
+            mm([(listed(m, k, "rec", j), M("idn"), F(k, 2 - j)) for j in range(ST)] + [(listed(m, k, "rec"), M("sel15"), sa)])
 
     def places(m):
-        store("s_yp%d" % m, lambda T: T.yp[:, 384 * m:384 * m + 384], A("ypb", 384 * m, 384 * m + 384, 1, 0, 128, 16))
-
-    for m in range(RU):
         for s in range(ST):
-            for q in (1, 0):
-                step(m, s, q)
-                if s == 1:
-                    bound(m, q)
-        for q in (1, 0):
-            verdict(m, q)
-        if m < RU - 1:
-            commit(m)
+            z, c = 128 * (m * ST + s), 384 * m + 128 * (2 - s)
+            store(lambda T, z=z: T.yp[:, z:z + 128], R("ypb", c, c + 128, 1, (0, 128, 16)))
+
+    def bound(m):
+        c = 256 * m
+        P = R("p7", 384, 512)
+        mm([(P, ID, R("own", c + 1, c + 256, 2)), (P, NID, R("nxt", c + 1, c + 256, 2))])
+        act(M("ab"), P, AF.Abs)
+        mm([(P, R("sel8", 0, 128, 1, eight), R("slf", 128 * m, 128 * m + 128, 1, eight))]
+           + [(R("p7", 384 + (k - m) % 4, 512, 4), M("blk"), x) for k in range(4)
+              for x in (R("ab", 32 * k, 32 * k + 32), R("nxt", c + 64 * k + 1, c + 64 * k + 64, 2))])
+        act(M("bsl"), P, AF.Identity, bias=0.25)
+
+    def verdict(m, q, roles):
+        k0, n, P = roles[0], 32 * len(roles), "pu%d" % q
+        c, to = 256 * m + 64 * k0, 256 * (m + 1) + 64 * ((k0 + 1) % 4)
+        v, e, last = U("vin", [12 + k for k in roles]), R("own", c + 1, c + 2 * n, 2), m == RU - 1
+        tt(R("mx", 32 * k0, 32 * k0 + n), v, R("nxt", c + 1, c + 2 * n, 2), ALU.max)
+        mm([(R(P, 1, 2 * n, 2), M("idn") if last else ID, e)])
+        mm([(R(P, 0, 2 * n, 2), M("nidn") if last else NID, e), (R(P, 0, 2 * n, 2), M("idn") if last else ID, v)])
+        for k in roles:
+            r = (k - m) % 4
+            Z = listed(m, k, "z", 0)
+            mm([(Z, M("nbig"), R("bsl", r, 128, 4)), (Z, M("nblkb"), U("vin", [12 + k])), (Z, M("blk2b"), R("mx", 32 * k, 32 * k + 32))])
+            ts(R("d0e", 64 * k + 1, 64 * k + 64, 2), Z, 0.0, None, ALU.is_le)
+            act(R("yvb", 128 * m + r, 128 * m + 128, 4), R("d0e", 64 * k + 1, 64 * k + 64, 2), AF.Copy)
+        scan(R("own", to, to + 2 * n), R("d0e", 64 * k0, 64 * k0 + 2 * n), R(P, 0, 2 * n), 0.0, ALU.mult, ALU.add)
+        if not last:
+            send("a_p%d%d" % (m + 1, k0), "next", R("prv", to, to + 2 * n), R("own", to, to + 2 * n))
+        else:
+            for j, k in enumerate(roles):
+                cp(R("yeb", (k - m) % 4, 128, 4), R("own", to + 64 * j + 1, to + 64 * j + 64, 2))
+
+    def commit(m):
+        K, w = par["reach"], R("win", 0, WEND)
+        act(R("rec", 0, 384), R("p7", 0, 384), AF.Identity, bias=col(9))
+        tt(R("plc", 0, 384), R("p6", 0, 384), R("cc", 0, 384), ALU.max)
+        for j in (2, 1, 0):
+            tt(R("pm", 128 * j, 128 * j + 128), R("p6", 384, 512), R("plc", 128 * j, 128 * j + 128), ALU.max)
+        for a, b in par["parts"]:
+            begun.append(1)
+            scan(R("hold", a, b), R("dg0", a, b), R("pm", a, b), -5.0, ALU.max, ALU.min)
+            terms = [(R("p7", a, b), ID, R("cc", a, b))]
+            for k in range(K):
+                e = R("eq", 384 * k + a, 384 * k + b - 16 * k)
+                tt(e, R("p6", a + 16 * k, b), R("hold", a, b - 16 * k), ALU.is_equal)
+                terms.append((R("p7", a + 16 * k, b), M("blk2b"), e))
+            mm(terms[:-1], terms[-1:])
+            scan(R("drop", a, b), R("dg0", a, b), R("p7", a, b), -5.0, ALU.max, ALU.min)
+            tt(R("offf", a // 16, b // 16), R("hold", a + 15, b, 16), R("drop", a + 15, b, 16), ALU.max)
+            ts(R("offs", a // 16, b // 16), R("offf", a // 16, b // 16), float(DB), None, ALU.add)
+            for c in range(b // 16 - K, a // 16 - 1, -K):
+                src, off = R("rec", 16 * c, 16 * (c + K)), R("offs", c, c + K)
+                add("V", lambda e, T, X, src=src, off=off: e.tensor_copy(res(T, w).indirect(res(T, off)), res(T, src)),
+                    [src, off], [w], ("s", 16 * K))
+
+    home = {k: q for q, st in enumerate(par["streams"]) for j in st for k, s in j[0]}
+    for m in range(RU):
+        done, todo = set(), [list(st) for st in par["streams"]]
+        while any(todo):
+            for q, st in enumerate(todo):
+                for k in (C, B, A):
+                    if (k, k) not in done and (k == 0 or (k, k - 1) in done):
+                        begun.append(1)
+                        idle(m, home[k], k)
+                        done.add((k, k))
+                if st and all(s == 0 or (k, s - 1) in done for k, s in st[0][0] + st[0][1]):
+                    begun.append(1)
+                    job(m, q, *st[0])
+                    done.update(st.pop(0)[0])
+        bound(m)
+        for roles in par["verdicts"]:
+            for k in roles:
+                begun.append(1)
+                shadow(m, home[k], k)
+            begun.append(1)
+            verdict(m, home[roles[0]], roles)
         places(m)
-    store("s_ye", lambda T: T.ye[:], M("yeb"))
-    store("s_yv", lambda T: T.yv[:], A("yvb", 0, 384, 1, 0, 128, 16))
+        if m < RU - 1:
+            send("a_n%d" % (m + 1), "prev", R("nxt", 256 * m + 256, 256 * m + 512), R("own", 256 * m + 256, 256 * m + 512))
+            begun.append(1)
+            commit(m)
+    store(lambda T: T.ye[:], M("yeb"))
+    store(lambda T: T.yv[:], R("yvb", 0, 384, 1, (0, 128, 16)))
     return ops
 
 
@@ -415,43 +498,77 @@ def price(ops, k):
     cost = []
     for o in ops:
         kind, n = o["cost"]
-        cost.append({"v": k["fix"] + n * k["c"], "p": 5 + n * k["p"], "g": 65 + n * k["g"] * k["c"], "s": 55 + n * k["s"] * k["c"], "n": n}[kind])
+        cost.append({"v": k["fix"] + n * k["c"], "p": n * k["p"], "g": 65 + n * k["g"] * k["c"], "s": 55 + n * k["s"] * k["c"], "n": n}[kind])
     late = [k["net"] if o["late"] < 0 else o["late"] for o in ops]
-    pred = [[(d, (late[d] + (k["own"] if ops[d]["eng"] == o["eng"] else k["hop"])) if need else 0.0) for d, need in o["deps"].items()] for o in ops]
-    return cost, late, pred
-
-
-def schedule(ops, priced, noise, look):
-    cost, late, pred = priced
-    n = len(ops)
     succ = [[] for _ in ops]
-    for i in range(n):
-        for d, w in pred[i]:
-            succ[d].append((i, w))
-    level = [0.0] * n
-    for i in range(n - 1, -1, -1):
+    for i, o in enumerate(ops):
+        for d, need in o["deps"].items():
+            succ[d].append((i, (late[d] + (k["own"] if ops[d]["eng"] == o["eng"] else k["hop"])) if need else 0.0))
+    level = [0.0] * len(ops)
+    for i in range(len(ops) - 1, -1, -1):
         level[i] = cost[i] + max([w + level[j] for j, w in succ[i]] + [late[i]])
+    return cost, late, succ, level, k
+
+
+def schedule(ops, priced, noise, look=0.3, order=None):
+    cost, late, succ, level, k = priced
+    n = len(ops)
     level = [x + y for x, y in zip(level, noise)]
     for i in range(len(LOADS)):
         level[i] = 1e9 - i
-    left = [len(p) for p in pred]
+    left = [len(o["deps"]) for o in ops]
     can = [0.0] * n
     ready = [i for i in range(n) if left[i] == 0]
-    free, order = {}, []
+    free, bank, out, end = {}, {}, [], [0.0] * n
+
+    def start(i):
+        e = ops[i]["eng"]
+        t = max(can[i], free.get(e, 0.0))
+        for b in ops[i]["banks"]:
+            for e2, x in bank.get(b, {}).items():
+                if e2 != e and x + k["hop"] > t:
+                    t = x + k["hop"]
+        return t
     while ready:
-        first = min(ready, key=lambda i: (max(can[i], free.get(ops[i]["eng"], 0.0)), -level[i]))
-        e = ops[first]["eng"]
-        t = max(can[first], free.get(e, 0.0)) + look * cost[first]
-        i = max((j for j in ready if ops[j]["eng"] == e and can[j] <= t), key=lambda j: level[j])
-        free[e] = max(can[i], free.get(e, 0.0)) + cost[i]
-        order.append(i)
+        if order:
+            i = order[len(out)]
+        else:
+            when = {j: start(j) for j in ready}
+            first = min(ready, key=lambda j: (when[j], -level[j]))
+            t = when[first] + look * cost[first]
+            i = max((j for j in ready if ops[j]["eng"] == ops[first]["eng"] and when[j] <= t), key=lambda j: level[j])
+        e = ops[i]["eng"]
+        end[i] = free[e] = start(i) + cost[i]
+        for b in ops[i]["banks"]:
+            bank.setdefault(b, {})[e] = end[i]
+        out.append(i)
         ready.remove(i)
+        for j in ops[i]["either"]:
+            can[j] = max(can[j], end[i] + (k["own"] if ops[j]["eng"] == e else k["hop"]))
         for j, w in succ[i]:
-            can[j] = max(can[j], free[e] + w)
+            can[j] = max(can[j], end[i] + w)
             left[j] -= 1
             if left[j] == 0:
                 ready.append(j)
-    return order
+    return max(x + y for x, y in zip(end, late)), out, end
+
+
+def search(ops, tries):
+    priced = price(ops, PICTURE)
+    rng, z = np.random.RandomState(0), np.zeros(len(ops))
+    part = np.array([o["part"] for o in ops])
+    best = schedule(ops, priced, z.tolist())
+    for _ in range(tries):
+        y = z.copy()
+        if rng.rand() < 0.3:
+            y[part == rng.randint(part.max() + 1)] += rng.randn() * 1500
+        else:
+            a, w = rng.randint(len(z)), (1, 3, 10, 30)[rng.randint(4)]
+            y[a:a + w] += rng.randn() * 500
+        t = schedule(ops, priced, y.tolist())
+        if t[0] <= best[0]:
+            best, z = t, y
+    return best
 
 
 PLAN = {}
@@ -459,21 +576,22 @@ PLAN = {}
 
 def plan():
     if not PLAN:
-        ops = build()
-        z = np.zeros(len(ops))
-        for t in MOVES:
-            rng = np.random.RandomState(t)
-            a, w = rng.randint(len(z)), (5, 20, 80, 200)[rng.randint(4)]
-            z[a:a + w] += rng.randn() * 600 if rng.rand() < 0.5 else rng.randn(len(z[a:a + w])) * 300
-        order = schedule(ops, price(ops, PICTURE), z.tolist(), 0.3)
+        ops = build(PARAMS)
+        best = search(ops, PARAMS["tries"])
+        order = best[1]
         place = {i: k for k, i in enumerate(order)}
-        for o in ops:
+        bank = {}
+        for i in order:
+            o = ops[i]
+            need = [d for d, x in o["deps"].items() if x] + [d for d in o["either"] if place[d] < place[i]]
+            for b in o["banks"]:
+                need += [d for e, d in bank.get(b, {}).items() if e != o["eng"]]
+                bank.setdefault(b, {})[o["eng"]] = i
             last = {}
-            for d, need in o["deps"].items():
-                if need:
-                    key = ops[d]["eng"] if ops[d]["sem"] is None else d
-                    if key not in last or place[d] > place[last[key]]:
-                        last[key] = d
+            for d in need:
+                key = ops[d]["eng"] if ops[d]["sem"] is None else d
+                if key not in last or place[d] > place[last[key]]:
+                    last[key] = d
             o["waits"] = list(last.values())
         seen, wanted = {}, set()
         for i in order:
@@ -489,7 +607,7 @@ def plan():
             if i in wanted:
                 total[o["eng"]] = total.get(o["eng"], 0) + 1
             o["tick"] = total.get(o["eng"], 0)
-        PLAN.update(ops=ops, order=order, wanted=wanted)
+        PLAN.update(ops=ops, order=order, wanted=wanted, time=best[0])
     return PLAN
 
 
@@ -501,6 +619,7 @@ def rank_program(g, core, T, topo):
     after, before = T.cores[(rank + 1) % n], T.cores[(rank - 1) % n]
     X = {name: tuple(topo.addr(other, core)) + (topo.mask(core, other),) for name, other in (("next", after), ("prev", before))}
     came = {"p": len(topo.engines(before, core)), "n": len(topo.engines(after, core))}
+    went = {"p": len(topo.engines(core, after)), "n": len(topo.engines(core, before))}
     p = plan()
     ops = p["ops"]
     queue = {"V": g.vector, "S": g.scalar, "P": g.tensor, "G": g, "Y": g.sync}
@@ -526,6 +645,5 @@ def rank_program(g, core, T, topo):
             ins.then_inc(T.sem["c" + o["eng"]], 1)
         elif o["sem"] is not None and o["sem"][1] == 16:
             ins.then_inc(T.sem[o["sem"][0]], 16)
-    g.wait_ge(T.sem.sent, len(topo.engines(core, after)) * (2 * RU - 1) + len(topo.engines(core, before)) * RU)
-    for sem in STORES:
-        g.sync.wait_ge(T.sem[sem], 16)
+    g.wait_ge(T.sem.sent, sum(went[o["sem"][0][2]] for o in ops if o["eng"] == "N"))
+    g.sync.wait_ge(T.sem.stored, sum(16 for o in ops if o["sem"] == ("stored", 16)))

@@ -1,3 +1,4 @@
+import math
 import numpy as np
 from concourse.mybir import AluOpType as ALU, ActivationFunctionType as AF
 
@@ -11,41 +12,44 @@ GA = 192
 C, B, A, D = 0, 1, 2, 3
 
 PARAMS = dict(
-    streams=[[([(D, 0)], []), ([(D, 1)], []), ([(D, 2)], [])],
+    streams=[[([(D, 0)], []), ([(D, 1)], [(C, 0)]), ([(D, 2)], [(B, 1)])],
              [([(A, 0)], []), ([(A, 1)], []), ([], [(A, 2)])],
-             [([(C, 1), (B, 0)], [(C, 0)]), ([(C, 2), (B, 2)], [(B, 1)])]],
+             [([(C, 1), (B, 0)], []), ([(C, 2), (B, 2)], [])]],
     verdicts=[[A], [C, B], [D]],
-    cut1=(16, 8, 24), cut2=(16, 0, 24), scans=(1, 1, 2), vq=("V", "S", "S"), reach=4, parts=((192, 384), (0, 192)), tries=2000,
+    cut1=((12, 12, 12), (0, 0), (24, 24)), cut2=((8, 8, 8), (0, 0), (16, 16)),
+    scans=(2, 1, 2), vq=("Z", "S", "Z"),
+    reach=4, parts=((192, 384), (0, 192)), tri="pd1", z="pd0", tries=30000,
 )
 PICTURE = dict(c=0.83, p=0.45, hop=220.0, own=160.0, fix=30.0, g=1.5, s=3.8, net=3500.0)
+PICTURES = [PICTURE, dict(PICTURE, c=1.1, p=0.55, hop=180.0, own=130.0, net=4200.0)]
 
 SCRATCH = {
     "win": ("sbuf", [128, WEND], BF16), "endn": ("sbuf", [128, 128], BF16), "wtb": ("sbuf", [128, 16], BF16),
     "salti": ("sbuf", [128, 128], I32), "nzb": ("sbuf", [128, 1152], BF16), "sli": ("sbuf", [128, 384], I32),
-    "slf": ("sbuf", [128, 384], F32), "saltf": ("sbuf", [128, 7, 32], F32), "salt8": ("sbuf", [128, 21, 32], F32),
+    "slf": ("sbuf", [128, 384], F32), "saltf": ("sbuf", [128, 4, 32], F32), "salt8": ("sbuf", [128, 21, 32], F32),
     "own": ("sbuf", [128, 1024], BF16), "prv": ("sbuf", [128, 768], BF16), "nxt": ("sbuf", [128, 768], BF16),
     "dif": ("sbuf", [128, 144], F32), "gi": ("sbuf", [128, 128], F32), "ai": ("sbuf", [128, 384], F32), "xi": ("sbuf", [128, 384], F32),
     "pi": ("sbuf", [128, 4], I32), "pc": ("sbuf", [128, 16], F32), "w1": ("sbuf", [128, 16], F32), "w2": ("sbuf", [128, 16], F32),
     "rep": ("sbuf", [128, 8], U16), "zb": ("sbuf", [128, 144], BF16), "tmp": ("sbuf", [128, 768], F32),
-    "cst": ("sbuf", [128, 8, 128], BF16), "fid": ("sbuf", [128, 96], BF16),
-    "keep": ("sbuf", [128, 1536], BF16), "rst": ("sbuf", [128, 1536], BF16),
-    "dg0": ("sbuf", [128, 384], F32), "cc": ("sbuf", [128, 384], BF16),
-    "pl": ("sbuf", [128, 12, 32], I32), "adr": ("sbuf", [128, 128], F32), "hold": ("sbuf", [128, 384], F32), "mf": ("sbuf", [128, 12, 64], BF16), "ask": ("sbuf", [128, 12, 32], BF16),
-    "vin": ("sbuf", [128, 16, 32], BF16), "mx": ("sbuf", [128, 128], BF16), "d0e": ("sbuf", [128, 256], BF16),
-    "ab": ("sbuf", [128, 128], BF16), "bsl": ("sbuf", [128, 128], F32), "sg": ("sbuf", [128, 128], F32),
+    "cst": ("sbuf", [128, 8, 128], BF16), "fid": ("sbuf", [128, 96], BF16), "r3": ("sbuf", [128, 64], BF16),
+    "keep": ("sbuf", [128, 1024], BF16), "rst": ("sbuf", [128, 1024], BF16), "vm": ("sbuf", [128, 224], BF16),
+    "dg0": ("sbuf", [128, 384], F32), "cc": ("sbuf", [128, 384], BF16), "adr": ("sbuf", [128, 128], F32), "pos": ("sbuf", [128, 64], F32),
+    "pl": ("sbuf", [128, 12, 32], I32), "mf": ("sbuf", [128, 12, 32], BF16), "ask": ("sbuf", [128, 12, 32], BF16),
+    "vin": ("sbuf", [128, 16, 224], BF16), "mx": ("sbuf", [128, 128], BF16), "d0e": ("sbuf", [128, 256], BF16),
+    "ab": ("sbuf", [128, 128], BF16), "bsl": ("sbuf", [128, 128], F32),
     "sp": ("sbuf", [128, 384], F32), "sa": ("sbuf", [128, 384], BF16), "rec": ("sbuf", [128, 384], BF16),
-    "plc": ("sbuf", [128, 384], F32), "pm": ("sbuf", [128, 384], F32), "eq": ("sbuf", [128, 3072], BF16),
+    "plc": ("sbuf", [128, 384], F32), "pm": ("sbuf", [128, 384], F32), "hold": ("sbuf", [128, 384], F32), "eq": ("sbuf", [128, 2304], BF16),
     "drop": ("sbuf", [128, 384], F32), "offf": ("sbuf", [128, 24], F32), "offs": ("sbuf", [128, 24], U16),
     "yeb": ("sbuf", [128, 128], BF16), "yvb": ("sbuf", [128, 384], F32), "ypb": ("sbuf", [128, 1152], F32),
     "p6": ("psum", [128, 512], F32), "p7": ("psum", [128, 512], F32),
 }
-for _n in ("ident", "nid", "nid1", "idh1", "id3", "idq", "idn", "nidn", "blk", "nblkb", "blk2b", "tri", "ntri", "sel15", "wbd", "wneg"):
+for _n in ("ident", "nid", "nid1", "idh1", "id3", "idq", "idn", "nidn", "blk", "nblkb", "blk2b", "nbigb", "trib", "sel15", "wbd", "wneg", "l3"):
     SCRATCH[_n] = ("sbuf", [128, 128], BF16)
 for _n in ("blkf", "nbig", "sel8"):
     SCRATCH[_n] = ("sbuf", [128, 128], F32)
 for _q in range(3):
-    for _n, _w, _d in (("y", 128, I32), ("o1", 128, U16), ("o2", 128, U16), ("so", 256, F32),
-                       ("ga", 1408, BF16), ("gb", 1024, BF16), ("hi", 1024, BF16), ("lo", 1024, BF16)):
+    for _n, _w, _d in (("y", 128, I32), ("o1", 128, U16), ("o2", 128, U16), ("so", 128, F32),
+                       ("ga", 1408, BF16), ("gb", 1024, BF16), ("hl", 7376, BF16)):
         SCRATCH["%s%d" % (_n, _q)] = ("sbuf", [128, _w], _d)
     for _n in ("pu", "pd"):
         SCRATCH["%s%d" % (_n, _q)] = ("psum", [128, 512], F32)
@@ -116,35 +120,28 @@ def bits(a, exact=True):
 
 
 def build(par):
-    ops, seen, begun = [], {}, []
+    ops, seen = [], {}
 
-    def add(eng, fn, reads, writes, cost, sem=None, late=0.0, after=(), loose=None, held=False):
+    def add(eng, fn, reads, writes, cost, sem=None, late=0.0, after=(), held=False):
         i = len(ops)
-        deps, either = {d: True for d in after}, []
-        dma = sem is not None
-        uses = [(a, False, False) for a in reads if isinstance(a, tuple)] + [(a, True, False) for a in writes]
-        if loose:
-            uses.append((loose, False, True))
+        deps = {d: True for d in after}
+        uses = [(a, False) for a in reads if isinstance(a, tuple)] + [(a, True) for a in writes]
         mine = []
-        for a, wr, lo in uses:
+        for a, wr in uses:
             e, w = bits(a), bits(a, False)
-            for j, be, bw, bwr, blo in seen.get(a[0], []):
+            for j, be, bw, bwr in seen.get(a[0], []):
                 o = ops[j]
                 if eng == "P" and o["eng"] == "P" and psum(a):
                     if held or o["held"] or e & be:
                         deps.setdefault(j, False)
-                elif (wr or bwr) and ((w & bw) if dma or o["sem"] is not None else (e & be)):
-                    if (lo or blo) and not o["first"]:
-                        either.append(j)
-                        o["either"].append(i)
-                    else:
-                        deps[j] = True
-            mine.append((a[0], (i, e, w, wr, lo)))
+                elif (wr or bwr) and ((w & bw) if sem is not None or o["sem"] is not None else (e & be)):
+                    deps[j] = True
+            mine.append((a[0], (i, e, w, wr)))
         for n, x in mine:
             seen.setdefault(n, []).append(x)
-        ops.append(dict(eng=eng, fn=fn, deps=deps, cost=cost, sem=sem, late=late, either=either, first=not begun, held=held, part=len(begun),
+        ops.append(dict(eng=eng, fn=fn, deps=deps, cost=cost, sem=sem, late=late, held=held,
                         tag=(writes or reads)[0][0] + str((writes or reads)[0][1][0]),
-                        banks=sorted(set(a[0] for a, _, _ in uses if psum(a)))))
+                        banks=sorted(set(a[0] for a, _ in uses if psum(a)))))
         return i
 
     def vc(n, rate):
@@ -174,6 +171,9 @@ def build(par):
     def act(o, a, func, bias=0.0, scale=1.0):
         return add("S", lambda q, T, X: q.activation(res(T, o), res(T, a), func, bias=res(T, bias), scale=scale), [a, bias], [o], vc(cnt(o), 1))
 
+    def fill(o, val):
+        return act(o, R("dif", 0, cnt(o)), AF.Identity, bias=val, scale=0.0)
+
     def mm(*parts):
         for k, terms in enumerate(parts):
             def fn(q, T, X, terms=terms, k=k):
@@ -183,20 +183,19 @@ def build(par):
             add("P", fn, [a for t in terms for a in t[1:]], [t[0] for t in terms],
                 ("p", sum(10 + max(64, cnt(r)) * (4 if SCRATCH[r[0]][2] == F32 else 1) for _, _, r in terms)), held=len(parts) > 1)
 
-    def gather(eng, o, w, off, loose=None):
-        whole = w if not loose else R(w[0], min(w[1][0], loose[1][0]), max(w[1][-1], loose[1][-1]) + 1)
+    def gather(eng, o, w, off):
         if eng == "V":
-            fn = lambda q, T, X: q.tensor_copy(res(T, o), res(T, whole).indirect(res(T, off)))
+            fn = lambda q, T, X: q.tensor_copy(res(T, o), res(T, w).indirect(res(T, off)))
         else:
-            fn = lambda q, T, X: q.activation(res(T, o), res(T, whole).indirect(res(T, off)), AF.Copy)
-        return add(eng, fn, [w, off], [o], ("g", cnt(o)), loose=loose)
+            fn = lambda q, T, X: q.activation(res(T, o), res(T, w).indirect(res(T, off)), AF.Copy)
+        return add(eng, fn, [w, off], [o], ("g", cnt(o)))
 
-    def iota(o, pat, base, mult):
+    def iota(o, pat, base, mult, after=()):
         if SCRATCH[o[0]][2] == I32:
             fn = lambda q, T, X: q.iota(res(T, o), pat, base, mult)
         else:
             fn = lambda q, T, X: q.iota(res(T, o), pat, base, mult, allow_small_or_imprecise_dtypes=True)
-        return add("G", fn, [], [o], ("n", 150 + 2.1 * cnt(o)))
+        return add("G", fn, [], [o], ("n", 150 + 2.1 * cnt(o)), after=after)
 
     def load(eng, sem, o, src, late):
         return add(eng, lambda q, T, X: q.dma_start(res(T, o), src(T)), [], [o], ("n", 60), sem=(sem, 16), late=late)
@@ -209,17 +208,20 @@ def build(par):
             rid, pid, mask = X[to]
             q.remote_dma(res(T, o), res(T, a), T.sem[sem], T.sem.sent, pid, rid, mask)
         i = add("G", fn, [a], [], ("n", 300), sem=("sent", 0))
-        return add("N", None, [], [o], ("n", 0), sem=(sem, -1), late=-1.0, after=[i])
+        add("N", None, [], [o], ("n", 0), sem=(sem, -1), late=-1.0, after=[i])
+        return i
 
     M = lambda n: R(n, 0, 128)
     col = lambda k: R("pc", k, k + 1)
     ID, NID, D128 = M("ident"), M("nid"), M("dif")
+    three, eight = (0, 3, 1), (0, 8, 1)
     const = lambda k, n: ("cst", tuple(range(128 * k, 128 * k + n)), (0, 128, 1))
     unit = lambda k, s: 4 * (2 - s) + k
     fresh = {it: ("ga%d" % q, 64 * j + 32 * i) for q, st in enumerate(par["streams"]) for j, jb in enumerate(st) for i, it in enumerate(jb[0])}
     fresh.update({(k, k): ("fid", 32 * k) for k in (C, B, A)})
     F = lambda k, s: R(fresh[k, s][0], fresh[k, s][1], fresh[k, s][1] + 32)
-    after = lambda k, s: U("vin", [unit(k, s + 1) if s < ST - 1 else 12 + k])
+    vin = lambda units: U("vin", units, 5, 7)
+    after = lambda k, s: unit(k, s + 1) if s < ST - 1 else 12 + k
 
     load("Y", "l_end", M("endn"), lambda T: T.ends[:], 2200.0)
     load("S", "l_db0", R("win", DB, DB + 2048), lambda T: T.db[:, 0:2048], 6000.0)
@@ -227,24 +229,30 @@ def build(par):
     load("Y", "l_salt", M("salti"), lambda T: T.salt[:], 3000.0)
     load("Y", "l_db1", R("win", DB + 2048, SP), lambda T: T.db[:, 2048:4096], 6000.0)
     load("S", "l_nz", R("nzb", 0, 1152), lambda T: T.nz[:], 6500.0)
-    load("Y", "l_sl", R("sli", 0, 384, 1, (0, 8, 1)), lambda T: T.sl[:], 6500.0)
-    send("a_p0", "next", R("prv", 0, 128), M("endn"))
+    load("Y", "l_sl", R("sli", 0, 384, 1, eight), lambda T: T.sl[:], 6500.0)
+    sent = send("a_p0", "next", R("prv", 0, 128), M("endn"))
 
     iota(R("pi", 0, 1), [[0, 1]], 0, 1)
     iota(R("dif", 0, 144), [[1, 144]], 0, -1)
     iota(M("gi"), [[1, 8], [0, 16]], 0, 0)
-    iota(R("xi", 0, 384), [[1, 384]], 0, 0)
-    iota(R("ai", 0, 384), [[0, 24], [1, 16]], 0, 0)
+    iota(R("xi", 0, 384), [[1, 384]], 0, 0, [sent])
+    iota(R("ai", 0, 384), [[0, 24], [1, 16]], 0, 0, [sent])
     ts(R("pi", 1, 2), R("pi", 0, 1), 4, None, ALU.arith_shift_right)
     ts(R("pi", 2, 3), R("pi", 0, 1), 15, None, ALU.bitwise_and)
     cp(R("pc", 0, 3), R("pi", 0, 3))
-    for k, val in ((3, 1.0), (4, ONE), (5, -55.0 / 8192), (6, 7.0 / 128), (7, 1.75), (8, -1.0 / 256), (9, -121.0)):
+    for k, val in ((3, 1.0), (4, ONE), (5, -55.0 / 8192), (6, 7.0 / 128), (7, 1.75), (8, -1.0 / 256), (9, -121.0), (13, BIG)):
         ts(col(k), col(2), 15.0, val, ALU.is_equal, ALU.mult)
     ts(col(10), col(2), 15.0, None, ALU.not_equal)
     ts(col(11), col(3), 0.5 + 1.0 / 256, 0.5, ALU.mult, ALU.add)
-    ms(R("own", 0, 256, 2), 0.0)
+    ts(col(12), col(2), float(GA), None, ALU.add)
+    ts(col(14), col(3), ONE + 0.75, -0.75, ALU.mult, ALU.add)
+    ts(col(15), col(3), 0.5, 0.5, ALU.mult, ALU.add)
+    ms(R("vm", 0, 224), 1.0)
+    for k, val in ((0, 0.0), (2, 0.5), (3, col(10)), (4, col(15))):
+        fill(R("vm", k, 224, 7), val)
+    fill(R("own", 0, 256, 2), 0.0)
     for k in range(4):
-        ts(R("own", 64 * k + 1, 64 * k + 64, 2), R("endn", k, 128, 4), col(4), None, ALU.add)
+        act(R("own", 64 * k + 1, 64 * k + 64, 2), R("endn", k, 128, 4), AF.Identity, bias=col(4))
     send("a_n0", "prev", R("nxt", 0, 256), R("own", 0, 256))
     ts(ID, D128, 0.0, None, ALU.is_equal)
     ts(M("blkf"), M("gi"), col(1), None, ALU.is_equal)
@@ -255,15 +263,18 @@ def build(par):
             [R(w, 0, 16), R("rep", 0, 8), M("blkf")], [M(to)], ("g", 128))
     for k, val in ((0, M1), (1, M8), (2, -M8), (3, M256), (4, -M256), (5, 15.0), (7, M2)):
         ms(const(k, 128), val)
-    ts(const(6, 128), M("gi"), 0.0, col(4), ALU.mult, ALU.add)
-    for r in range(7):
-        cp(U("saltf", [r]), R("salti", r % 4, 128, 4))
+    fill(const(6, 128), col(4))
+    for r in range(4):
+        cp(U("saltf", [r]), R("salti", r, 128, 4))
     for s in range(ST):
-        act(U("salt8", range(14 - 7 * s, 21 - 7 * s)), U("saltf", range(7)), AF.Identity, bias=8.0 * 211 * s - 148.0 ** 2, scale=8.0)
+        for a, n in ((14, 4), (18, 3)):
+            act(U("salt8", range(a - 7 * s, a + n - 7 * s)), U("saltf", range(n)), AF.Identity, bias=8.0 * 211 * s - 148.0 ** 2, scale=8.0)
     act(NID, ID, AF.Copy, scale=-1.0)
+    act(M("nbigb"), ID, AF.Copy, scale=-BIG)
+    act(M("nbig"), ID, AF.Copy, scale=-BIG)
     ts(R("tmp", 0, 128), M("blkf"), col(7), None, ALU.mult)
     tt(M("nid1"), R("tmp", 0, 128), ID, ALU.subtract)
-    ts(R("zb", 0, 144), R("dif", 0, 144), 0.0, col(3), ALU.is_equal, ALU.mult)
+    ts(R("zb", 0, 144), R("dif", 0, 144), 0.0, col(13), ALU.is_equal, ALU.mult)
     ts(M("idn"), D128, 0.0, col(10), ALU.is_equal, ALU.mult)
     act(M("idq"), M("idn"), AF.Copy, scale=0.25)
     act(M("nidn"), M("idn"), AF.Copy, scale=-1.0)
@@ -274,39 +285,47 @@ def build(par):
     tt(M("id3"), R("tmp", 640, 768), M("idn"), ALU.add)
     ms(R("win", 0, DB), 0.0)
     ms(R("win", SP, WEND), 0.0)
-    for q in range(3):
-        ms(R("ga%d" % q, 0, GA), 0.0)
-    wide = 512 * max(len(j[0]) for st in par["streams"] for j in st)
-    ms(R("keep", 0, wide), 1.0)
-    ms(R("keep", 0, wide, 16), 0.0)
-    act(R("rst", 0, wide), R("keep", 0, wide), AF.Identity, bias=255.0, scale=-255.0)
-    ms(U("mf", range(12)), -BIG)
-    ts(col(12), col(2), float(GA), None, ALU.add)
-    act(R("adr", 0, 128, 2), R("xi", 0, 64), AF.Identity, bias=col(12), scale=16.0)
+    ms(R("keep", 0, 1024), 1.0)
+    ms(R("keep", 0, 1024, 16), 0.0)
+    act(R("rst", 0, 1024), R("keep", 0, 1024), AF.Identity, bias=255.0, scale=-255.0)
+    fill(U("mf", (2, 5, 8)), 1.0)
+    act(R("pos", 0, 64), R("xi", 0, 64), AF.Identity, bias=col(12), scale=16.0)
+    fill(R("adr", 0, 128, 2), 1e6)
     act(R("adr", 1, 128, 2), R("xi", 0, 64), AF.Copy)
-    ms(R("d0e", 0, 256, 2), 0.0)
+    for q, st in enumerate(par["streams"]):
+        na = 32 * len(st[0][0])
+        ms(R("ga%d" % q, 0, GA), 0.0)
+        act(R("pd%d" % q, 1, 2 * na, 2), R("xi", 0, na), AF.Identity, bias=float(GA + 16 * na))
+        if par["vq"][q] == "Z":
+            for k, val in ((3, col(14)), (4, M1), (5, -M1), (6, 0.0)):
+                fill(R("hl%d" % q, 105 + 16 * k, 112 * na + 105, 112), val)
+    fill(R("d0e", 0, 256, 2), 0.0)
     act(M("blk"), M("blkf"), AF.Copy)
     act(M("nblkb"), M("blkf"), AF.Copy, scale=-BIG)
     act(M("blk2b"), M("blkf"), AF.Copy, scale=2 * BIG)
-    act(M("nbig"), ID, AF.Copy, scale=-BIG)
-    ts(R("tmp", 384, 512), D128, 0.0, None, ALU.is_gt)
-    tt(R("tmp", 512, 640), R("tmp", 384, 512), ID, ALU.subtract)
-    tt(M("ntri"), R("tmp", 512, 640), M("blkf"), ALU.mult)
+    ts(R("tmp", 384, 512), D128, 0.0, -BIG, ALU.is_gt, ALU.mult)
+    tt(R("tmp", 512, 640), R("tmp", 384, 512), M("nbig"), ALU.subtract)
+    tt(M("trib"), R("tmp", 512, 640), M("blkf"), ALU.mult)
+    ms(R("l3", 0, 128, 1, three), 136 * BIG)
+    cp(R("l3", 0, 128, 1, (0, 2, 1)), R("ai", 0, 128, 1, (0, 2, 1)))
+    ms(R("l3", 0, 128, 1, (0, 1, 1)), 1.0)
+    ms(R("r3", 0, 64, 1, three), 1.0)
+    ts(R("r3", 0, 64, 1, (0, 1, 1)), R("xi", 0, 64, 1, (0, 1, 1)), 16.0, float(GA), ALU.mult, ALU.add)
     ms(M("sel15"), 0.0)
     cp(R("sel15", 15, 128, 16), R("blkf", 15, 128, 16))
-    eight = (0, 8, 1)
     ts(R("sel8", 0, 128, 1, eight), R("gi", 0, 128, 1, eight), R("pc", 0, 1, 1, eight), None, ALU.is_equal)
     cp(R("slf", 0, 384, 1, eight), R("sli", 0, 384, 1, eight))
     ts(R("pm", 0, 384), R("ai", 0, 384), col(2), 4 * BIG, ALU.not_equal, ALU.mult)
     act(R("drop", 0, 384), R("xi", 0, 384), AF.Identity, bias=4096.0)
     tt(R("dg0", 0, 384), R("drop", 0, 384), R("pm", 0, 384), ALU.subtract)
     act(R("cc", 0, 384), R("pm", 0, 384), AF.Identity, bias=-3 * BIG, scale=2.0)
-    begun.append(1)
+
+    def start(m, k, s):
+        return vin([unit(k, s)]) if s else R("prv", 256 * m + 64 * k + 1, 256 * m + 64 * k + 64, 2) if m else R("prv", k, 128, 4)
 
     def of_v(m, items, P, c0, l):
-        src = [U("vin", [unit(k, s)]) if s else R("prv", 256 * m + 64 * k + 1, 256 * m + 64 * k + 64, 2) if m else R("prv", k, 128, 4) for k, s in items]
         out = [R(P, c0 + 32 * j, c0 + 32 * j + 32) for j in range(len(items))]
-        terms = [(o, l, v) for o, v in join(out, src)]
+        terms = [(o, l, v) for o, v in join(out, [start(m, k, s) for k, s in items])]
         if l is not ID:
             terms += [(o[0], l, const(6, cnt(o[0]))) for o in join([o for o, (k, s) in zip(out, items) if m == 0 and s == 0])]
         return terms
@@ -319,27 +338,22 @@ def build(par):
                 + [(R(P, c0, c0 + n), ID, const(3, n)), (R(P, c0, c0 + n), ID, const(4, n))]
                 + [(o, ID, z) for o, z in zip(out, nz)] + of_v(m, items, P, c0, l))
 
-    def fresh_of(m, items, P, c0):
+    def fresh_of(m, items, P, c0, again=None):
         mm(fresh_terms(m, items, P, c0, ID))
+        if again:
+            act(again, R(P, c0, c0 + cnt(again)), AF.Copy)
         for o, a in join([F(k, s) for k, s in items], [R(P, c0 + 32 * j, c0 + 32 * j + 32) for j in range(len(items))]):
             act(o, a, AF.Copy)
-
-    def state(m, q, items, P, c0, terms):
-        n = 32 * len(items)
-        on_s = par["vq"][q] == "S"
-        mm(of_v(m, items, P, c0, M("idh1")) + terms + ([(R(P, c0, c0 + n), ID, const(0, n))] if on_s else []))
-        for o, a in join([after(k, s) for k, s in items], [R(P, c0 + 32 * j, c0 + 32 * j + 32) for j in range(len(items))]):
-            if on_s:
-                act(o, a, AF.Identity, bias=-M1)
-            else:
-                ts(o, a, M1, M1, ALU.add, ALU.subtract)
 
     def idle(m, q, k):
         P = "pu%d" % q
         mm(fresh_terms(m, [(k, k)], P, 416, M("id3")) + [(R(P, 416, 448), ID, const(7, 32))])
-        act(after(k, k), R(P, 416, 448), AF.Identity, bias=-M2 / 2, scale=0.5)
+        act(vin([after(k, k)]), R(P, 416, 448), AF.Identity, bias=-M2 / 2, scale=0.5)
         if m < RU - 1:
             fresh_of(m, [(k, k)], P, 384)
+
+    def pieces(e, n):
+        return [x for x in (("V", 0, e), ("S", e, n)) if x[2] > x[1]]
 
     def job(m, q, real, riders):
         items = real + riders
@@ -357,10 +371,8 @@ def build(par):
             w0 = fresh[real[0]][1]
             for o, x in join(each("o1%d" % q, real), [U("pl", [unit(k, s)]) for k, s in real]):
                 cp(o, x)
-            e = par["cut1"][q]
-            for eng, a0, a1 in (("S", e, na), ("V", 0, e)):
-                if a1 > a0:
-                    gather(eng, b("ga", w0 + GA + 16 * a0, w0 + GA + 16 * a1), R("win", DB, SP), b("o1", a0, a1))
+            for eng, a0, a1 in pieces(par["cut1"][q][w0 // 64], na):
+                gather(eng, b("ga", w0 + GA + 16 * a0, w0 + GA + 16 * a1), R("win", DB, SP), b("o1", a0, a1))
         its = items if m < RU - 1 else real
         if its:
             w = 32 * len(its)
@@ -370,45 +382,49 @@ def build(par):
                 act(o, x, AF.Identity, bias=136.0)
         if not real:
             return
-        fresh_of(m, real, PU, 128)
-        mm([(o, NID, x) for o, x in join(each(PD, real), [U("ask", [unit(k, s)]) for k, s in real])]
-           + [(R(PD, 0, na), R("zb", 15 - p, 143 - p), b("ga", w0 + GA + p, w0 + GA + 16 * na, 16)) for p in range(16)])
-        for o, x in join([U("mf", [unit(k, s)], 1, 2) for k, s in real], each(PD, real)):
-            ts(o, x, -136.0, -BIG, ALU.not_equal, ALU.mult)
-        for j, (k, s) in enumerate(real):
-            scan(b("so", 64 * j, 64 * j + 64), U("mf", [unit(k, s)]), R("adr", 64 * j, 64 * j + 64), 0.0, ALU.add, ALU.max)
+        fresh_of(m, real, PU, 128, b("ga", w0 + GA + 16 * na, w0 + GA + 17 * na))
+        E = R(PD, 0, 2 * na, 2)
+        mm([(E, R("l3", 0, 128, 1, three), R("r3", 0, na, 1, three))]
+           + [(o, M("nbigb"), x) for o, x in join(each(PD, real, 64, 0, 2), [U("ask", [unit(k, s)]) for k, s in real])],
+           [(E, R("zb", 15 - p, 143 - p), b("ga", w0 + GA + p, w0 + GA + 16 * na, 16)) for p in range(16)])
+        scan(b("so", 0, 2 * na), R("adr", 0, 2 * na), R(PD, 0, 2 * na), 0.0, ALU.max, ALU.min)
         cp(b("o2", 0, na), b("so", 1, 2 * na, 2))
-        e = par["cut2"][q]
-        for eng, a0, a1 in (("S", e, na), ("V", 0, e)):
-            if a1 > a0:
-                gather(eng, b("gb", 16 * a0, 16 * a1), b("ga", w0, w0 + GA + 16 * na), b("o2", a0, a1))
-        for a0, a1 in ((0, e), (e, na)) if par["scans"][q] == 2 and 0 < e < na else ((0, na),):
-            scan(b("hi", 16 * a0, 16 * a1), R("keep", 0, 16 * (a1 - a0)), b("gb", 16 * a0, 16 * a1), 0.0, ALU.mult, ALU.max)
-            scan(b("lo", 16 * a0, 16 * a1), R("rst", 0, 16 * (a1 - a0)), b("gb", 16 * a0, 16 * a1), 0.0, ALU.max, ALU.min)
-        state(m, q, real, PU, 256, [(R(PU, 256, 256 + na), M("idq"), b(x, 15, 16 * na, 16)) for x in ("hi", "lo")])
+        for o, x, z in join([U("mf", [unit(k, s)]) for k, s in real], each("so%d" % q, real, 64, 1, 2), each("pos", real)):
+            tt(o, x, z, ALU.not_equal)
+        cut = pieces(par["cut2"][q][w0 // 64], na)
+        for eng, a0, a1 in cut:
+            gather(eng, b("gb", 16 * a0, 16 * a1), b("ga", w0, w0 + GA + 17 * na), b("o2", a0, a1))
+        for a0, a1 in [x[1:] for x in cut] if par["scans"][q] == 2 else ((0, na),):
+            scan(b("hl", 112 * a0, 112 * a1, 7), R("keep", 0, 16 * (a1 - a0)), b("gb", 16 * a0, 16 * a1), 0.0, ALU.mult, ALU.max)
+            scan(b("hl", 112 * a0 + 16, 112 * a1 + 16, 7), R("rst", 0, 16 * (a1 - a0)), b("gb", 16 * a0, 16 * a1), 0.0, ALU.max, ALU.min)
+        if par["vq"][q] == "Z":
+            for j, (k, s) in enumerate(real):
+                act(b("hl", 3584 * j + 137, 3584 * (j + 1) + 105, 112), start(m, k, s), AF.Copy)
+                scan(U("vin", [after(k, s)]), R("vm", 0, 224), b("hl", 3584 * j + 105, 3584 * (j + 1) + 105, 16), 0.0, ALU.mult, ALU.add)
+        else:
+            P = R(PU, 256, 256 + na)
+            mm(of_v(m, real, PU, 256, M("idh1")) + [(P, M("idq"), b("hl", x, 112 * na + 105, 112)) for x in (105, 121)] + [(P, ID, const(0, na))])
+            for o, a in join([vin([after(k, s)]) for k, s in real], [R(PU, 256 + 32 * j, 288 + 32 * j) for j in range(len(real))]):
+                act(o, a, AF.Identity, bias=-M1)
 
-    def listed(m, k, what, j=None):
-        P, c = dict(place=("p6", 0), rec=("p7", 0), z=("p6", 384))[what]
-        r = (k - m) % 4
-        return R(P, c + r, c + 384, 4) if j is None else R(P, c + 128 * j + r, c + 128 * (j + 1), 4)
+    def listed(m, k, P, x0):
+        return R(P, x0 + (k - m) % 4, x0 + 128, 4)
 
-    def shadow(m, q, k):
-        r, units = (k - m) % 4, (k, k + 4, k + 8)
-        P, sp, sa = R("pd%d" % q, 256, 352), R("sp", 96 * k, 96 * k + 96), R("sa", 96 * k, 96 * k + 96)
-        mm([(P, M("ntri"), U("mf", units, 1, 2))])
+    def shadow(m, s):
+        units, x0, P = range(8 - 4 * s, 12 - 4 * s), 128 * (2 - s), R(par["tri"], 256, 384)
+        mm([(P, M("trib"), U("mf", units))])
         ts(P, P, -1.0, -1.0, ALU.add, ALU.max)
-        tt(sp, P, U("pl", units), ALU.min)
+        tt(R("sp", x0, x0 + 128), P, U("pl", units), ALU.min)
         if m < RU - 1:
-            tt(sa, P, U("ask", units), ALU.min)
-        mm([(listed(m, k, "place"), ID, const(5, 96)), (listed(m, k, "place"), M("blkf"), sp)])
-        act(R("ypb", 384 * m + r, 384 * m + 384, 4), listed(m, k, "place"), AF.Copy)
+            tt(R("sa", x0, x0 + 128), P, U("ask", units), ALU.min)
+        mm([(R("p6", x0, x0 + 128), ID, const(5, 128))] + [(listed(m, k, "p6", x0), M("blkf"), R("sp", x0 + 32 * k, x0 + 32 * k + 32)) for k in range(4)])
+        act(R("ypb", 384 * m + x0, 384 * m + x0 + 128), R("p6", x0, x0 + 128), AF.Copy)
+        z = 128 * (m * ST + s)
+        store(lambda T: T.yp[:, z:z + 128], R("ypb", 384 * m + x0, 384 * m + x0 + 128, 1, (0, 128, 16)))
         if m < RU - 1:
-            mm([(listed(m, k, "rec", j), M("idn"), F(k, 2 - j)) for j in range(ST)] + [(listed(m, k, "rec"), M("sel15"), sa)])
-
-    def places(m):
-        for s in range(ST):
-            z, c = 128 * (m * ST + s), 384 * m + 128 * (2 - s)
-            store(lambda T, z=z: T.yp[:, z:z + 128], R("ypb", c, c + 128, 1, (0, 128, 16)))
+            tt(R("plc", x0, x0 + 128), R("p6", x0, x0 + 128), R("cc", x0, x0 + 128), ALU.max)
+            mm([(listed(m, k, "p7", x0), l, x) for k in range(4) for l, x in ((M("idn"), F(k, s)), (M("sel15"), R("sa", x0 + 32 * k, x0 + 32 * k + 32)))])
+            act(R("rec", x0, x0 + 128), R("p7", x0, x0 + 128), AF.Identity, bias=col(9))
 
     def bound(m):
         c = 256 * m
@@ -416,21 +432,20 @@ def build(par):
         mm([(P, ID, R("own", c + 1, c + 256, 2)), (P, NID, R("nxt", c + 1, c + 256, 2))])
         act(M("ab"), P, AF.Abs)
         mm([(P, R("sel8", 0, 128, 1, eight), R("slf", 128 * m, 128 * m + 128, 1, eight))]
-           + [(R("p7", 384 + (k - m) % 4, 512, 4), M("blk"), x) for k in range(4)
+           + [(listed(m, k, "p7", 384), M("blk"), x) for k in range(4)
               for x in (R("ab", 32 * k, 32 * k + 32), R("nxt", c + 64 * k + 1, c + 64 * k + 64, 2))])
         act(M("bsl"), P, AF.Identity, bias=0.25)
 
     def verdict(m, q, roles):
         k0, n, P = roles[0], 32 * len(roles), "pu%d" % q
         c, to = 256 * m + 64 * k0, 256 * (m + 1) + 64 * ((k0 + 1) % 4)
-        v, e, last = U("vin", [12 + k for k in roles]), R("own", c + 1, c + 2 * n, 2), m == RU - 1
+        v, e, last = vin([12 + k for k in roles]), R("own", c + 1, c + 2 * n, 2), m == RU - 1
         tt(R("mx", 32 * k0, 32 * k0 + n), v, R("nxt", c + 1, c + 2 * n, 2), ALU.max)
         mm([(R(P, 1, 2 * n, 2), M("idn") if last else ID, e)])
         mm([(R(P, 0, 2 * n, 2), M("nidn") if last else NID, e), (R(P, 0, 2 * n, 2), M("idn") if last else ID, v)])
         for k in roles:
-            r = (k - m) % 4
-            Z = listed(m, k, "z", 0)
-            mm([(Z, M("nbig"), R("bsl", r, 128, 4)), (Z, M("nblkb"), U("vin", [12 + k])), (Z, M("blk2b"), R("mx", 32 * k, 32 * k + 32))])
+            r, Z = (k - m) % 4, listed(m, k, par["z"], 384)
+            mm([(Z, M("nbig"), R("bsl", r, 128, 4)), (Z, M("nblkb"), vin([12 + k])), (Z, M("blk2b"), R("mx", 32 * k, 32 * k + 32))])
             ts(R("d0e", 64 * k + 1, 64 * k + 64, 2), Z, 0.0, None, ALU.is_le)
             act(R("yvb", 128 * m + r, 128 * m + 128, 4), R("d0e", 64 * k + 1, 64 * k + 64, 2), AF.Copy)
         scan(R("own", to, to + 2 * n), R("d0e", 64 * k0, 64 * k0 + 2 * n), R(P, 0, 2 * n), 0.0, ALU.mult, ALU.add)
@@ -438,16 +453,13 @@ def build(par):
             send("a_p%d%d" % (m + 1, k0), "next", R("prv", to, to + 2 * n), R("own", to, to + 2 * n))
         else:
             for j, k in enumerate(roles):
-                cp(R("yeb", (k - m) % 4, 128, 4), R("own", to + 64 * j + 1, to + 64 * j + 64, 2))
+                cp(listed(m, k, "yeb", 0), R("own", to + 64 * j + 1, to + 64 * j + 64, 2))
 
     def commit(m):
         K, w = par["reach"], R("win", 0, WEND)
-        act(R("rec", 0, 384), R("p7", 0, 384), AF.Identity, bias=col(9))
-        tt(R("plc", 0, 384), R("p6", 0, 384), R("cc", 0, 384), ALU.max)
         for j in (2, 1, 0):
-            tt(R("pm", 128 * j, 128 * j + 128), R("p6", 384, 512), R("plc", 128 * j, 128 * j + 128), ALU.max)
+            tt(R("pm", 128 * j, 128 * j + 128), R(par["z"], 384, 512), R("plc", 128 * j, 128 * j + 128), ALU.max)
         for a, b in par["parts"]:
-            begun.append(1)
             scan(R("hold", a, b), R("dg0", a, b), R("pm", a, b), -5.0, ALU.max, ALU.min)
             terms = [(R("p7", a, b), ID, R("cc", a, b))]
             for k in range(K):
@@ -470,27 +482,28 @@ def build(par):
             for q, st in enumerate(todo):
                 for k in (C, B, A):
                     if (k, k) not in done and (k == 0 or (k, k - 1) in done):
-                        begun.append(1)
                         idle(m, home[k], k)
                         done.add((k, k))
                 if st and all(s == 0 or (k, s - 1) in done for k, s in st[0][0] + st[0][1]):
-                    begun.append(1)
                     job(m, q, *st[0])
                     done.update(st.pop(0)[0])
         bound(m)
+        for s in range(ST):
+            shadow(m, s)
         for roles in par["verdicts"]:
-            for k in roles:
-                begun.append(1)
-                shadow(m, home[k], k)
-            begun.append(1)
             verdict(m, home[roles[0]], roles)
-        places(m)
         if m < RU - 1:
             send("a_n%d" % (m + 1), "prev", R("nxt", 256 * m + 256, 256 * m + 512), R("own", 256 * m + 256, 256 * m + 512))
-            begun.append(1)
             commit(m)
     store(lambda T: T.ye[:], M("yeb"))
     store(lambda T: T.yv[:], R("yvb", 0, 384, 1, (0, 128, 16)))
+    above = []
+    for o in ops:
+        far = 0
+        for d in o["deps"]:
+            far |= above[d]
+        o["near"] = {d: x for d, x in o["deps"].items() if not far >> d & 1}
+        above.append(far | sum(1 << d for d in o["near"]))
     return ops
 
 
@@ -500,75 +513,120 @@ def price(ops, k):
         kind, n = o["cost"]
         cost.append({"v": k["fix"] + n * k["c"], "p": n * k["p"], "g": 65 + n * k["g"] * k["c"], "s": 55 + n * k["s"] * k["c"], "n": n}[kind])
     late = [k["net"] if o["late"] < 0 else o["late"] for o in ops]
-    succ = [[] for _ in ops]
-    for i, o in enumerate(ops):
-        for d, need in o["deps"].items():
-            succ[d].append((i, (late[d] + (k["own"] if ops[d]["eng"] == o["eng"] else k["hop"])) if need else 0.0))
-    level = [0.0] * len(ops)
-    for i in range(len(ops) - 1, -1, -1):
-        level[i] = cost[i] + max([w + level[j] for j, w in succ[i]] + [late[i]])
-    return cost, late, succ, level, k
+    pred = [[(d, (late[d] + (k["own"] if ops[d]["eng"] == o["eng"] else k["hop"])) if need else 0.0) for d, need in o["near"].items()] for o in ops]
+    return cost, late, pred
 
 
-def schedule(ops, priced, noise, look=0.3, order=None):
-    cost, late, succ, level, k = priced
+def first_order(ops, k, look=0.3):
+    cost, late, pred = price(ops, k)
     n = len(ops)
-    level = [x + y for x, y in zip(level, noise)]
+    succ = [[] for _ in ops]
+    for i in range(n):
+        for d, w in pred[i]:
+            succ[d].append((i, w))
+    level = [0.0] * n
+    for i in range(n - 1, -1, -1):
+        level[i] = cost[i] + max([w + level[j] for j, w in succ[i]] + [late[i]])
     for i in range(len(LOADS)):
         level[i] = 1e9 - i
-    left = [len(o["deps"]) for o in ops]
+    left = [len(p) for p in pred]
     can = [0.0] * n
     ready = [i for i in range(n) if left[i] == 0]
-    free, bank, out, end = {}, {}, [], [0.0] * n
+    free, bank, out = {}, {}, []
 
     def start(i):
         e = ops[i]["eng"]
-        t = max(can[i], free.get(e, 0.0))
-        for b in ops[i]["banks"]:
-            for e2, x in bank.get(b, {}).items():
-                if e2 != e and x + k["hop"] > t:
-                    t = x + k["hop"]
-        return t
+        return max([can[i], free.get(e, 0.0)] + [x + k["hop"] for b in ops[i]["banks"] for e2, x in bank.get(b, {}).items() if e2 != e])
     while ready:
-        if order:
-            i = order[len(out)]
-        else:
-            when = {j: start(j) for j in ready}
-            first = min(ready, key=lambda j: (when[j], -level[j]))
-            t = when[first] + look * cost[first]
-            i = max((j for j in ready if ops[j]["eng"] == ops[first]["eng"] and when[j] <= t), key=lambda j: level[j])
-        e = ops[i]["eng"]
-        end[i] = free[e] = start(i) + cost[i]
+        when = {j: start(j) for j in ready}
+        first = min(ready, key=lambda j: (when[j], -level[j]))
+        t = when[first] + look * cost[first]
+        i = max((j for j in ready if ops[j]["eng"] == ops[first]["eng"] and when[j] <= t), key=lambda j: level[j])
+        end = free[ops[i]["eng"]] = when[i] + cost[i]
         for b in ops[i]["banks"]:
-            bank.setdefault(b, {})[e] = end[i]
+            bank.setdefault(b, {})[ops[i]["eng"]] = end
         out.append(i)
         ready.remove(i)
-        for j in ops[i]["either"]:
-            can[j] = max(can[j], end[i] + (k["own"] if ops[j]["eng"] == e else k["hop"]))
         for j, w in succ[i]:
-            can[j] = max(can[j], end[i] + w)
+            can[j] = max(can[j], end + w)
             left[j] -= 1
             if left[j] == 0:
                 ready.append(j)
-    return max(x + y for x, y in zip(end, late)), out, end
+    return out
 
 
-def search(ops, tries):
-    priced = price(ops, PICTURE)
-    rng, z = np.random.RandomState(0), np.zeros(len(ops))
-    part = np.array([o["part"] for o in ops])
-    best = schedule(ops, priced, z.tolist())
-    for _ in range(tries):
-        y = z.copy()
-        if rng.rand() < 0.3:
-            y[part == rng.randint(part.max() + 1)] += rng.randn() * 1500
+def timer(ops, k):
+    cost, late, pred = price(ops, k)
+    queues, names = sorted(set(o["eng"] for o in ops)), sorted(set(b for o in ops for b in o["banks"]))
+    eng = [queues.index(o["eng"]) for o in ops]
+    banks = [[names.index(b) for b in o["banks"]] for o in ops]
+    hop = k["hop"]
+
+    def time_of(order):
+        end, why, last = [0.0] * len(ops), [-1] * len(ops), [-1] * len(queues)
+        user = [[-1] * len(queues) for _ in names]
+        top, at = 0.0, -1
+        for i in order:
+            e = eng[i]
+            y = last[e]
+            t = end[y] if y >= 0 else 0.0
+            for d, w in pred[i]:
+                if end[d] + w > t:
+                    t, y = end[d] + w, d
+            for b in banks[i]:
+                row = user[b]
+                for e2, d in enumerate(row):
+                    if d >= 0 and e2 != e and end[d] + hop > t:
+                        t, y = end[d] + hop, d
+                row[e] = i
+            end[i], why[i], last[e] = t + cost[i], y, i
+            if end[i] + late[i] > top:
+                top, at = end[i] + late[i], i
+        return top, at, why, end
+    return time_of
+
+
+def improve(ops, order, tries, pictures, temp=80.0, seed=0):
+    rng = np.random.RandomState(seed)
+    timers = [timer(ops, k) for k in pictures]
+    near = [set(o["near"]) for o in ops]
+    now = [t(order) for t in timers]
+    scale = [now[0][0] / x[0] / len(now) for x in now]
+    cur = best = now[0][0]
+    keep = order
+    for n in range(tries):
+        _, at, why, _ = now[n % len(now)]
+        pairs = []
+        while why[at] >= 0:
+            if why[at] not in near[at] and why[at] >= len(LOADS):
+                pairs.append((why[at], at))
+            at = why[at]
+        i, j = pairs[rng.randint(len(pairs))]
+        a, b = order.index(i), order.index(j)
+        mid = order[a:b + 1]
+        if rng.rand() < 0.5:
+            go, todo = {j}, set(near[j])
+            for x in mid[-2::-1]:
+                if x in todo:
+                    go.add(x)
+                    todo |= near[x]
+            new = [x for x in mid if x in go] + [x for x in mid if x not in go]
         else:
-            a, w = rng.randint(len(z)), (1, 3, 10, 30)[rng.randint(4)]
-            y[a:a + w] += rng.randn() * 500
-        t = schedule(ops, priced, y.tolist())
-        if t[0] <= best[0]:
-            best, z = t, y
-    return best
+            go = {i}
+            for x in mid[1:]:
+                if near[x] & go:
+                    go.add(x)
+            new = [x for x in mid if x not in go] + [x for x in mid if x in go]
+        if i in go and j in go:
+            continue
+        cand = order[:a] + new + order[b + 1:]
+        got = [t(cand) for t in timers]
+        s = sum(x[0] * y for x, y in zip(got, scale))
+        if s <= cur or rng.rand() < math.exp((cur - s) / (temp * (1 - n / tries) + 1)):
+            order, now, cur = cand, got, s
+            if s < best:
+                best, keep = s, cand
+    return keep
 
 
 PLAN = {}
@@ -577,13 +635,12 @@ PLAN = {}
 def plan():
     if not PLAN:
         ops = build(PARAMS)
-        best = search(ops, PARAMS["tries"])
-        order = best[1]
+        order = improve(ops, first_order(ops, PICTURE), PARAMS["tries"], PICTURES)
         place = {i: k for k, i in enumerate(order)}
         bank = {}
         for i in order:
             o = ops[i]
-            need = [d for d, x in o["deps"].items() if x] + [d for d in o["either"] if place[d] < place[i]]
+            need = [d for d, x in o["deps"].items() if x]
             for b in o["banks"]:
                 need += [d for e, d in bank.get(b, {}).items() if e != o["eng"]]
                 bank.setdefault(b, {})[o["eng"]] = i
@@ -607,7 +664,7 @@ def plan():
             if i in wanted:
                 total[o["eng"]] = total.get(o["eng"], 0) + 1
             o["tick"] = total.get(o["eng"], 0)
-        PLAN.update(ops=ops, order=order, wanted=wanted, time=best[0])
+        PLAN.update(ops=ops, order=order, wanted=wanted)
     return PLAN
 
 
@@ -635,6 +692,8 @@ def rank_program(g, core, T, topo):
                 sem, val = "c" + b["eng"], b["tick"]
             elif b["eng"] == "N":
                 sem, val = b["sem"][0], came[b["sem"][0][2]]
+            elif b["sem"][0] == "sent":
+                continue
             else:
                 sem, val = b["sem"]
             if known.get((o["eng"], sem), 0) < val:

@@ -13,15 +13,16 @@ C, B, A, D = 0, 1, 2, 3
 
 PARAMS = dict(
     streams=[[([(D, 0)], []), ([(D, 1)], [(C, 0)]), ([(D, 2)], [(B, 1)])],
-             [([(A, 0)], []), ([(A, 1)], []), ([], [(A, 2)])],
-             [([(C, 1), (B, 0)], []), ([(C, 2), (B, 2)], [])]],
+             [([(B, 0), (A, 0)], []), ([(A, 1)], []), ([], [(A, 2)])],
+             [([(C, 1)], []), ([(C, 2), (B, 2)], [])]],
     verdicts=[[A], [C, B], [D]],
-    cut1=((12, 12, 12), (0, 0), (24, 24)), cut2=((8, 8, 8), (0, 0), (16, 16)),
-    scans=(2, 1, 2), vq=("Z", "S", "Z"),
-    reach=4, parts=((192, 384), (0, 192)), tri="pd1", z="pd0", tries=30000,
+    cut1=((12, 8, 8), (28, 0), (0, 28)), cut2=((12, 12, 4), (20, 0), (0, 12)),
+    reach=4, parts=((192, 384), (0, 192)), tri="pd1", z="pd0",
+    rounds=((50000, 1, 150.0), (36000, 3, 25.0), (50000, 3, 20.0)), seed=2,
 )
-PICTURE = dict(c=0.83, p=0.45, hop=220.0, own=160.0, fix=30.0, g=1.5, s=3.8, net=3500.0)
-PICTURES = [PICTURE, dict(PICTURE, c=1.1, p=0.55, hop=180.0, own=130.0, net=4200.0)]
+PICTURE = dict(c=0.83, p=0.45, hop=180.0, own=130.0, fix=30.0, g=1.5, s=3.8, call=700.0, net=3100.0)
+PICTURES = [PICTURE, dict(PICTURE, c=1.1, p=0.55, hop=220.0, own=160.0, call=1000.0, net=4000.0),
+            dict(PICTURE, p=0.36, hop=140.0, own=140.0, fix=45.0, g=1.7, call=450.0, net=2700.0)]
 
 SCRATCH = {
     "win": ("sbuf", [128, WEND], BF16), "endn": ("sbuf", [128, 128], BF16), "wtb": ("sbuf", [128, 16], BF16),
@@ -30,20 +31,21 @@ SCRATCH = {
     "own": ("sbuf", [128, 1024], BF16), "prv": ("sbuf", [128, 768], BF16), "nxt": ("sbuf", [128, 768], BF16),
     "dif": ("sbuf", [128, 144], F32), "gi": ("sbuf", [128, 128], F32), "ai": ("sbuf", [128, 384], F32), "xi": ("sbuf", [128, 384], F32),
     "pi": ("sbuf", [128, 4], I32), "pc": ("sbuf", [128, 16], F32), "w1": ("sbuf", [128, 16], F32), "w2": ("sbuf", [128, 16], F32),
-    "rep": ("sbuf", [128, 8], U16), "zb": ("sbuf", [128, 144], BF16), "tmp": ("sbuf", [128, 768], F32),
-    "cst": ("sbuf", [128, 8, 128], BF16), "fid": ("sbuf", [128, 96], BF16), "r3": ("sbuf", [128, 64], BF16),
+    "rep": ("sbuf", [128, 8], U16), "zb": ("sbuf", [128, 144], BF16), "zc": ("sbuf", [128, 144], BF16), "tmp": ("sbuf", [128, 384], BF16),
+    "cst": ("sbuf", [128, 8, 128], BF16), "r3": ("sbuf", [128, 64], BF16), "r5": ("sbuf", [128, 64], BF16),
     "keep": ("sbuf", [128, 1024], BF16), "rst": ("sbuf", [128, 1024], BF16), "vm": ("sbuf", [128, 224], BF16),
-    "dg0": ("sbuf", [128, 384], F32), "cc": ("sbuf", [128, 384], BF16), "adr": ("sbuf", [128, 128], F32), "pos": ("sbuf", [128, 64], F32),
+    "dg0": ("sbuf", [128, 384], F32), "cc": ("sbuf", [128, 384], BF16),
+    "adr": ("sbuf", [128, 128], F32), "ad4": ("sbuf", [128, 128], F32), "pos": ("sbuf", [128, 64], F32),
     "pl": ("sbuf", [128, 12, 32], I32), "mf": ("sbuf", [128, 12, 32], BF16), "ask": ("sbuf", [128, 12, 32], BF16),
     "vin": ("sbuf", [128, 16, 224], BF16), "mx": ("sbuf", [128, 128], BF16), "d0e": ("sbuf", [128, 256], BF16),
     "ab": ("sbuf", [128, 128], BF16), "bsl": ("sbuf", [128, 128], F32),
     "sp": ("sbuf", [128, 384], F32), "sa": ("sbuf", [128, 384], BF16), "rec": ("sbuf", [128, 384], BF16),
-    "plc": ("sbuf", [128, 384], F32), "pm": ("sbuf", [128, 384], F32), "hold": ("sbuf", [128, 384], F32), "eq": ("sbuf", [128, 2304], BF16),
+    "pm": ("sbuf", [128, 384], F32), "hold": ("sbuf", [128, 384], F32), "eq": ("sbuf", [128, 1536], BF16),
     "drop": ("sbuf", [128, 384], F32), "offf": ("sbuf", [128, 24], F32), "offs": ("sbuf", [128, 24], U16),
     "yeb": ("sbuf", [128, 128], BF16), "yvb": ("sbuf", [128, 384], F32), "ypb": ("sbuf", [128, 1152], F32),
     "p6": ("psum", [128, 512], F32), "p7": ("psum", [128, 512], F32),
 }
-for _n in ("ident", "nid", "nid1", "idh1", "id3", "idq", "idn", "nidn", "blk", "nblkb", "blk2b", "nbigb", "trib", "sel15", "wbd", "wneg", "l3"):
+for _n in ("ident", "nid", "nid1", "id3", "idn", "nidn", "blk", "nblkb", "blk2b", "nbigb", "trib", "cz", "sel15", "wbd", "wneg", "l3"):
     SCRATCH[_n] = ("sbuf", [128, 128], BF16)
 for _n in ("blkf", "nbig", "sel8"):
     SCRATCH[_n] = ("sbuf", [128, 128], F32)
@@ -56,7 +58,7 @@ for _q in range(3):
 
 LOADS = ["l_end", "l_wt", "l_salt", "l_nz", "l_sl", "l_db0", "l_db1"]
 ARRIVALS = ["a_p0"] + ["a_p%d%d" % (m, k) for m in range(1, RU) for k in range(4)] + ["a_n%d" % m for m in range(RU)]
-SEMAPHORES = ["cV", "cS", "cP", "cG", "sent", "stored"] + LOADS + ARRIVALS
+SEMAPHORES = ["cV", "cS", "cP", "cG", "gone", "sent", "stored", "l_nz1"] + LOADS + ARRIVALS
 
 
 def R(name, c0, c1, step=1, part=(0, 128, 1)):
@@ -169,10 +171,16 @@ def build(par):
                    vc(cnt(o), 0.5 if two(o, a, b) else 1))
 
     def act(o, a, func, bias=0.0, scale=1.0):
-        return add("S", lambda q, T, X: q.activation(res(T, o), res(T, a), func, bias=res(T, bias), scale=scale), [a, bias], [o], vc(cnt(o), 1))
+        return add("S", lambda q, T, X: q.activation(res(T, o), res(T, a), func, bias=res(T, bias), scale=res(T, scale)), [a, bias, scale], [o], vc(cnt(o), 1))
 
     def fill(o, val):
         return act(o, R("dif", 0, cnt(o)), AF.Identity, bias=val, scale=0.0)
+
+    def pick(o, a, op, other, step):
+        return add("G", lambda q, T, X: q.affine_select(res(T, o), res(T, a), [[step, cnt(o)]], op, other, 0, -step), [a], [o], ("a", cnt(o)))
+
+    def move(o, a):
+        return pick(o, a, ALU.is_ge, 0.0, 0)
 
     def mm(*parts):
         for k, terms in enumerate(parts):
@@ -181,7 +189,7 @@ def build(par):
                     ins = q.matmul(res(T, o), res(T, l), res(T, r), k == 0 and j == 0, k == len(parts) - 1 and j == len(terms) - 1)
                 return ins
             add("P", fn, [a for t in terms for a in t[1:]], [t[0] for t in terms],
-                ("p", sum(10 + max(64, cnt(r)) * (4 if SCRATCH[r[0]][2] == F32 else 1) for _, _, r in terms)), held=len(parts) > 1)
+                ("p", sum(10 + max(min(64, cnt(l)), cnt(r)) * (4 if SCRATCH[r[0]][2] == F32 else 1) for _, l, r in terms)), held=len(parts) > 1)
 
     def gather(eng, o, w, off):
         if eng == "V":
@@ -197,29 +205,29 @@ def build(par):
             fn = lambda q, T, X: q.iota(res(T, o), pat, base, mult, allow_small_or_imprecise_dtypes=True)
         return add("G", fn, [], [o], ("n", 150 + 2.1 * cnt(o)), after=after)
 
-    def load(eng, sem, o, src, late):
-        return add(eng, lambda q, T, X: q.dma_start(res(T, o), src(T)), [], [o], ("n", 60), sem=(sem, 16), late=late)
+    def load(eng, sem, o, src, late, after=()):
+        return add(eng, lambda q, T, X: q.dma_start(res(T, o), src(T)), [], [o], ("n", 60), sem=(sem, 16), late=late, after=after)
 
     def store(dst, a):
         return add("Y", lambda q, T, X: q.dma_start(dst(T), res(T, a)), [a], [], ("n", 60), sem=("stored", 16), late=2200.0)
 
-    def send(sem, to, o, a):
+    def send(sem, to, o, a, left="sent"):
         def fn(q, T, X):
             rid, pid, mask = X[to]
-            q.remote_dma(res(T, o), res(T, a), T.sem[sem], T.sem.sent, pid, rid, mask)
-        i = add("G", fn, [a], [], ("n", 300), sem=("sent", 0))
+            q.remote_dma(res(T, o), res(T, a), T.sem[sem], T.sem[left], pid, rid, mask)
+        i = add("G", fn, [a], [], ("r", 1), sem=(left, 0))
         add("N", None, [], [o], ("n", 0), sem=(sem, -1), late=-1.0, after=[i])
         return i
 
     M = lambda n: R(n, 0, 128)
     col = lambda k: R("pc", k, k + 1)
+    top = lambda n: (0, n, 1)
     ID, NID, D128 = M("ident"), M("nid"), M("dif")
-    three, eight = (0, 3, 1), (0, 8, 1)
     const = lambda k, n: ("cst", tuple(range(128 * k, 128 * k + n)), (0, 128, 1))
     unit = lambda k, s: 4 * (2 - s) + k
     fresh = {it: ("ga%d" % q, 64 * j + 32 * i) for q, st in enumerate(par["streams"]) for j, jb in enumerate(st) for i, it in enumerate(jb[0])}
-    fresh.update({(k, k): ("fid", 32 * k) for k in (C, B, A)})
     F = lambda k, s: R(fresh[k, s][0], fresh[k, s][1], fresh[k, s][1] + 32)
+    widest = [32 * max(len(jb[0]) for jb in st) for st in par["streams"]]
     vin = lambda units: U("vin", units, 5, 7)
     after = lambda k, s: unit(k, s + 1) if s < ST - 1 else 12 + k
 
@@ -228,22 +236,22 @@ def build(par):
     load("Y", "l_wt", R("wtb", 0, 16), lambda T: T.wt[:], 3000.0)
     load("Y", "l_salt", M("salti"), lambda T: T.salt[:], 3000.0)
     load("Y", "l_db1", R("win", DB + 2048, SP), lambda T: T.db[:, 2048:4096], 6000.0)
-    load("S", "l_nz", R("nzb", 0, 1152), lambda T: T.nz[:], 6500.0)
-    load("Y", "l_sl", R("sli", 0, 384, 1, eight), lambda T: T.sl[:], 6500.0)
-    sent = send("a_p0", "next", R("prv", 0, 128), M("endn"))
+    load("S", "l_nz", R("nzb", 0, 384), lambda T: T.nz[:, 0:384], 6000.0)
+    load("Y", "l_sl", R("sli", 0, 384, 1, top(8)), lambda T: T.sl[:], 6500.0)
+    sent = send("a_p0", "next", R("prv", 0, 128), M("endn"), "gone")
+    load("Y", "l_nz1", R("nzb", 384, 1152), lambda T: T.nz[:, 384:1152], 4000.0, [sent])
 
     iota(R("pi", 0, 1), [[0, 1]], 0, 1)
     iota(R("dif", 0, 144), [[1, 144]], 0, -1)
     iota(M("gi"), [[1, 8], [0, 16]], 0, 0)
-    iota(R("xi", 0, 384), [[1, 384]], 0, 0, [sent])
-    iota(R("ai", 0, 384), [[0, 24], [1, 16]], 0, 0, [sent])
+    iota(R("xi", 0, 64), [[1, 64]], 0, 0)
+    iota(M("ai"), [[0, 8], [1, 16]], 0, 0)
     ts(R("pi", 1, 2), R("pi", 0, 1), 4, None, ALU.arith_shift_right)
     ts(R("pi", 2, 3), R("pi", 0, 1), 15, None, ALU.bitwise_and)
     cp(R("pc", 0, 3), R("pi", 0, 3))
-    for k, val in ((3, 1.0), (4, ONE), (5, -55.0 / 8192), (6, 7.0 / 128), (7, 1.75), (8, -1.0 / 256), (9, -121.0), (13, BIG)):
+    for k, val in ((3, 1.0), (4, ONE), (5, -55.0 / 8192), (6, 7.0 / 128), (7, 1.75), (8, -1.0 / 128), (9, -121.0), (13, BIG)):
         ts(col(k), col(2), 15.0, val, ALU.is_equal, ALU.mult)
     ts(col(10), col(2), 15.0, None, ALU.not_equal)
-    ts(col(11), col(3), 0.5 + 1.0 / 256, 0.5, ALU.mult, ALU.add)
     ts(col(12), col(2), float(GA), None, ALU.add)
     ts(col(14), col(3), ONE + 0.75, -0.75, ALU.mult, ALU.add)
     ts(col(15), col(3), 0.5, 0.5, ALU.mult, ALU.add)
@@ -272,17 +280,13 @@ def build(par):
     act(NID, ID, AF.Copy, scale=-1.0)
     act(M("nbigb"), ID, AF.Copy, scale=-BIG)
     act(M("nbig"), ID, AF.Copy, scale=-BIG)
-    ts(R("tmp", 0, 128), M("blkf"), col(7), None, ALU.mult)
-    tt(M("nid1"), R("tmp", 0, 128), ID, ALU.subtract)
+    for j, (to, k, val) in enumerate((("nid1", 7, -1.0), ("id3", 8, 2.0))):
+        ts(R("tmp", 128 * j, 128 * j + 128), M("blkf"), col(k), None, ALU.mult)
+        pick(M(to), R("tmp", 128 * j, 128 * j + 128), ALU.not_equal, val, 1)
     ts(R("zb", 0, 144), R("dif", 0, 144), 0.0, col(13), ALU.is_equal, ALU.mult)
+    tt(R("zc", 8, 144), R("zb", 8, 144), R("zb", 0, 136), ALU.add)
     ts(M("idn"), D128, 0.0, col(10), ALU.is_equal, ALU.mult)
-    act(M("idq"), M("idn"), AF.Copy, scale=0.25)
     act(M("nidn"), M("idn"), AF.Copy, scale=-1.0)
-    ts(R("tmp", 128, 256), M("blkf"), col(8), None, ALU.mult)
-    ts(R("tmp", 256, 384), D128, 0.0, col(11), ALU.is_equal, ALU.mult)
-    tt(M("idh1"), R("tmp", 128, 256), R("tmp", 256, 384), ALU.add)
-    act(R("tmp", 640, 768), M("idh1"), AF.Copy, scale=2.0)
-    tt(M("id3"), R("tmp", 640, 768), M("idn"), ALU.add)
     ms(R("win", 0, DB), 0.0)
     ms(R("win", SP, WEND), 0.0)
     ms(R("keep", 0, 1024), 1.0)
@@ -292,65 +296,70 @@ def build(par):
     act(R("pos", 0, 64), R("xi", 0, 64), AF.Identity, bias=col(12), scale=16.0)
     fill(R("adr", 0, 128, 2), 1e6)
     act(R("adr", 1, 128, 2), R("xi", 0, 64), AF.Copy)
-    for q, st in enumerate(par["streams"]):
-        na = 32 * len(st[0][0])
+    ms(M("ad4"), -1e6)
+    fill(R("ad4", 0, 128, 4), 1e6)
+    act(R("ad4", 3, 128, 4), R("xi", 0, 32), AF.Copy)
+    for q, na in enumerate(widest):
         ms(R("ga%d" % q, 0, GA), 0.0)
-        act(R("pd%d" % q, 1, 2 * na, 2), R("xi", 0, na), AF.Identity, bias=float(GA + 16 * na))
-        if par["vq"][q] == "Z":
-            for k, val in ((3, col(14)), (4, M1), (5, -M1), (6, 0.0)):
-                fill(R("hl%d" % q, 105 + 16 * k, 112 * na + 105, 112), val)
+        if na > 32 * len(par["streams"][q][0][0]):
+            ms(R("ga%d" % q, GA + 512, GA + 1088), 0.0)
+        if na > 32:
+            act(R("pd%d" % q, 1, 128, 2), R("xi", 0, 64), AF.Identity, bias=float(GA + 16 * na))
+        z = 384 if na > 32 else 0
+        act(R("pd%d" % q, z + 3, z + 128, 4), R("xi", 0, 32), AF.Identity, bias=float(GA + 16 * na))
+        fill(R("pd%d" % q, z + 1, z + 128, 4), 1e6)
+        fill(R("hl%d" % q, 153, 112 * na + 105, 112), col(14))
+        for k, val in ((4, M1), (5, -M1), (6, 0)):
+            iota(R("hl%d" % q, 105 + 16 * k, 112 * na + 105, 112), [[0, na]], int(val), 0, [sent])
+    ts(R("l3", 0, 128, 1, top(5)), R("ai", 0, 128, 1, top(5)), 8.0, 2 * BIG, ALU.is_ge, ALU.mult)
+    ts(R("l3", 0, 128, 1, top(4)), R("ai", 0, 128, 1, top(4)), 8.0, 2 * BIG, ALU.is_lt, ALU.mult)
+    ms(R("l3", 0, 128, 1, top(3)), 136 * BIG)
+    cp(R("l3", 0, 128, 1, top(2)), R("ai", 0, 128, 1, top(2)))
+    ms(R("l3", 0, 128, 1, top(1)), 1.0)
+    for n, pat, base in ((5, [[0, 32], [-16, 2]], 16), (4, [[0, 32], [16, 2]], 0), (3, [[0, 64]], 1), (1, [[16, 32], [0, 2]], GA)):
+        iota(R("r5", 0, 64, 1, top(n)), pat, base, 0, [sent])
+    for n, pat, base in ((3, [[0, 64]], 1), (1, [[16, 64]], GA)):
+        iota(R("r3", 0, 64, 1, top(n)), pat, base, 0, [sent])
     fill(R("d0e", 0, 256, 2), 0.0)
     act(M("blk"), M("blkf"), AF.Copy)
     act(M("nblkb"), M("blkf"), AF.Copy, scale=-BIG)
     act(M("blk2b"), M("blkf"), AF.Copy, scale=2 * BIG)
-    ts(R("tmp", 384, 512), D128, 0.0, -BIG, ALU.is_gt, ALU.mult)
-    tt(R("tmp", 512, 640), R("tmp", 384, 512), M("nbig"), ALU.subtract)
-    tt(M("trib"), R("tmp", 512, 640), M("blkf"), ALU.mult)
-    ms(R("l3", 0, 128, 1, three), 136 * BIG)
-    cp(R("l3", 0, 128, 1, (0, 2, 1)), R("ai", 0, 128, 1, (0, 2, 1)))
-    ms(R("l3", 0, 128, 1, (0, 1, 1)), 1.0)
-    ms(R("r3", 0, 64, 1, three), 1.0)
-    ts(R("r3", 0, 64, 1, (0, 1, 1)), R("xi", 0, 64, 1, (0, 1, 1)), 16.0, float(GA), ALU.mult, ALU.add)
+    pick(R("tmp", 256, 384), M("nblkb"), ALU.is_gt, 0.0, 1)
+    pick(M("trib"), R("tmp", 256, 384), ALU.not_equal, BIG, 1)
     ms(M("sel15"), 0.0)
     cp(R("sel15", 15, 128, 16), R("blkf", 15, 128, 16))
-    ts(R("sel8", 0, 128, 1, eight), R("gi", 0, 128, 1, eight), R("pc", 0, 1, 1, eight), None, ALU.is_equal)
-    cp(R("slf", 0, 384, 1, eight), R("sli", 0, 384, 1, eight))
+    ts(R("sel8", 0, 128, 1, top(8)), R("gi", 0, 128, 1, top(8)), R("pc", 0, 1, 1, top(8)), None, ALU.is_equal)
+    cp(R("slf", 0, 384, 1, top(8)), R("sli", 0, 384, 1, top(8)))
+    iota(R("xi", 64, 384), [[1, 320]], 64, 0, [sent])
+    iota(R("ai", 128, 384), [[0, 16], [1, 16]], 0, 0, [sent])
     ts(R("pm", 0, 384), R("ai", 0, 384), col(2), 4 * BIG, ALU.not_equal, ALU.mult)
-    act(R("drop", 0, 384), R("xi", 0, 384), AF.Identity, bias=4096.0)
-    tt(R("dg0", 0, 384), R("drop", 0, 384), R("pm", 0, 384), ALU.subtract)
+    act(R("p6", 0, 384), R("xi", 0, 384), AF.Identity, bias=4096.0)
+    tt(R("dg0", 0, 384), R("p6", 0, 384), R("pm", 0, 384), ALU.subtract)
     act(R("cc", 0, 384), R("pm", 0, 384), AF.Identity, bias=-3 * BIG, scale=2.0)
+    act(M("cz"), R("pm", 0, 128), AF.Copy, scale=4096.0)
 
     def start(m, k, s):
         return vin([unit(k, s)]) if s else R("prv", 256 * m + 64 * k + 1, 256 * m + 64 * k + 64, 2) if m else R("prv", k, 128, 4)
 
-    def of_v(m, items, P, c0, l):
-        out = [R(P, c0 + 32 * j, c0 + 32 * j + 32) for j in range(len(items))]
+    def of_v(m, items, P, c0, l, w=1):
+        out = [R(P, c0 + 32 * j * w, c0 + 32 * j * w + 31 * w + 1, w) for j in range(len(items))]
         terms = [(o, l, v) for o, v in join(out, [start(m, k, s) for k, s in items])]
         if l is not ID:
             terms += [(o[0], l, const(6, cnt(o[0]))) for o in join([o for o, (k, s) in zip(out, items) if m == 0 and s == 0])]
         return terms
 
-    def fresh_terms(m, items, P, c0, l):
+    def fresh_terms(m, items, P, c0, l, w=1):
         n = 32 * len(items)
-        out = [R(P, c0 + 32 * j, c0 + 32 * j + 32) for j in range(len(items))]
+        out = [R(P, c0 + 32 * j * w, c0 + 32 * j * w + 31 * w + 1, w) for j in range(len(items))]
         nz = [R("nzb", 128 * (m * ST + s) + (k - m) % 4, 128 * (m * ST + s) + 128, 4) for k, s in items]
-        return ([(o, NID, z) for o, z in zip(out, nz)] + of_v(m, items, P, c0, M("nid1"))
-                + [(R(P, c0, c0 + n), ID, const(3, n)), (R(P, c0, c0 + n), ID, const(4, n))]
-                + [(o, ID, z) for o, z in zip(out, nz)] + of_v(m, items, P, c0, l))
-
-    def fresh_of(m, items, P, c0, again=None):
-        mm(fresh_terms(m, items, P, c0, ID))
-        if again:
-            act(again, R(P, c0, c0 + cnt(again)), AF.Copy)
-        for o, a in join([F(k, s) for k, s in items], [R(P, c0 + 32 * j, c0 + 32 * j + 32) for j in range(len(items))]):
-            act(o, a, AF.Copy)
+        return ([(o, NID, z) for o, z in zip(out, nz)] + of_v(m, items, P, c0, M("nid1"), w)
+                + [(R(P, c0, c0 + (n - 1) * w + 1, w), ID, const(k, n)) for k in (3, 4)]
+                + [(o, ID, z) for o, z in zip(out, nz)] + of_v(m, items, P, c0, l, w))
 
     def idle(m, q, k):
         P = "pu%d" % q
         mm(fresh_terms(m, [(k, k)], P, 416, M("id3")) + [(R(P, 416, 448), ID, const(7, 32))])
         act(vin([after(k, k)]), R(P, 416, 448), AF.Identity, bias=-M2 / 2, scale=0.5)
-        if m < RU - 1:
-            fresh_of(m, [(k, k)], P, 384)
 
     def pieces(e, n):
         return [x for x in (("V", 0, e), ("S", e, n)) if x[2] > x[1]]
@@ -358,7 +367,7 @@ def build(par):
     def job(m, q, real, riders):
         items = real + riders
         n, na = 32 * len(items), 32 * len(real)
-        PU, PD = "pu%d" % q, "pd%d" % q
+        PU, PD, over = "pu%d" % q, "pd%d" % q, GA + 16 * widest[q]
         b = lambda name, c0, c1, step=1: R("%s%d" % (name, q), c0, c1, step)
         each = lambda name, its, w=32, c0=0, step=1: [R(name, w * j + c0, w * j + w, step) for j in range(len(its))]
         mm(of_v(m, items, PU, 0, M("wbd")) + [(R(PU, 0, n), ID, const(0, n))])
@@ -382,30 +391,31 @@ def build(par):
                 act(o, x, AF.Identity, bias=136.0)
         if not real:
             return
-        fresh_of(m, real, PU, 128, b("ga", w0 + GA + 16 * na, w0 + GA + 17 * na))
-        E = R(PD, 0, 2 * na, 2)
-        mm([(E, R("l3", 0, 128, 1, three), R("r3", 0, na, 1, three))]
-           + [(o, M("nbigb"), x) for o, x in join(each(PD, real, 64, 0, 2), [U("ask", [unit(k, s)]) for k, s in real])],
-           [(E, R("zb", 15 - p, 143 - p), b("ga", w0 + GA + p, w0 + GA + 16 * na, 16)) for p in range(16)])
-        scan(b("so", 0, 2 * na), R("adr", 0, 2 * na), R(PD, 0, 2 * na), 0.0, ALU.max, ALU.min)
-        cp(b("o2", 0, na), b("so", 1, 2 * na, 2))
-        for o, x, z in join([U("mf", [unit(k, s)]) for k, s in real], each("so%d" % q, real, 64, 1, 2), each("pos", real)):
-            tt(o, x, z, ALU.not_equal)
-        cut = pieces(par["cut2"][q][w0 // 64], na)
-        for eng, a0, a1 in cut:
-            gather(eng, b("gb", 16 * a0, 16 * a1), b("ga", w0, w0 + GA + 17 * na), b("o2", a0, a1))
-        for a0, a1 in [x[1:] for x in cut] if par["scans"][q] == 2 else ((0, na),):
-            scan(b("hl", 112 * a0, 112 * a1, 7), R("keep", 0, 16 * (a1 - a0)), b("gb", 16 * a0, 16 * a1), 0.0, ALU.mult, ALU.max)
-            scan(b("hl", 112 * a0 + 16, 112 * a1 + 16, 7), R("rst", 0, 16 * (a1 - a0)), b("gb", 16 * a0, 16 * a1), 0.0, ALU.max, ALU.min)
-        if par["vq"][q] == "Z":
-            for j, (k, s) in enumerate(real):
-                act(b("hl", 3584 * j + 137, 3584 * (j + 1) + 105, 112), start(m, k, s), AF.Copy)
-                scan(U("vin", [after(k, s)]), R("vm", 0, 224), b("hl", 3584 * j + 105, 3584 * (j + 1) + 105, 16), 0.0, ALU.mult, ALU.add)
+        mm(fresh_terms(m, real, PU, 128, ID))
+        act(b("ga", w0, w0 + na), R(PU, 128, 128 + na), AF.Copy)
+        move(b("ga", w0 + over, w0 + over + na), b("ga", w0, w0 + na))
+        asked = [U("ask", [unit(k, s)]) for k, s in real]
+        if na > 32:
+            E, w = R(PD, 0, 128, 2), 2
+            mm([(E, R("l3", 0, 128, 1, top(3)), R("r3", 0, 64, 1, top(3)))] + [(o, M("nbigb"), x) for o, x in join(each(PD, real, 64, 0, 2), asked)],
+               [(E, R("zb", 15 - p, 143 - p), b("ga", w0 + GA + p, w0 + GA + 1024, 16)) for p in range(16)])
+            scan(b("so", 0, 128), M("adr"), R(PD, 0, 128), 0.0, ALU.max, ALU.min)
         else:
-            P = R(PU, 256, 256 + na)
-            mm(of_v(m, real, PU, 256, M("idh1")) + [(P, M("idq"), b("hl", x, 112 * na + 105, 112)) for x in (105, 121)] + [(P, ID, const(0, na))])
-            for o, a in join([vin([after(k, s)]) for k, s in real], [R(PU, 256 + 32 * j, 288 + 32 * j) for j in range(len(real))]):
-                act(o, a, AF.Identity, bias=-M1)
+            z, w = 384 if widest[q] > 32 else 0, 4
+            E = R(PD, z, z + 128, 2)
+            mm([(E, R("l3", 0, 128, 1, top(5)), R("r5", 0, 64, 1, top(5)))] + [(R(PD, z + h, z + 128, 4), M("nbigb"), asked[0]) for h in (0, 2)],
+               [(E, R("zc", 15 - p, 143 - p), b("ga", w0 + GA + p, w0 + GA + 512, 8)) for p in range(8)])
+            scan(b("so", 0, 128), M("ad4"), R(PD, z, z + 128), 0.0, ALU.max, ALU.min)
+        cp(b("o2", 0, na), b("so", w - 1, 128, w))
+        for o, x, z in join([U("mf", [unit(k, s)]) for k, s in real], each("so%d" % q, real, 32 * w, w - 1, w), each("pos", real)):
+            tt(o, x, z, ALU.not_equal)
+        for eng, a0, a1 in pieces(par["cut2"][q][w0 // 64], na):
+            gather(eng, b("gb", 16 * a0, 16 * a1), b("ga", w0, w0 + over + na), b("o2", a0, a1))
+        scan(b("hl", 0, 112 * na, 7), R("keep", 0, 16 * na), b("gb", 0, 16 * na), 0.0, ALU.mult, ALU.max)
+        scan(b("hl", 16, 112 * na + 16, 7), R("rst", 0, 16 * na), b("gb", 0, 16 * na), 0.0, ALU.max, ALU.min)
+        for j, (k, s) in enumerate(real):
+            move(b("hl", 3584 * j + 137, 3584 * (j + 1) + 105, 112), start(m, k, s))
+            scan(U("vin", [after(k, s)]), R("vm", 0, 224), b("hl", 3584 * j + 105, 3584 * (j + 1) + 105, 16), 0.0, ALU.mult, ALU.add)
 
     def listed(m, k, P, x0):
         return R(P, x0 + (k - m) % 4, x0 + 128, 4)
@@ -417,13 +427,16 @@ def build(par):
         tt(R("sp", x0, x0 + 128), P, U("pl", units), ALU.min)
         if m < RU - 1:
             tt(R("sa", x0, x0 + 128), P, U("ask", units), ALU.min)
-        mm([(R("p6", x0, x0 + 128), ID, const(5, 128))] + [(listed(m, k, "p6", x0), M("blkf"), R("sp", x0 + 32 * k, x0 + 32 * k + 32)) for k in range(4)])
-        act(R("ypb", 384 * m + x0, 384 * m + x0 + 128), R("p6", x0, x0 + 128), AF.Copy)
+        w = 16 if m == RU - 1 else 1
+        rows = top(128 // w)
+        mm([(R("p6", x0, x0 + 128, 1, rows), R("ident", 0, 128, w), const(5, 128))]
+           + [(listed(m, k, "p6", x0)[:2] + (rows,), R("blkf", 0, 128, w), R("sp", x0 + 32 * k, x0 + 32 * k + 32)) for k in range(4)])
+        act(R("ypb", 384 * m + x0, 384 * m + x0 + 128, 1, rows), R("p6", x0, x0 + 128, 1, rows), AF.Copy)
         z = 128 * (m * ST + s)
-        store(lambda T: T.yp[:, z:z + 128], R("ypb", 384 * m + x0, 384 * m + x0 + 128, 1, (0, 128, 16)))
+        store(lambda T: T.yp[:, z:z + 128], R("ypb", 384 * m + x0, 384 * m + x0 + 128, 1, (0, 128 // w, 16 // w)))
         if m < RU - 1:
-            tt(R("plc", x0, x0 + 128), R("p6", x0, x0 + 128), R("cc", x0, x0 + 128), ALU.max)
-            mm([(listed(m, k, "p7", x0), l, x) for k in range(4) for l, x in ((M("idn"), F(k, s)), (M("sel15"), R("sa", x0 + 32 * k, x0 + 32 * k + 32)))])
+            mm(fresh_terms(m, [(s, s)], "p7", x0 + (s - m) % 4, M("idn"), 4) + [(listed(m, k, "p7", x0), M("idn"), F(k, s)) for k in range(4) if k != s],
+               [(listed(m, k, "p7", x0), M("sel15"), R("sa", x0 + 32 * k, x0 + 32 * k + 32)) for k in range(4)])
             act(R("rec", x0, x0 + 128), R("p7", x0, x0 + 128), AF.Identity, bias=col(9))
 
     def bound(m):
@@ -431,9 +444,8 @@ def build(par):
         P = R("p7", 384, 512)
         mm([(P, ID, R("own", c + 1, c + 256, 2)), (P, NID, R("nxt", c + 1, c + 256, 2))])
         act(M("ab"), P, AF.Abs)
-        mm([(P, R("sel8", 0, 128, 1, eight), R("slf", 128 * m, 128 * m + 128, 1, eight))]
-           + [(listed(m, k, "p7", 384), M("blk"), x) for k in range(4)
-              for x in (R("ab", 32 * k, 32 * k + 32), R("nxt", c + 64 * k + 1, c + 64 * k + 64, 2))])
+        mm([(P, M("blk"), M("ab")), (P, M("blk"), R("nxt", c + 1, c + 256, 2))]
+           + [(R("p7", 384 + 32 * k, 416 + 32 * k), R("sel8", 0, 128, 1, top(8)), listed(m, k, "slf", 128 * m)[:2] + (top(8),)) for k in range(4)])
         act(M("bsl"), P, AF.Identity, bias=0.25)
 
     def verdict(m, q, roles):
@@ -443,11 +455,14 @@ def build(par):
         tt(R("mx", 32 * k0, 32 * k0 + n), v, R("nxt", c + 1, c + 2 * n, 2), ALU.max)
         mm([(R(P, 1, 2 * n, 2), M("idn") if last else ID, e)])
         mm([(R(P, 0, 2 * n, 2), M("nidn") if last else NID, e), (R(P, 0, 2 * n, 2), M("idn") if last else ID, v)])
+        Z = R(P, 128, 128 + n)
+        mm([(Z, M("nbig"), R("bsl", 32 * k0, 32 * k0 + n)), (Z, M("nblkb"), v), (Z, M("blk2b"), R("mx", 32 * k0, 32 * k0 + n))])
+        ts(R("d0e", 64 * k0 + 1, 64 * k0 + 2 * n, 2), Z, 0.0, None, ALU.is_le)
         for k in roles:
-            r, Z = (k - m) % 4, listed(m, k, par["z"], 384)
-            mm([(Z, M("nbig"), R("bsl", r, 128, 4)), (Z, M("nblkb"), vin([12 + k])), (Z, M("blk2b"), R("mx", 32 * k, 32 * k + 32))])
-            ts(R("d0e", 64 * k + 1, 64 * k + 64, 2), Z, 0.0, None, ALU.is_le)
-            act(R("yvb", 128 * m + r, 128 * m + 128, 4), R("d0e", 64 * k + 1, 64 * k + 64, 2), AF.Copy)
+            act(listed(m, k, "yvb", 128 * m), R("d0e", 64 * k + 1, 64 * k + 64, 2), AF.Copy)
+            if not last:
+                Z = listed(m, k, par["z"], 384)
+                mm([(Z, ID, listed(m, k, "cz", 0)), (Z, M("nbig"), R("bsl", 32 * k, 32 * k + 32)), (Z, M("nblkb"), vin([12 + k])), (Z, M("blk2b"), R("mx", 32 * k, 32 * k + 32))])
         scan(R("own", to, to + 2 * n), R("d0e", 64 * k0, 64 * k0 + 2 * n), R(P, 0, 2 * n), 0.0, ALU.mult, ALU.add)
         if not last:
             send("a_p%d%d" % (m + 1, k0), "next", R("prv", to, to + 2 * n), R("own", to, to + 2 * n))
@@ -458,7 +473,7 @@ def build(par):
     def commit(m):
         K, w = par["reach"], R("win", 0, WEND)
         for j in (2, 1, 0):
-            tt(R("pm", 128 * j, 128 * j + 128), R(par["z"], 384, 512), R("plc", 128 * j, 128 * j + 128), ALU.max)
+            tt(R("pm", 128 * j, 128 * j + 128), R(par["z"], 384, 512), R("ypb", 384 * m + 128 * j, 384 * m + 128 * j + 128), ALU.max)
         for a, b in par["parts"]:
             scan(R("hold", a, b), R("dg0", a, b), R("pm", a, b), -5.0, ALU.max, ALU.min)
             terms = [(R("p7", a, b), ID, R("cc", a, b))]
@@ -511,7 +526,8 @@ def price(ops, k):
     cost = []
     for o in ops:
         kind, n = o["cost"]
-        cost.append({"v": k["fix"] + n * k["c"], "p": n * k["p"], "g": 65 + n * k["g"] * k["c"], "s": 55 + n * k["s"] * k["c"], "n": n}[kind])
+        cost.append({"v": k["fix"] + n * k["c"], "p": n * k["p"], "g": 65 + n * k["g"] * k["c"], "s": 55 + n * k["s"] * k["c"],
+                     "a": (205 + 2 * n) * k["c"], "r": k["call"], "n": n}[kind])
     late = [k["net"] if o["late"] < 0 else o["late"] for o in ops]
     pred = [[(d, (late[d] + (k["own"] if ops[d]["eng"] == o["eng"] else k["hop"])) if need else 0.0) for d, need in o["near"].items()] for o in ops]
     return cost, late, pred
@@ -560,13 +576,21 @@ def timer(ops, k):
     queues, names = sorted(set(o["eng"] for o in ops)), sorted(set(b for o in ops for b in o["banks"]))
     eng = [queues.index(o["eng"]) for o in ops]
     banks = [[names.index(b) for b in o["banks"]] for o in ops]
-    hop = k["hop"]
+    hop, busy = k["hop"], [queues.index("V"), queues.index("S")]
 
-    def time_of(order):
-        end, why, last = [0.0] * len(ops), [-1] * len(ops), [-1] * len(queues)
-        user = [[-1] * len(queues) for _ in names]
-        top, at = 0.0, -1
-        for i in order:
+    def time_of(order, same=0, old=None, again=0, slack=0.0):
+        if old:
+            end, why, marks = old[3][:], old[2][:], old[4][:same // 32 + 1]
+        else:
+            end, why, marks = [0.0] * len(ops), [-1] * len(ops), [([-1] * len(queues), [[-1] * len(queues) for _ in names], 0.0, -1)]
+        last, user, top, at = marks[-1]
+        last, user = last[:], [row[:] for row in user]
+        for n in range(32 * len(marks) - 32, len(order)):
+            if n == 32 * len(marks):
+                if old and n > again + 64 and min(end[last[v]] - old[3][old[4][len(marks)][0][v]] for v in busy) > slack:
+                    return None
+                marks.append((last[:], [row[:] for row in user], top, at))
+            i = order[n]
             e = eng[i]
             y = last[e]
             t = end[y] if y >= 0 else 0.0
@@ -582,7 +606,7 @@ def timer(ops, k):
             end[i], why[i], last[e] = t + cost[i], y, i
             if end[i] + late[i] > top:
                 top, at = end[i] + late[i], i
-        return top, at, why, end
+        return top, at, why, end, marks
     return time_of
 
 
@@ -593,14 +617,16 @@ def improve(ops, order, tries, pictures, temp=80.0, seed=0):
     now = [t(order) for t in timers]
     scale = [now[0][0] / x[0] / len(now) for x in now]
     cur = best = now[0][0]
-    keep = order
+    keep, pairs = order, None
     for n in range(tries):
-        _, at, why, _ = now[n % len(now)]
-        pairs = []
-        while why[at] >= 0:
-            if why[at] not in near[at] and why[at] >= len(LOADS):
-                pairs.append((why[at], at))
-            at = why[at]
+        if pairs is None:
+            pairs = []
+            for x in now:
+                at, why = x[1:3]
+                while why[at] >= 0:
+                    if why[at] not in near[at] and why[at] >= len(LOADS):
+                        pairs.append((why[at], at))
+                    at = why[at]
         i, j = pairs[rng.randint(len(pairs))]
         a, b = order.index(i), order.index(j)
         mid = order[a:b + 1]
@@ -620,12 +646,18 @@ def improve(ops, order, tries, pictures, temp=80.0, seed=0):
         if i in go and j in go:
             continue
         cand = order[:a] + new + order[b + 1:]
-        got = [t(cand) for t in timers]
-        s = sum(x[0] * y for x, y in zip(got, scale))
-        if s <= cur or rng.rand() < math.exp((cur - s) / (temp * (1 - n / tries) + 1)):
-            order, now, cur = cand, got, s
-            if s < best:
-                best, keep = s, cand
+        slack = -math.log(rng.rand() + 1e-12) * (temp * (1 - n / tries) + 1)
+        got = []
+        for t, x in zip(timers, now):
+            got.append(t(cand, a, x, b, slack * len(now) + 200))
+            if not got[-1]:
+                break
+        else:
+            s = sum(x[0] * y for x, y in zip(got, scale))
+            if s <= cur + slack:
+                order, now, cur, pairs = cand, got, s, None
+                if s < best:
+                    best, keep = s, cand
     return keep
 
 
@@ -635,7 +667,9 @@ PLAN = {}
 def plan():
     if not PLAN:
         ops = build(PARAMS)
-        order = improve(ops, first_order(ops, PICTURE), PARAMS["tries"], PICTURES)
+        order = first_order(ops, PICTURE)
+        for tries, n, heat in PARAMS["rounds"]:
+            order = improve(ops, order, tries, PICTURES[:n], heat, PARAMS["seed"])
         place = {i: k for k, i in enumerate(order)}
         bank = {}
         for i in order:
@@ -692,8 +726,10 @@ def rank_program(g, core, T, topo):
                 sem, val = "c" + b["eng"], b["tick"]
             elif b["eng"] == "N":
                 sem, val = b["sem"][0], came[b["sem"][0][2]]
-            elif b["sem"][0] == "sent":
-                continue
+            elif b["sem"][0] == "gone":
+                if o["eng"] == "G":
+                    continue
+                sem, val = "gone", went["p"]
             else:
                 sem, val = b["sem"]
             if known.get((o["eng"], sem), 0) < val:
@@ -704,5 +740,5 @@ def rank_program(g, core, T, topo):
             ins.then_inc(T.sem["c" + o["eng"]], 1)
         elif o["sem"] is not None and o["sem"][1] == 16:
             ins.then_inc(T.sem[o["sem"][0]], 16)
-    g.wait_ge(T.sem.sent, sum(went[o["sem"][0][2]] for o in ops if o["eng"] == "N"))
+    g.wait_ge(T.sem.sent, sum(went[o["sem"][0][2]] for o in ops if o["eng"] == "N") - went["p"])
     g.sync.wait_ge(T.sem.stored, sum(16 for o in ops if o["sem"] == ("stored", 16)))

import math
import numpy as np
from concourse.mybir import AluOpType as ALU, ActivationFunctionType as AF

F32, BF16, I32, U16 = "float32", "bfloat16", "int32", "uint16"
RU, ST = 3, 3
M1, M2, M8, M256 = 1.5 * 2 ** 23, 1.5 * 2 ** 24, 1.5 * 2 ** 26, 1.5 * 2 ** 31
BIG = 8192.0
ONE = 73.0
DB, SP, WEND = 16, 4112, 4496
GA = 192
C, B, A, D = 0, 1, 2, 3

PARAMS = dict(
    streams=[[([(D, 0)], []), ([(D, 1)], [(C, 0)]), ([(D, 2)], [(B, 1)])],
             [([(B, 0), (A, 0)], []), ([(A, 1)], []), ([], [(A, 2)])],
             [([(C, 1)], []), ([(C, 2), (B, 2)], [])]],
    verdicts=[[A], [C, B], [D]],
    cut1=((12, 8, 8), (28, 0), (0, 28)), cut2=((12, 12, 4), (20, 0), (0, 12)),
    reach=4, parts=((192, 384), (0, 192)), tri="pd1", z="pd0",
    rounds=((50000, 1, 150.0), (36000, 3, 25.0), (50000, 3, 20.0)), seed=2,
)
PICTURE = dict(c=0.83, p=0.45, hop=180.0, own=130.0, fix=30.0, g=1.5, s=3.8, call=700.0, net=3100.0)
PICTURES = [PICTURE, dict(PICTURE, c=1.1, p=0.55, hop=220.0, own=160.0, call=1000.0, net=4000.0),
            dict(PICTURE, p=0.36, hop=140.0, own=140.0, fix=45.0, g=1.7, call=450.0, net=2700.0)]

SCRATCH = {
    "win": ("sbuf", [128, WEND], BF16), "endn": ("sbuf", [128, 128], BF16), "wtb": ("sbuf", [128, 16], BF16),
    "salti": ("sbuf", [128, 128], I32), "nzb": ("sbuf", [128, 1152], BF16), "sli": ("sbuf", [128, 384], I32),
    "slf": ("sbuf", [128, 384], F32), "saltf": ("sbuf", [128, 4, 32], F32), "salt8": ("sbuf", [128, 21, 32], F32),
    "own": ("sbuf", [128, 1024], BF16), "prv": ("sbuf", [128, 768], BF16), "nxt": ("sbuf", [128, 768], BF16),
    "dif": ("sbuf", [128, 144], F32), "gi": ("sbuf", [128, 128], F32), "ai": ("sbuf", [128, 384], F32), "xi": ("sbuf", [128, 384], F32),
    "pi": ("sbuf", [128, 4], I32), "pc": ("sbuf", [128, 16], F32), "w1": ("sbuf", [128, 16], F32), "w2": ("sbuf", [128, 16], F32),
    "rep": ("sbuf", [128, 8], U16), "zb": ("sbuf", [128, 144], BF16), "zc": ("sbuf", [128, 144], BF16), "tmp": ("sbuf", [128, 384], BF16),
    "cst": ("sbuf", [128, 8, 128], BF16), "r3": ("sbuf", [128, 64], BF16), "r5": ("sbuf", [128, 64], BF16),
    "keep": ("sbuf", [128, 1024], BF16), "rst": ("sbuf", [128, 1024], BF16), "vm": ("sbuf", [128, 224], BF16),
    "dg0": ("sbuf", [128, 384], F32), "cc": ("sbuf", [128, 384], BF16),
    "adr": ("sbuf", [128, 128], F32), "ad4": ("sbuf", [128, 128], F32), "pos": ("sbuf", [128, 64], F32),
    "pl": ("sbuf", [128, 12, 32], I32), "mf": ("sbuf", [128, 12, 32], BF16), "ask": ("sbuf", [128, 12, 32], BF16),
    "vin": ("sbuf", [128, 16, 224], BF16), "mx": ("sbuf", [128, 128], BF16), "d0e": ("sbuf", [128, 256], BF16),
    "ab": ("sbuf", [128, 128], BF16), "bsl": ("sbuf", [128, 128], F32),
    "sp": ("sbuf", [128, 384], F32), "sa": ("sbuf", [128, 384], BF16), "rec": ("sbuf", [128, 384], BF16),
    "pm": ("sbuf", [128, 384], F32), "hold": ("sbuf", [128, 384], F32), "eq": ("sbuf", [128, 1536], BF16),
    "drop": ("sbuf", [128, 384], F32), "offf": ("sbuf", [128, 24], F32), "offs": ("sbuf", [128, 24], U16),
    "yeb": ("sbuf", [128, 128], BF16), "yvb": ("sbuf", [128, 384], F32), "ypb": ("sbuf", [128, 1152], F32),
    "p6": ("psum", [128, 512], F32), "p7": ("psum", [128, 512], F32),
}
for _n in ("ident", "nid", "nid1", "id3", "idn", "nidn", "blk", "nblkb", "blk2b", "nbigb", "trib", "cz", "sel15", "wbd", "wneg", "l3"):
    SCRATCH[_n] = ("sbuf", [128, 128], BF16)
for _n in ("blkf", "nbig", "sel8"):
    SCRATCH[_n] = ("sbuf", [128, 128], F32)
for _q in range(3):
    for _n, _w, _d in (("y", 128, I32), ("o1", 128, U16), ("o2", 128, U16), ("so", 128, F32),
                       ("ga", 1408, BF16), ("gb", 1024, BF16), ("hl", 7376, BF16)):
        SCRATCH["%s%d" % (_n, _q)] = ("sbuf", [128, _w], _d)
    for _n in ("pu", "pd"):
        SCRATCH["%s%d" % (_n, _q)] = ("psum", [128, 512], F32)

LOADS = ["l_end", "l_wt", "l_salt", "l_nz", "l_sl", "l_db0", "l_db1"]
ARRIVALS = ["a_p0"] + ["a_p%d%d" % (m, k) for m in range(1, RU) for k in range(4)] + ["a_n%d" % m for m in range(RU)]
SEMAPHORES = ["cV", "cS", "cP", "cG", "gone", "sent", "stored", "l_nz1"] + LOADS + ARRIVALS


def R(name, c0, c1, step=1, part=(0, 128, 1)):
    return (name, tuple(range(c0, c1, step)), part)


def U(name, units, c0=0, step=1):
    w = SCRATCH[name][1][2]
    return (name, tuple(u * w + c for u in units for c in range(c0, w, step)), (0, 128, 1))


def run_of(x):
    step = x[1] - x[0] if len(x) > 1 else 1
    return slice(x[0], x[-1] + 1, step) if step > 0 and list(x) == list(range(x[0], x[-1] + 1, step)) else None


def index(a):
    shape, part = SCRATCH[a[0]][1], slice(*a[2])
    if len(shape) == 2:
        s = run_of(a[1])
        return None if s is None else (part, s)
    units = sorted(set(c // shape[2] for c in a[1]))
    inner = [c % shape[2] for c in a[1] if c // shape[2] == units[0]]
    if tuple(u * shape[2] + c for u in units for c in inner) != a[1] or run_of(units) is None or run_of(inner) is None:
        return None
    return (part, units[0] if len(units) == 1 else run_of(units), run_of(inner))


def join(*rows):
    out = []
    for item in zip(*rows):
        if out:
            both = [(a[0], a[1] + b[1], a[2]) if a[0] == b[0] else None for a, b in zip(out[-1], item)]
            if all(x is not None and index(x) is not None for x in both):
                out[-1] = both
                continue
        out.append(list(item))
    return out


def res(T, a):
    return T[a[0]][index(a)] if isinstance(a, tuple) else a


def cnt(a):
    return len(a[1])


def two(*aps):
    return all(SCRATCH[a[0]][2] in (BF16, U16) for a in aps)


def psum(a):
    return SCRATCH[a[0]][0] == "psum"


def bits(a, exact=True):
    if exact:
        return sum(1 << c for c in a[1])
    return (1 << (max(a[1]) // 8 * 8 + 8)) - (1 << (min(a[1]) // 8 * 8))


def build(par):
    ops, seen = [], {}

    def add(eng, fn, reads, writes, cost, sem=None, late=0.0, after=(), held=False):
        i = len(ops)
        deps = {d: True for d in after}
        uses = [(a, False) for a in reads if isinstance(a, tuple)] + [(a, True) for a in writes]
        mine = []
        for a, wr in uses:
            e, w = bits(a), bits(a, False)
            for j, be, bw, bwr in seen.get(a[0], []):
                o = ops[j]
                if eng == "P" and o["eng"] == "P" and psum(a):
                    if held or o["held"] or e & be:
                        deps.setdefault(j, False)
                elif (wr or bwr) and ((w & bw) if sem is not None or o["sem"] is not None else (e & be)):
                    deps[j] = True
            mine.append((a[0], (i, e, w, wr)))
        for n, x in mine:
            seen.setdefault(n, []).append(x)
        ops.append(dict(eng=eng, fn=fn, deps=deps, cost=cost, sem=sem, late=late, held=held,
                        tag=(writes or reads)[0][0] + str((writes or reads)[0][1][0]),
                        banks=sorted(set(a[0] for a, _ in uses if psum(a)))))
        return i

    def vc(n, rate):
        return ("v", max(64.0, n * rate))

    def ts(o, a, s1, s2, op0, op1=None):
        if op1 is None:
            fn = lambda q, T, X: q.tensor_scalar(res(T, o), res(T, a), res(T, s1), None, op0)
        else:
            fn = lambda q, T, X: q.tensor_scalar(res(T, o), res(T, a), res(T, s1), res(T, s2), op0, op1)
        return add("V", fn, [a, s1, s2], [o], vc(cnt(o), 0.5 if two(o, a) else 1))

    def tt(o, a, b, op):
        return add("V", lambda q, T, X: q.tensor_tensor(res(T, o), res(T, a), res(T, b), op), [a, b], [o],
                   vc(cnt(o), 1 if psum(a) or psum(b) else 2))

    def cp(o, a):
        return add("V", lambda q, T, X: q.tensor_copy(res(T, o), res(T, a)), [a], [o], vc(cnt(o), 0.5 if two(o, a) else 1))

    def ms(o, val):
        return add("V", lambda q, T, X: q.memset(res(T, o), val), [], [o], vc(cnt(o), 0.5 if two(o) else 1))

    def scan(o, a, b, init, op0, op1):
        return add("V", lambda q, T, X: q.tensor_tensor_scan(res(T, o), res(T, a), res(T, b), init, op0, op1), [a, b], [o],
                   vc(cnt(o), 0.5 if two(o, a, b) else 1))

    def act(o, a, func, bias=0.0, scale=1.0):
        return add("S", lambda q, T, X: q.activation(res(T, o), res(T, a), func, bias=res(T, bias), scale=res(T, scale)), [a, bias, scale], [o], vc(cnt(o), 1))

    def fill(o, val):
        return act(o, R("dif", 0, cnt(o)), AF.Identity, bias=val, scale=0.0)

    def pick(o, a, op, other, step):
        return add("G", lambda q, T, X: q.affine_select(res(T, o), res(T, a), [[step, cnt(o)]], op, other, 0, -step), [a], [o], ("a", cnt(o)))

    def move(o, a):
        return pick(o, a, ALU.is_ge, 0.0, 0)

    def mm(*parts):
        for k, terms in enumerate(parts):
            def fn(q, T, X, terms=terms, k=k):
                for j, (o, l, r) in enumerate(terms):
                    ins = q.matmul(res(T, o), res(T, l), res(T, r), k == 0 and j == 0, k == len(parts) - 1 and j == len(terms) - 1)
                return ins
            add("P", fn, [a for t in terms for a in t[1:]], [t[0] for t in terms],
                ("p", sum(10 + max(min(64, cnt(l)), cnt(r)) * (4 if SCRATCH[r[0]][2] == F32 else 1) for _, l, r in terms)), held=len(parts) > 1)

    def gather(eng, o, w, off):
        if eng == "V":
            fn = lambda q, T, X: q.tensor_copy(res(T, o), res(T, w).indirect(res(T, off)))
        else:
            fn = lambda q, T, X: q.activation(res(T, o), res(T, w).indirect(res(T, off)), AF.Copy)
        return add(eng, fn, [w, off], [o], ("g", cnt(o)))

    def iota(o, pat, base, mult, after=()):
        if SCRATCH[o[0]][2] == I32:
            fn = lambda q, T, X: q.iota(res(T, o), pat, base, mult)
        else:
            fn = lambda q, T, X: q.iota(res(T, o), pat, base, mult, allow_small_or_imprecise_dtypes=True)
        return add("G", fn, [], [o], ("n", 150 + 2.1 * cnt(o)), after=after)

    def load(eng, sem, o, src, late, after=()):
        return add(eng, lambda q, T, X: q.dma_start(res(T, o), src(T)), [], [o], ("n", 60), sem=(sem, 16), late=late, after=after)

    def store(dst, a):
        return add("Y", lambda q, T, X: q.dma_start(dst(T), res(T, a)), [a], [], ("n", 60), sem=("stored", 16), late=2200.0)

    def send(sem, to, o, a, left="sent"):
        def fn(q, T, X):
            rid, pid, mask = X[to]
            q.remote_dma(res(T, o), res(T, a), T.sem[sem], T.sem[left], pid, rid, mask)
        i = add("G", fn, [a], [], ("r", 1), sem=(left, 0))
        add("N", None, [], [o], ("n", 0), sem=(sem, -1), late=-1.0, after=[i])
        return i

    M = lambda n: R(n, 0, 128)
    col = lambda k: R("pc", k, k + 1)
    top = lambda n: (0, n, 1)
    ID, NID, D128 = M("ident"), M("nid"), M("dif")
    const = lambda k, n: ("cst", tuple(range(128 * k, 128 * k + n)), (0, 128, 1))
    unit = lambda k, s: 4 * (2 - s) + k
    fresh = {it: ("ga%d" % q, 64 * j + 32 * i) for q, st in enumerate(par["streams"]) for j, jb in enumerate(st) for i, it in enumerate(jb[0])}
    F = lambda k, s: R(fresh[k, s][0], fresh[k, s][1], fresh[k, s][1] + 32)
    widest = [32 * max(len(jb[0]) for jb in st) for st in par["streams"]]
    vin = lambda units: U("vin", units, 5, 7)
    after = lambda k, s: unit(k, s + 1) if s < ST - 1 else 12 + k

    load("Y", "l_end", M("endn"), lambda T: T.ends[:], 2200.0)
    load("S", "l_db0", R("win", DB, DB + 2048), lambda T: T.db[:, 0:2048], 6000.0)
    load("Y", "l_wt", R("wtb", 0, 16), lambda T: T.wt[:], 3000.0)
    load("Y", "l_salt", M("salti"), lambda T: T.salt[:], 3000.0)
    load("Y", "l_db1", R("win", DB + 2048, SP), lambda T: T.db[:, 2048:4096], 6000.0)
    load("S", "l_nz", R("nzb", 0, 384), lambda T: T.nz[:, 0:384], 6000.0)
    load("Y", "l_sl", R("sli", 0, 384, 1, top(8)), lambda T: T.sl[:], 6500.0)
    sent = send("a_p0", "next", R("prv", 0, 128), M("endn"), "gone")
    load("Y", "l_nz1", R("nzb", 384, 1152), lambda T: T.nz[:, 384:1152], 4000.0, [sent])

    iota(R("pi", 0, 1), [[0, 1]], 0, 1)
    iota(R("dif", 0, 144), [[1, 144]], 0, -1)
    iota(M("gi"), [[1, 8], [0, 16]], 0, 0)
    iota(R("xi", 0, 64), [[1, 64]], 0, 0)
    iota(M("ai"), [[0, 8], [1, 16]], 0, 0)
    ts(R("pi", 1, 2), R("pi", 0, 1), 4, None, ALU.arith_shift_right)
    ts(R("pi", 2, 3), R("pi", 0, 1), 15, None, ALU.bitwise_and)
    cp(R("pc", 0, 3), R("pi", 0, 3))
    for k, val in ((3, 1.0), (4, ONE), (5, -55.0 / 8192), (6, 7.0 / 128), (7, 1.75), (8, -1.0 / 128), (9, -121.0), (13, BIG)):
        ts(col(k), col(2), 15.0, val, ALU.is_equal, ALU.mult)
    ts(col(10), col(2), 15.0, None, ALU.not_equal)
    ts(col(12), col(2), float(GA), None, ALU.add)
    ts(col(14), col(3), ONE + 0.75, -0.75, ALU.mult, ALU.add)
    ts(col(15), col(3), 0.5, 0.5, ALU.mult, ALU.add)
    ms(R("vm", 0, 224), 1.0)
    for k, val in ((0, 0.0), (2, 0.5), (3, col(10)), (4, col(15))):
        fill(R("vm", k, 224, 7), val)
    fill(R("own", 0, 256, 2), 0.0)
    for k in range(4):
        act(R("own", 64 * k + 1, 64 * k + 64, 2), R("endn", k, 128, 4), AF.Identity, bias=col(4))
    send("a_n0", "prev", R("nxt", 0, 256), R("own", 0, 256))
    ts(ID, D128, 0.0, None, ALU.is_equal)
    ts(M("blkf"), M("gi"), col(1), None, ALU.is_equal)
    ts(R("rep", 0, 8), R("gi", 0, 8), col(2), None, ALU.add)
    for w, to, sign, k in (("w1", "wbd", 1.0, 5), ("w2", "wneg", -1.0, 6)):
        ts(R(w, 0, 16), R("wtb", 0, 16), sign / 64, col(k), ALU.mult, ALU.add)
        add("V", lambda q, T, X, w=w, to=to: q.tensor_tensor(T[to][:], T[w][:].indirect(T["rep"][:]), T["blkf"][:], ALU.mult),
            [R(w, 0, 16), R("rep", 0, 8), M("blkf")], [M(to)], ("g", 128))
    for k, val in ((0, M1), (1, M8), (2, -M8), (3, M256), (4, -M256), (5, 15.0), (7, M2)):
        ms(const(k, 128), val)
    fill(const(6, 128), col(4))
    for r in range(4):
        cp(U("saltf", [r]), R("salti", r, 128, 4))
    for s in range(ST):
        for a, n in ((14, 4), (18, 3)):
            act(U("salt8", range(a - 7 * s, a + n - 7 * s)), U("saltf", range(n)), AF.Identity, bias=8.0 * 211 * s - 148.0 ** 2, scale=8.0)
    act(NID, ID, AF.Copy, scale=-1.0)
    act(M("nbigb"), ID, AF.Copy, scale=-BIG)
    act(M("nbig"), ID, AF.Copy, scale=-BIG)
    for j, (to, k, val) in enumerate((("nid1", 7, -1.0), ("id3", 8, 2.0))):
        ts(R("tmp", 128 * j, 128 * j + 128), M("blkf"), col(k), None, ALU.mult)
        pick(M(to), R("tmp", 128 * j, 128 * j + 128), ALU.not_equal, val, 1)
    ts(R("zb", 0, 144), R("dif", 0, 144), 0.0, col(13), ALU.is_equal, ALU.mult)
    tt(R("zc", 8, 144), R("zb", 8, 144), R("zb", 0, 136), ALU.add)
    ts(M("idn"), D128, 0.0, col(10), ALU.is_equal, ALU.mult)
    act(M("nidn"), M("idn"), AF.Copy, scale=-1.0)
    ms(R("win", 0, DB), 0.0)
    ms(R("win", SP, WEND), 0.0)
    ms(R("keep", 0, 1024), 1.0)
    ms(R("keep", 0, 1024, 16), 0.0)
    act(R("rst", 0, 1024), R("keep", 0, 1024), AF.Identity, bias=255.0, scale=-255.0)
    fill(U("mf", (2, 5, 8)), 1.0)
    act(R("pos", 0, 64), R("xi", 0, 64), AF.Identity, bias=col(12), scale=16.0)
    fill(R("adr", 0, 128, 2), 1e6)
    act(R("adr", 1, 128, 2), R("xi", 0, 64), AF.Copy)
    ms(M("ad4"), -1e6)
    fill(R("ad4", 0, 128, 4), 1e6)
    act(R("ad4", 3, 128, 4), R("xi", 0, 32), AF.Copy)
    for q, na in enumerate(widest):
        ms(R("ga%d" % q, 0, GA), 0.0)
        if na > 32 * len(par["streams"][q][0][0]):
            ms(R("ga%d" % q, GA + 512, GA + 1088), 0.0)
        if na > 32:
            act(R("pd%d" % q, 1, 128, 2), R("xi", 0, 64), AF.Identity, bias=float(GA + 16 * na))
        z = 384 if na > 32 else 0
        act(R("pd%d" % q, z + 3, z + 128, 4), R("xi", 0, 32), AF.Identity, bias=float(GA + 16 * na))
        fill(R("pd%d" % q, z + 1, z + 128, 4), 1e6)
        fill(R("hl%d" % q, 153, 112 * na + 105, 112), col(14))
        for k, val in ((4, M1), (5, -M1), (6, 0)):
            iota(R("hl%d" % q, 105 + 16 * k, 112 * na + 105, 112), [[0, na]], int(val), 0, [sent])
    ts(R("l3", 0, 128, 1, top(5)), R("ai", 0, 128, 1, top(5)), 8.0, 2 * BIG, ALU.is_ge, ALU.mult)
    ts(R("l3", 0, 128, 1, top(4)), R("ai", 0, 128, 1, top(4)), 8.0, 2 * BIG, ALU.is_lt, ALU.mult)
    ms(R("l3", 0, 128, 1, top(3)), 136 * BIG)
    cp(R("l3", 0, 128, 1, top(2)), R("ai", 0, 128, 1, top(2)))
    ms(R("l3", 0, 128, 1, top(1)), 1.0)
    for n, pat, base in ((5, [[0, 32], [-16, 2]], 16), (4, [[0, 32], [16, 2]], 0), (3, [[0, 64]], 1), (1, [[16, 32], [0, 2]], GA)):
        iota(R("r5", 0, 64, 1, top(n)), pat, base, 0, [sent])
    for n, pat, base in ((3, [[0, 64]], 1), (1, [[16, 64]], GA)):
        iota(R("r3", 0, 64, 1, top(n)), pat, base, 0, [sent])
    fill(R("d0e", 0, 256, 2), 0.0)
    act(M("blk"), M("blkf"), AF.Copy)
    act(M("nblkb"), M("blkf"), AF.Copy, scale=-BIG)
    act(M("blk2b"), M("blkf"), AF.Copy, scale=2 * BIG)
    pick(R("tmp", 256, 384), M("nblkb"), ALU.is_gt, 0.0, 1)
    pick(M("trib"), R("tmp", 256, 384), ALU.not_equal, BIG, 1)
    ms(M("sel15"), 0.0)
    cp(R("sel15", 15, 128, 16), R("blkf", 15, 128, 16))
    ts(R("sel8", 0, 128, 1, top(8)), R("gi", 0, 128, 1, top(8)), R("pc", 0, 1, 1, top(8)), None, ALU.is_equal)
    cp(R("slf", 0, 384, 1, top(8)), R("sli", 0, 384, 1, top(8)))
    iota(R("xi", 64, 384), [[1, 320]], 64, 0, [sent])
    iota(R("ai", 128, 384), [[0, 16], [1, 16]], 0, 0, [sent])
    ts(R("pm", 0, 384), R("ai", 0, 384), col(2), 4 * BIG, ALU.not_equal, ALU.mult)
    act(R("p6", 0, 384), R("xi", 0, 384), AF.Identity, bias=4096.0)
    tt(R("dg0", 0, 384), R("p6", 0, 384), R("pm", 0, 384), ALU.subtract)
    act(R("cc", 0, 384), R("pm", 0, 384), AF.Identity, bias=-3 * BIG, scale=2.0)
    act(M("cz"), R("pm", 0, 128), AF.Copy, scale=4096.0)

    def start(m, k, s):
        return vin([unit(k, s)]) if s else R("prv", 256 * m + 64 * k + 1, 256 * m + 64 * k + 64, 2) if m else R("prv", k, 128, 4)

    def of_v(m, items, P, c0, l, w=1):
        out = [R(P, c0 + 32 * j * w, c0 + 32 * j * w + 31 * w + 1, w) for j in range(len(items))]
        terms = [(o, l, v) for o, v in join(out, [start(m, k, s) for k, s in items])]
        if l is not ID:
            terms += [(o[0], l, const(6, cnt(o[0]))) for o in join([o for o, (k, s) in zip(out, items) if m == 0 and s == 0])]
        return terms

    def fresh_terms(m, items, P, c0, l, w=1):
        n = 32 * len(items)
        out = [R(P, c0 + 32 * j * w, c0 + 32 * j * w + 31 * w + 1, w) for j in range(len(items))]
        nz = [R("nzb", 128 * (m * ST + s) + (k - m) % 4, 128 * (m * ST + s) + 128, 4) for k, s in items]
        return ([(o, NID, z) for o, z in zip(out, nz)] + of_v(m, items, P, c0, M("nid1"), w)
                + [(R(P, c0, c0 + (n - 1) * w + 1, w), ID, const(k, n)) for k in (3, 4)]
                + [(o, ID, z) for o, z in zip(out, nz)] + of_v(m, items, P, c0, l, w))

    def idle(m, q, k):
        P = "pu%d" % q
        mm(fresh_terms(m, [(k, k)], P, 416, M("id3")) + [(R(P, 416, 448), ID, const(7, 32))])
        act(vin([after(k, k)]), R(P, 416, 448), AF.Identity, bias=-M2 / 2, scale=0.5)

    def pieces(e, n):
        return [x for x in (("V", 0, e), ("S", e, n)) if x[2] > x[1]]

    def job(m, q, real, riders):
        items = real + riders
        n, na = 32 * len(items), 32 * len(real)
        PU, PD, over = "pu%d" % q, "pd%d" % q, GA + 16 * widest[q]
        b = lambda name, c0, c1, step=1: R("%s%d" % (name, q), c0, c1, step)
        each = lambda name, its, w=32, c0=0, step=1: [R(name, w * j + c0, w * j + w, step) for j in range(len(its))]
        mm(of_v(m, items, PU, 0, M("wbd")) + [(R(PU, 0, n), ID, const(0, n))])
        act(R(PU, 0, n), R(PU, 0, n), AF.Square, bias=148.0 - M1)
        for o, x, z in join(each("y%d" % q, items), each(PU, items), [U("salt8", [14 - 7 * s + (-m) % 4 + k]) for k, s in items]):
            tt(o, x, z, ALU.add)
        for o, x in join([U("pl", [unit(k, s)]) for k, s in items], each("y%d" % q, items)):
            ts(o, x, 3, 4095, ALU.arith_shift_right, ALU.bitwise_and)
        if real:
            w0 = fresh[real[0]][1]
            for o, x in join(each("o1%d" % q, real), [U("pl", [unit(k, s)]) for k, s in real]):
                cp(o, x)
            for eng, a0, a1 in pieces(par["cut1"][q][w0 // 64], na):
                gather(eng, b("ga", w0 + GA + 16 * a0, w0 + GA + 16 * a1), R("win", DB, SP), b("o1", a0, a1))
        its = items if m < RU - 1 else real
        if its:
            w = 32 * len(its)
            mm(of_v(m, its, PD, 128, M("wneg")) + [(R(PD, 128, 128 + w), ID, const(1, w)), (R(PD, 128, 128 + w), ID, const(2, w))]
               + of_v(m, its, PD, 128, M("wbd")))
            for o, x in join([U("ask", [unit(k, s)]) for k, s in its], [R(PD, 128 + 32 * j, 160 + 32 * j) for j in range(len(its))]):
                act(o, x, AF.Identity, bias=136.0)
        if not real:
            return
        mm(fresh_terms(m, real, PU, 128, ID))
        act(b("ga", w0, w0 + na), R(PU, 128, 128 + na), AF.Copy)
        move(b("ga", w0 + over, w0 + over + na), b("ga", w0, w0 + na))
        asked = [U("ask", [unit(k, s)]) for k, s in real]
        if na > 32:
            E, w = R(PD, 0, 128, 2), 2
            mm([(E, R("l3", 0, 128, 1, top(3)), R("r3", 0, 64, 1, top(3)))] + [(o, M("nbigb"), x) for o, x in join(each(PD, real, 64, 0, 2), asked)],
               [(E, R("zb", 15 - p, 143 - p), b("ga", w0 + GA + p, w0 + GA + 1024, 16)) for p in range(16)])
            scan(b("so", 0, 128), M("adr"), R(PD, 0, 128), 0.0, ALU.max, ALU.min)
        else:
            z, w = 384 if widest[q] > 32 else 0, 4
            E = R(PD, z, z + 128, 2)
            mm([(E, R("l3", 0, 128, 1, top(5)), R("r5", 0, 64, 1, top(5)))] + [(R(PD, z + h, z + 128, 4), M("nbigb"), asked[0]) for h in (0, 2)],
               [(E, R("zc", 15 - p, 143 - p), b("ga", w0 + GA + p, w0 + GA + 512, 8)) for p in range(8)])
            scan(b("so", 0, 128), M("ad4"), R(PD, z, z + 128), 0.0, ALU.max, ALU.min)
        cp(b("o2", 0, na), b("so", w - 1, 128, w))
        for o, x, z in join([U("mf", [unit(k, s)]) for k, s in real], each("so%d" % q, real, 32 * w, w - 1, w), each("pos", real)):
            tt(o, x, z, ALU.not_equal)
        for eng, a0, a1 in pieces(par["cut2"][q][w0 // 64], na):
            gather(eng, b("gb", 16 * a0, 16 * a1), b("ga", w0, w0 + over + na), b("o2", a0, a1))
        scan(b("hl", 0, 112 * na, 7), R("keep", 0, 16 * na), b("gb", 0, 16 * na), 0.0, ALU.mult, ALU.max)
        scan(b("hl", 16, 112 * na + 16, 7), R("rst", 0, 16 * na), b("gb", 0, 16 * na), 0.0, ALU.max, ALU.min)
        for j, (k, s) in enumerate(real):
            move(b("hl", 3584 * j + 137, 3584 * (j + 1) + 105, 112), start(m, k, s))
            scan(U("vin", [after(k, s)]), R("vm", 0, 224), b("hl", 3584 * j + 105, 3584 * (j + 1) + 105, 16), 0.0, ALU.mult, ALU.add)

    def listed(m, k, P, x0):
        return R(P, x0 + (k - m) % 4, x0 + 128, 4)

    def shadow(m, s):
        units, x0, P = range(8 - 4 * s, 12 - 4 * s), 128 * (2 - s), R(par["tri"], 256, 384)
        mm([(P, M("trib"), U("mf", units))])
        ts(P, P, -1.0, -1.0, ALU.add, ALU.max)
        tt(R("sp", x0, x0 + 128), P, U("pl", units), ALU.min)
        if m < RU - 1:
            tt(R("sa", x0, x0 + 128), P, U("ask", units), ALU.min)
        w = 16 if m == RU - 1 else 1
        rows = top(128 // w)
        mm([(R("p6", x0, x0 + 128, 1, rows), R("ident", 0, 128, w), const(5, 128))]
           + [(listed(m, k, "p6", x0)[:2] + (rows,), R("blkf", 0, 128, w), R("sp", x0 + 32 * k, x0 + 32 * k + 32)) for k in range(4)])
        act(R("ypb", 384 * m + x0, 384 * m + x0 + 128, 1, rows), R("p6", x0, x0 + 128, 1, rows), AF.Copy)
        z = 128 * (m * ST + s)
        store(lambda T: T.yp[:, z:z + 128], R("ypb", 384 * m + x0, 384 * m + x0 + 128, 1, (0, 128 // w, 16 // w)))
        if m < RU - 1:
            mm(fresh_terms(m, [(s, s)], "p7", x0 + (s - m) % 4, M("idn"), 4) + [(listed(m, k, "p7", x0), M("idn"), F(k, s)) for k in range(4) if k != s],
               [(listed(m, k, "p7", x0), M("sel15"), R("sa", x0 + 32 * k, x0 + 32 * k + 32)) for k in range(4)])
            act(R("rec", x0, x0 + 128), R("p7", x0, x0 + 128), AF.Identity, bias=col(9))

    def bound(m):
        c = 256 * m
        P = R("p7", 384, 512)
        mm([(P, ID, R("own", c + 1, c + 256, 2)), (P, NID, R("nxt", c + 1, c + 256, 2))])
        act(M("ab"), P, AF.Abs)
        mm([(P, M("blk"), M("ab")), (P, M("blk"), R("nxt", c + 1, c + 256, 2))]
           + [(R("p7", 384 + 32 * k, 416 + 32 * k), R("sel8", 0, 128, 1, top(8)), listed(m, k, "slf", 128 * m)[:2] + (top(8),)) for k in range(4)])
        act(M("bsl"), P, AF.Identity, bias=0.25)

    def verdict(m, q, roles):
        k0, n, P = roles[0], 32 * len(roles), "pu%d" % q
        c, to = 256 * m + 64 * k0, 256 * (m + 1) + 64 * ((k0 + 1) % 4)
        v, e, last = vin([12 + k for k in roles]), R("own", c + 1, c + 2 * n, 2), m == RU - 1
        tt(R("mx", 32 * k0, 32 * k0 + n), v, R("nxt", c + 1, c + 2 * n, 2), ALU.max)
        mm([(R(P, 1, 2 * n, 2), M("idn") if last else ID, e)])
        mm([(R(P, 0, 2 * n, 2), M("nidn") if last else NID, e), (R(P, 0, 2 * n, 2), M("idn") if last else ID, v)])
        Z = R(P, 128, 128 + n)
        mm([(Z, M("nbig"), R("bsl", 32 * k0, 32 * k0 + n)), (Z, M("nblkb"), v), (Z, M("blk2b"), R("mx", 32 * k0, 32 * k0 + n))])
        ts(R("d0e", 64 * k0 + 1, 64 * k0 + 2 * n, 2), Z, 0.0, None, ALU.is_le)
        for k in roles:
            act(listed(m, k, "yvb", 128 * m), R("d0e", 64 * k + 1, 64 * k + 64, 2), AF.Copy)
            if not last:
                Z = listed(m, k, par["z"], 384)
                mm([(Z, ID, listed(m, k, "cz", 0)), (Z, M("nbig"), R("bsl", 32 * k, 32 * k + 32)), (Z, M("nblkb"), vin([12 + k])), (Z, M("blk2b"), R("mx", 32 * k, 32 * k + 32))])
        scan(R("own", to, to + 2 * n), R("d0e", 64 * k0, 64 * k0 + 2 * n), R(P, 0, 2 * n), 0.0, ALU.mult, ALU.add)
        if not last:
            send("a_p%d%d" % (m + 1, k0), "next", R("prv", to, to + 2 * n), R("own", to, to + 2 * n))
        else:
            for j, k in enumerate(roles):
                cp(listed(m, k, "yeb", 0), R("own", to + 64 * j + 1, to + 64 * j + 64, 2))

    def commit(m):
        K, w = par["reach"], R("win", 0, WEND)
        for j in (2, 1, 0):
            tt(R("pm", 128 * j, 128 * j + 128), R(par["z"], 384, 512), R("ypb", 384 * m + 128 * j, 384 * m + 128 * j + 128), ALU.max)
        for a, b in par["parts"]:
            scan(R("hold", a, b), R("dg0", a, b), R("pm", a, b), -5.0, ALU.max, ALU.min)
            terms = [(R("p7", a, b), ID, R("cc", a, b))]
            for k in range(K):
                e = R("eq", 384 * k + a, 384 * k + b - 16 * k)
                tt(e, R("p6", a + 16 * k, b), R("hold", a, b - 16 * k), ALU.is_equal)
                terms.append((R("p7", a + 16 * k, b), M("blk2b"), e))
            mm(terms[:-1], terms[-1:])
            scan(R("drop", a, b), R("dg0", a, b), R("p7", a, b), -5.0, ALU.max, ALU.min)
            tt(R("offf", a // 16, b // 16), R("hold", a + 15, b, 16), R("drop", a + 15, b, 16), ALU.max)
            ts(R("offs", a // 16, b // 16), R("offf", a // 16, b // 16), float(DB), None, ALU.add)
            for c in range(b // 16 - K, a // 16 - 1, -K):
                src, off = R("rec", 16 * c, 16 * (c + K)), R("offs", c, c + K)
                add("V", lambda e, T, X, src=src, off=off: e.tensor_copy(res(T, w).indirect(res(T, off)), res(T, src)),
                    [src, off], [w], ("s", 16 * K))

    home = {k: q for q, st in enumerate(par["streams"]) for j in st for k, s in j[0]}
    for m in range(RU):
        done, todo = set(), [list(st) for st in par["streams"]]
        while any(todo):
            for q, st in enumerate(todo):
                for k in (C, B, A):
                    if (k, k) not in done and (k == 0 or (k, k - 1) in done):
                        idle(m, home[k], k)
                        done.add((k, k))
                if st and all(s == 0 or (k, s - 1) in done for k, s in st[0][0] + st[0][1]):
                    job(m, q, *st[0])
                    done.update(st.pop(0)[0])
        bound(m)
        for s in range(ST):
            shadow(m, s)
        for roles in par["verdicts"]:
            verdict(m, home[roles[0]], roles)
        if m < RU - 1:
            send("a_n%d" % (m + 1), "prev", R("nxt", 256 * m + 256, 256 * m + 512), R("own", 256 * m + 256, 256 * m + 512))
            commit(m)
    store(lambda T: T.ye[:], M("yeb"))
    store(lambda T: T.yv[:], R("yvb", 0, 384, 1, (0, 128, 16)))
    above = []
    for o in ops:
        far = 0
        for d in o["deps"]:
            far |= above[d]
        o["near"] = {d: x for d, x in o["deps"].items() if not far >> d & 1}
        above.append(far | sum(1 << d for d in o["near"]))
    return ops


def price(ops, k):
    cost = []
    for o in ops:
        kind, n = o["cost"]
        cost.append({"v": k["fix"] + n * k["c"], "p": n * k["p"], "g": 65 + n * k["g"] * k["c"], "s": 55 + n * k["s"] * k["c"],
                     "a": (205 + 2 * n) * k["c"], "r": k["call"], "n": n}[kind])
    late = [k["net"] if o["late"] < 0 else o["late"] for o in ops]
    pred = [[(d, (late[d] + (k["own"] if ops[d]["eng"] == o["eng"] else k["hop"])) if need else 0.0) for d, need in o["near"].items()] for o in ops]
    return cost, late, pred


def first_order(ops, k, look=0.3):
    cost, late, pred = price(ops, k)
    n = len(ops)
    succ = [[] for _ in ops]
    for i in range(n):
        for d, w in pred[i]:
            succ[d].append((i, w))
    level = [0.0] * n
    for i in range(n - 1, -1, -1):
        level[i] = cost[i] + max([w + level[j] for j, w in succ[i]] + [late[i]])
    for i in range(len(LOADS)):
        level[i] = 1e9 - i
    left = [len(p) for p in pred]
    can = [0.0] * n
    ready = [i for i in range(n) if left[i] == 0]
    free, bank, out = {}, {}, []

    def start(i):
        e = ops[i]["eng"]
        return max([can[i], free.get(e, 0.0)] + [x + k["hop"] for b in ops[i]["banks"] for e2, x in bank.get(b, {}).items() if e2 != e])
    while ready:
        when = {j: start(j) for j in ready}
        first = min(ready, key=lambda j: (when[j], -level[j]))
        t = when[first] + look * cost[first]
        i = max((j for j in ready if ops[j]["eng"] == ops[first]["eng"] and when[j] <= t), key=lambda j: level[j])
        end = free[ops[i]["eng"]] = when[i] + cost[i]
        for b in ops[i]["banks"]:
            bank.setdefault(b, {})[ops[i]["eng"]] = end
        out.append(i)
        ready.remove(i)
        for j, w in succ[i]:
            can[j] = max(can[j], end + w)
            left[j] -= 1
            if left[j] == 0:
                ready.append(j)
    return out


def timer(ops, k):
    cost, late, pred = price(ops, k)
    queues, names = sorted(set(o["eng"] for o in ops)), sorted(set(b for o in ops for b in o["banks"]))
    eng = [queues.index(o["eng"]) for o in ops]
    banks = [[names.index(b) for b in o["banks"]] for o in ops]
    hop, busy = k["hop"], [queues.index("V"), queues.index("S")]

    def time_of(order, same=0, old=None, again=0, slack=0.0):
        if old:
            end, why, marks = old[3][:], old[2][:], old[4][:same // 32 + 1]
        else:
            end, why, marks = [0.0] * len(ops), [-1] * len(ops), [([-1] * len(queues), [[-1] * len(queues) for _ in names], 0.0, -1)]
        last, user, top, at = marks[-1]
        last, user = last[:], [row[:] for row in user]
        for n in range(32 * len(marks) - 32, len(order)):
            if n == 32 * len(marks):
                if old and n > again + 64 and min(end[last[v]] - old[3][old[4][len(marks)][0][v]] for v in busy) > slack:
                    return None
                marks.append((last[:], [row[:] for row in user], top, at))
            i = order[n]
            e = eng[i]
            y = last[e]
            t = end[y] if y >= 0 else 0.0
            for d, w in pred[i]:
                if end[d] + w > t:
                    t, y = end[d] + w, d
            for b in banks[i]:
                row = user[b]
                for e2, d in enumerate(row):
                    if d >= 0 and e2 != e and end[d] + hop > t:
                        t, y = end[d] + hop, d
                row[e] = i
            end[i], why[i], last[e] = t + cost[i], y, i
            if end[i] + late[i] > top:
                top, at = end[i] + late[i], i
        return top, at, why, end, marks
    return time_of


def improve(ops, order, tries, pictures, temp=80.0, seed=0):
    rng = np.random.RandomState(seed)
    timers = [timer(ops, k) for k in pictures]
    near = [set(o["near"]) for o in ops]
    now = [t(order) for t in timers]
    scale = [now[0][0] / x[0] / len(now) for x in now]
    cur = best = now[0][0]
    keep, pairs = order, None
    for n in range(tries):
        if pairs is None:
            pairs = []
            for x in now:
                at, why = x[1:3]
                while why[at] >= 0:
                    if why[at] not in near[at] and why[at] >= len(LOADS):
                        pairs.append((why[at], at))
                    at = why[at]
        i, j = pairs[rng.randint(len(pairs))]
        a, b = order.index(i), order.index(j)
        mid = order[a:b + 1]
        if rng.rand() < 0.5:
            go, todo = {j}, set(near[j])
            for x in mid[-2::-1]:
                if x in todo:
                    go.add(x)
                    todo |= near[x]
            new = [x for x in mid if x in go] + [x for x in mid if x not in go]
        else:
            go = {i}
            for x in mid[1:]:
                if near[x] & go:
                    go.add(x)
            new = [x for x in mid if x not in go] + [x for x in mid if x in go]
        if i in go and j in go:
            continue
        cand = order[:a] + new + order[b + 1:]
        slack = -math.log(rng.rand() + 1e-12) * (temp * (1 - n / tries) + 1)
        got = []
        for t, x in zip(timers, now):
            got.append(t(cand, a, x, b, slack * len(now) + 200))
            if not got[-1]:
                break
        else:
            s = sum(x[0] * y for x, y in zip(got, scale))
            if s <= cur + slack:
                order, now, cur, pairs = cand, got, s, None
                if s < best:
                    best, keep = s, cand
    return keep


PLAN = {}


def plan():
    if not PLAN:
        ops = build(PARAMS)
        order = first_order(ops, PICTURE)
        for tries, n, heat in PARAMS["rounds"]:
            order = improve(ops, order, tries, PICTURES[:n], heat, PARAMS["seed"])
        place = {i: k for k, i in enumerate(order)}
        bank = {}
        for i in order:
            o = ops[i]
            need = [d for d, x in o["deps"].items() if x]
            for b in o["banks"]:
                need += [d for e, d in bank.get(b, {}).items() if e != o["eng"]]
                bank.setdefault(b, {})[o["eng"]] = i
            last = {}
            for d in need:
                key = ops[d]["eng"] if ops[d]["sem"] is None else d
                if key not in last or place[d] > place[last[key]]:
                    last[key] = d
            o["waits"] = list(last.values())
        seen, wanted = {}, set()
        for i in order:
            o = ops[i]
            for d in o["waits"]:
                key = (o["eng"], ops[d]["eng"])
                if ops[d]["sem"] is None and seen.get(key, -1) < place[d]:
                    seen[key] = place[d]
                    wanted.add(d)
        total = {}
        for i in order:
            o = ops[i]
            if i in wanted:
                total[o["eng"]] = total.get(o["eng"], 0) + 1
            o["tick"] = total.get(o["eng"], 0)
        PLAN.update(ops=ops, order=order, wanted=wanted)
    return PLAN


def rank_program(g, core, T, topo):
    rank = T.rank_of(core)
    if rank is None:
        return
    n = len(T.cores)
    after, before = T.cores[(rank + 1) % n], T.cores[(rank - 1) % n]
    X = {name: tuple(topo.addr(other, core)) + (topo.mask(core, other),) for name, other in (("next", after), ("prev", before))}
    came = {"p": len(topo.engines(before, core)), "n": len(topo.engines(after, core))}
    went = {"p": len(topo.engines(core, after)), "n": len(topo.engines(core, before))}
    p = plan()
    ops = p["ops"]
    queue = {"V": g.vector, "S": g.scalar, "P": g.tensor, "G": g, "Y": g.sync}
    known = {}
    for i in p["order"]:
        o = ops[i]
        if o["eng"] == "N":
            continue
        q = queue[o["eng"]]
        for d in o["waits"]:
            b = ops[d]
            if b["sem"] is None:
                sem, val = "c" + b["eng"], b["tick"]
            elif b["eng"] == "N":
                sem, val = b["sem"][0], came[b["sem"][0][2]]
            elif b["sem"][0] == "gone":
                if o["eng"] == "G":
                    continue
                sem, val = "gone", went["p"]
            else:
                sem, val = b["sem"]
            if known.get((o["eng"], sem), 0) < val:
                q.wait_ge(T.sem[sem], val)
                known[(o["eng"], sem)] = val
        ins = o["fn"](q, T, X)
        if i in p["wanted"]:
            ins.then_inc(T.sem["c" + o["eng"]], 1)
        elif o["sem"] is not None and o["sem"][1] == 16:
            ins.then_inc(T.sem[o["sem"][0]], 16)
    g.wait_ge(T.sem.sent, sum(went[o["sem"][0][2]] for o in ops if o["eng"] == "N") - went["p"])
    g.sync.wait_ge(T.sem.stored, sum(16 for o in ops if o["sem"] == ("stored", 16)))
